import numpy as np, ml_dtypes
CORES = [2,3,42,43,82,83,122,123]
N = 8
BF = ml_dtypes.bfloat16
S, V, KW, L, ST = 3072, 1024, 512, 192, 7
def parts(rng):
    lev = rng.integers(0, 256, (N, 8, 1, S)); x = np.clip(lev + rng.integers(-48, 49, (N, 8, 16, S)), 0, 255)
    order = np.argsort(lev[:, :, 0], axis=-1); w = S // 8
    pos = rng.integers(0, S - w + 1, (N, 8, 1, 2 * V)) + rng.integers(0, w, (N, 8, 16, 2 * V))
    near = np.take_along_axis(order, pos.reshape(N, 8, -1), 2).reshape(pos.shape)
    b = np.where(rng.random((N, 8, 1, 2 * V)) < 0.6, near, rng.integers(0, S, (N, 8, 16, 2 * V)))
    k = rng.integers(0, S, (N, 8, 16, KW))
    return x, b, k, rng.integers(0, S, (N, 8, L)), rng.integers(0, V, (N, 8, L)), rng.integers(0, 2, (N, 8, L))
def pack(x, b, k, c, v, d):
    return {"x": np.ascontiguousarray(x.reshape(N, 128, S)).astype(np.float32).astype(BF), "bnd": np.ascontiguousarray(b.reshape(N, 128, 2 * V)).astype(np.int32),
            "kt": np.ascontiguousarray(k.reshape(N, 128, KW)).astype(np.int32), "lc": c.astype(np.int32), "lv": v.astype(np.int32), "ld": d.astype(np.int32)}
def setup_inputs(rng):
    return pack(*parts(rng))
def setup_inputs_spread(rng):
    x, b, k, c, v, d = parts(rng)
    x = np.minimum((np.exp2(8.2 * rng.random((N, 8, 1, S))) * rng.random((N, 8, 16, S))).astype(np.int64), 255)
    def low(n, shape): return np.minimum((n * rng.random(shape) ** 3).astype(np.int64), n - 1)
    b = np.where(rng.random(b.shape) < 0.5, low(S, b.shape), b); k = np.where(rng.random(k.shape) < 0.5, low(S, k.shape), k)
    return pack(x, b, k, low(S, c.shape), low(V, v.shape), (rng.random(d.shape) < rng.random((N, 8, 1))).astype(np.int64))
def setup_inputs_ends(rng):
    def ends(hi, shape):
        u = rng.random(shape)
        return np.where(u < 0.37, 0, np.where(u < 0.75, hi, rng.integers(0, hi + 1, shape)))
    kind = rng.integers(0, 3, (N, 8, 1, S)); kind[..., 1:S - 1:2] = 2
    kind[..., S - 1] = 1; kind[:, 1, :, S - 1] = 0; kind[..., S - 2] = 0; kind[..., 0] = 0; kind[:, 3, :, 0] = 1; kind[:, 7, :, 0] = 1
    x = np.where(kind == 2, 255 * rng.integers(0, 2, (N, 8, 16, S)), 255 * kind)
    b = ends(S - 1, (N, 8, 16, 2 * V)); k = ends(S - 1, (N, 8, 16, KW)); c = ends(S - 1, (N, 8, L)); v = ends(V - 1, (N, 8, L)); d = rng.integers(0, 2, (N, 8, L))
    b[..., 0] = 0; b[..., 1] = 0; b[..., 2 * V - 2] = S - 2
    b[:, :, :15, 2 * V - 1] = 1 + 2 * rng.integers(0, S // 2 - 1, (N, 8, 15)); b[:, :, 15, 2 * V - 1] = S - 1
    for i, w, s in ((0, 0, 1), (1, 0, 0), (L - 2, V - 1, 1), (L - 1, V - 1, 0)):
        c[..., i] = S - 1; v[..., i] = w; d[..., i] = s
    b[..., 10] = S - 1; b[:, :, 15, 10] = S - 2; c[..., 2] = S - 2; v[..., 2] = 5; d[..., 2] = 1
    return pack(x, b, k, c, v, d)
def setup_inputs_corners(rng):
    base = rng.choice(np.array([1, 4, 100, 128, 254]), (N, 8, 1, 1)); sh = np.arange(S); h = S // 4
    m = 8 + (sh // 2) % 3; sgn = np.where(sh % 2 == 0, 1, -1)
    rk = np.argsort(rng.random((N, 8, 16, S)), axis=2)
    x = base + np.where(sh < h, 0, sgn * np.where(rk < m, rng.integers(0, 2, rk.shape), -1))
    kind = rng.integers(0, 5, (N, 8, 1, 2 * V)); at = rng.choice(np.array([0, 7, 15]), kind.shape); hit = np.arange(16)[:, None] == at
    mm = np.where(kind == 4, rng.integers(8, 11, (N, 8, 16, 2 * V)), np.where(kind == 1, 9, np.where((kind == 2) & hit, 10, np.where((kind == 3) & hit, 9, 8))))
    b = 6 * rng.integers((h + 5) // 6, (S - 6) // 6 + 1, mm.shape) + 2 * (mm - 8) + (1 - np.arange(2 * V) % 2)
    few = np.array([0, h - 1, h // 2, S - 1])
    k = np.where(rng.random((N, 8, 16, KW)) < 0.7, rng.integers(0, h, (N, 8, 16, KW)), rng.choice(few, (N, 8, 16, KW)))
    c = np.where(rng.random((N, 8, L)) < 0.7, rng.integers(0, h, (N, 8, L)), rng.choice(few, (N, 8, L)))
    v = np.where(rng.random((N, 8, L)) < 0.7, rng.integers(0, V, (N, 8, L)), rng.choice(np.array([0, V - 1]), (N, 8, L))); d = rng.integers(0, 2, (N, 8, L))
    for i in range(8):
        v[..., i] = V - 1 - i; d[..., i] = i % 2; w = 2 * (V - 1 - i) + 1 - i % 2
        if i < 4: b[:, :, :, w] = c[:, :, i][:, :, None]
        else: b[:, :, 15, w] = c[:, :, i]
    return pack(x, b, k, c, v, d)
def setup_inputs_crowd(rng):
    x, b, k, c, v, d = parts(rng)
    for q in range(N):
        for g in range(8):
            kind = (g + q) % 8; o = rng.permutation(S); s = int(rng.integers(0, 2)); w = int(rng.choice(np.array([0, V - 1, V // 2, 5])))
            one = int(rng.choice(np.array([0, L // 2, L - 1])))
            if kind < 4:
                top = 255 if s == 0 else 0
                a, z, e = o[:48], o[48:96], o[96:112]
                x[q, g][:, a] = top; x[q, g][:, z] = 255 - top; x[q, g][:, e] = np.clip(x[q, g][:, e], 1, 254)
                b[q, g, :, 2 * w + 1 - s] = e; v[q, g] = w; d[q, g] = s
                u, y = (a, z) if kind < 2 else (z, a)
                c[q, g] = u[0] if (kind + q) % 2 == 0 and q % 4 < 2 else rng.choice(u, L)
                if kind % 2 == 1: c[q, g, one] = y[3]
            elif kind == 4: v[q, g] = rng.choice(np.array([0, V - 1, 7, w]), L); c[q, g] = rng.choice(np.array([0, S - 1, int(o[0]), int(o[1])]), L)
            elif kind == 5: k[q, g] = k[q, g, :, :1]
            elif kind == 6: k[q, g] = rng.choice(np.array([0, S - 1]), (16, KW))
            else: c[q, g] = o[0]; v[q, g] = w; d[q, g] = s
    return pack(x, b, k, c, v, d)
def setup_inputs_limits(rng):
    x, b, k, c, v, d = parts(rng); w = S // 8
    for q in range(N):
        for g in range(8):
            o = rng.permutation(S - w); z = o[:14]; at = np.arange(S); at[z] = o[14:28]
            if g % 2 == 1:
                at[S - w:] = o[28:28 + w]; x[q, g][:, S - w:] = 255 * rng.integers(0, 2, (16, 1)); x[q, g, 15, S - w:] = 255
            b[q, g] = at[b[q, g]]; k[q, g] = at[k[q, g]]; c[q, g] = at[c[q, g]]
            x[q, g][:, z] = np.array([255, 255, 255, 255, 0, 0, 0, 0, 200, 200, 200, 200, 40, 160])
            f = int(rng.integers(0, 16)); x[q, g, f, z[1]] = 254; x[q, g, f, z[5]] = 1; x[q, g, f, z[6]] = 3
            x[q, g, rng.permutation(16)[:8], z[3]] = 254
            r = rng.permutation(V - 1); u = [int(a) for a in r[:9]] + [V - 1]; v[q, g] = r[9 + rng.integers(0, V - 10, L)]
            for n, (i, own, s, rest, row, one) in enumerate(((0, 0, 0, 1, 15, 2), (L - 1, 0, 1, 1, 15, 2), (1, 3, 1, 2, 15, 4), (L - 2, 3, 1, 2, 0, 6), (2, 0, 0, 4, 15, 5), (L - 3, 7, 1, 2, 15, 1))):
                c[q, g, i] = z[own]; v[q, g, i] = u[n]; d[q, g, i] = s
                b[q, g, :, 2 * u[n] + 1 - s] = z[rest]; b[q, g, row, 2 * u[n] + 1 - s] = z[one]
            for n, j in enumerate((16, 32, 64, 128)):
                c[q, g, j - 1] = z[12]; c[q, g, j] = z[13]; v[q, g, j - 1:j + 1] = u[6 + n]; d[q, g, j - 1:j + 1] = 0
                b[q, g, :, 2 * u[6 + n] + 1] = z[8 + n]
    return pack(x, b, k, c, v, d)
def check_inputs(d):
    bad = []
    for k, hi in (("x", 255), ("bnd", S - 1), ("kt", S - 1), ("lc", S - 1), ("lv", V - 1), ("ld", 1)):
        a = np.asarray(d[k]).astype(np.float32)
        if not (np.min(a) >= 0 and np.max(a) <= hi): bad.append("range of " + k)
        elif k == "x" and np.any(np.floor(a) != a): bad.append("whole numbers in x")
    return bad
def first(w):
    return ~np.any((w[..., :, None] == w[..., None, :]) & np.tril(np.ones((L, L), bool), -1), axis=-1)
def append(b, col, val, t):
    n, g, i = np.nonzero(first(col)); b[n, g, (5 * t + i) & 15, col[n, g, i]] = val[n, g, i]
def reference(x, bnd, kt, lc, lv, ld):
    X = x.astype(np.float32).astype(np.int32).reshape(N, 8, 16, S).copy(); B = bnd.astype(np.int32).reshape(N, 8, 16, 2 * V).copy(); K = kt.astype(np.int32).reshape(N, 8, 16, KW)
    c, v, d = lc.astype(np.int64), lv.astype(np.int64), ld.astype(np.int64); A = np.zeros((N, 8), np.int64); miss = []
    for t in range(ST):
        q = np.take_along_axis(X, c[:, :, None, :], 3)
        E = np.take_along_axis(B, (2 * v + 1 - d)[:, :, None, :], 3).astype(np.int64)
        xe = np.take_along_axis(X, E.reshape(N, 8, 1, 16 * L), 3).reshape(N, 8, 16, 16, L)
        qq = q[:, :, :, None, :]
        fits = np.where((d == 0)[:, :, None, None, :], qq <= xe, xe <= qq)
        good = np.add.reduce(fits.astype(np.int32), axis=2) >= (9 + (A & 1))[:, :, None, None]
        M = np.add.reduce(np.minimum(xe, qq), axis=2); D = np.add.reduce(np.abs(xe - qq), axis=2)
        hit = np.any(good, axis=2)
        ks = np.where(hit, np.argmax(np.where(good, M, -1), axis=2), np.argmin(D, axis=2))[:, :, None, :]
        e = np.take_along_axis(E, ks, 2)[:, :, 0]; p = (np.take_along_axis(D, ks, 2)[:, :, 0] & 15).astype(np.int64)
        y = np.take_along_axis(X, e[:, :, None, :], 3)
        place = np.where(hit, e, c); value = np.where(hit[:, :, None, :], np.abs(y - (q >> 2)), (q + y) >> 1)
        n, g, i = np.nonzero(first(place)); X[n, g, :, place[n, g, i]] = value[n, g, :, i]
        append(B, 2 * v + d, c, t)
        kc = np.take_along_axis(K, (c & (KW - 1))[:, :, None, :], 3).astype(np.int64); ke = np.take_along_axis(K, (e & (KW - 1))[:, :, None, :], 3).astype(np.int64)
        pair = []
        for z in (p, p ^ 1):
            pair.append((np.take_along_axis(kc, z[:, :, None, :], 2)[:, :, 0], np.take_along_axis(ke, z[:, :, None, :], 2)[:, :, 0] & (V - 1), d ^ (z & 1)))
        c2, v2, d2 = [np.roll(a, 1 + t % (N - 1), axis=0) for a in pair[1]]
        append(B, 2 * v2 + d2, c2, t)
        c, v, d = pair[0]; A = np.add.reduce((~hit).astype(np.int64), axis=2); miss.append(A)
    ys = np.add.reduce(X.reshape(N, 8, 16, 8, S // 8), axis=4)
    return {"yb": B.reshape(N, 128, 2 * V).astype(np.float32), "yc": c.astype(np.float32), "yv": v.astype(np.float32), "yd": d.astype(np.float32),
            "ys": ys.reshape(N, 128, 8).astype(np.float32), "ym": np.stack(miss, axis=2).astype(np.float32)}

@@ -1,0 +1,665 @@
+import numpy as np
+from concourse.bass import DstId, RemoteDMATransfer
+from concourse.mybir import dt, AluOpType, AxisListType, ActivationFunctionType
+
+S, NV, KW, L, ST = 3072, 2048, 512, 192, 7
+F32, BF, F16, I32, U16 = "float32", "bfloat16", "float16", "int32", "uint16"
+MB = 4
+NS = 12 // MB
+PS = MB
+SEG = [sum(16 * (b + 1) + 2 for b in range(a)) for a in range(MB + 1)]
+SL = SEG[MB]
+NE = SL * NS
+XS, BS = S + 16 * MB, NV + 16 * MB
+
+
+def _sb(n, d):
+    return ("sbuf", [128, n], d)
+
+
+SCRATCH = {
+    "xin": _sb(S, BF), "X": _sb(XS + 16, BF), "Bi": _sb(NV, I32), "B": _sb(BS, F32),
+    "k1": _sb(KW, I32), "ka": _sb(KW, I32), "TT": _sb(5120, F32),
+    "li": _sb(3 * L, I32), "lcol": _sb(L, F32),
+    "pi": _sb(4, I32), "pj": _sb(4, I32), "pc": _sb(16, F32), "it": _sb(1024, F32), "it2": _sb(208, F32),
+    "it4": _sb(144, F32), "it5": _sb(128, F32), "it6": _sb(128, F32), "it7": _sb(16, F32),
+    "Wd": _sb(144, BF), "Wd10": _sb(144, BF), "BO": _sb(128, BF), "BOf": _sb(128, F32), "RR": _sb(2048, BF),
+    "Ib": _sb(128, BF), "Ih": _sb(128, BF), "In": _sb(128, BF), "If": _sb(128, F32), "I10": _sb(128, F32), "Sel": _sb(1024, BF),
+    "DG": _sb(208, F32), "NDG": _sb(208, F32), "sc1": _sb(L, F32), "sc2": _sb(NE, F16), "sc3": _sb(SL, F32),
+    "EE": _sb(2048, BF), "DGc": _sb(208, BF), "I9": _sb(128, F32), "I192": _sb(128, BF), "nid16": _sb(16, F16),
+    "cJ": _sb(12, U16), "perm": _sb(12, U16), "nid": _sb(12, F32), "nq": _sb(12, I32), "nf": _sb(12, F32), "cst": _sb(64, BF),
+    "row": _sb(16, F32), "rowd": _sb(16, F32), "col": _sb(8, F32), "cOff": _sb(2, U16),
+    "E": _sb(L, U16), "Ec": _sb(L, F16), "xe": _sb(S, BF), "H": _sb(S, F16),
+    "QS": _sb(2 * L, BF), "QT": _sb(2 * L, BF), "qN": _sb(L, BF), "f4": _sb(L, BF), "yN": _sb(L, BF),
+    "LN": _sb(16, F32), "LX": _sb(L, F32), "SX": _sb(L, F32), "th": _sb(4, F32), "hb": _sb(4, BF), "ab": _sb(4, F32),
+    "Y": _sb(L, F32), "a1": _sb(L, F32), "a2": _sb(L, F32), "tt": _sb(L, F32), "R1": _sb(L, I32), "R2": _sb(L, F32),
+    "key": _sb(L, F32), "scn": _sb(L, F32),
+    "Z": _sb(12, I32), "kk": _sb(12, I32), "kb": _sb(16, BF), "z2": _sb(12, I32), "lo": _sb(12, I32), "hit": _sb(12, BF),
+    "pa": _sb(12, F32), "pb": _sb(12, F32), "pd": _sb(12, I32), "pe": _sb(12, I32), "pf": _sb(16, BF),
+    "ms": _sb(12, F32), "mc": _sb(4, F32), "ymt": _sb(8, F32),
+    "prE": _sb(L, F16), "mp": _sb(L, F32), "pr1": _sb(2 * L, F16), "pv2": _sb(L, F16), "pc2": _sb(L, F16),
+    "ei": _sb(12, I32), "ej": _sb(12, I32), "eo": _sb(12, U16), "eN": _sb(12, U16),
+    "m1": _sb(24 * ST, U16), "m2": _sb(16 * ST, U16), "r1": _sb(24 * ST, U16), "r2": _sb(16 * ST, U16),
+    "pl": _sb(16, F32), "oo": _sb(16, U16), "op": _sb(16, U16), "V": _sb(16, F16),
+    "nw2": _sb(16, F32), "nwo": _sb(16, F32), "nwp": _sb(16, F32), "sw2": _sb(16, F32), "swo": _sb(16, F32), "swp": _sb(16, F32),
+    "eq2": _sb(NE, BF), "eqo": _sb(NE, BF), "eqp": _sb(NE, BF),
+    "ds2": _sb(NE, BF), "dso": _sb(NE, BF), "dsp": _sb(NE, BF),
+    "of2": _sb(16, F32), "ofo": _sb(16, F32), "ofp": _sb(16, F32),
+    "t1": _sb(L, F32), "t2": _sb(L, F32), "t3": _sb(L, F32), "t4": _sb(L, F32),
+    "pm": _sb(12, F32), "pn": _sb(12, F32), "p16": _sb(32, F16), "so": _sb(12, F32), "sq": _sb(12, F32), "su": _sb(12, U16),
+    "zr": _sb(L, F32), "zs": _sb(L, F32), "vals": _sb(2 * L, F32), "nv": _sb(L, BF),
+    "I": _sb(48, I32), "D": _sb(24, I32), "cm": _sb(12, I32), "cu": _sb(12, U16), "nu": _sb(24, U16), "QO": _sb(24, U16),
+    "d4": _sb(16, BF), "sg": _sb(32, F32), "sb": _sb(16, BF), "oq": _sb(12, F32), "ou": _sb(12, U16), "cN": _sb(12, F32), "cR": _sb(12, F32),
+    "yst": _sb(8, F32), "junk": _sb(S, BF), "oc": _sb(3 * L, F32), "oi": _sb(L, I32), "oj": _sb(2 * L, I32),
+    "Q0": ("psum", [128, 512], F32), "Q1": ("psum", [128, 512], F32), "Q2": ("psum", [128, 512], F32), "Q3": ("psum", [128, 512], F32),
+    "P1": ("psum", [128, 512], F32), "P2": ("psum", [128, 512], F32), "MA": ("psum", [128, 512], F32), "MB": ("psum", [128, 512], F32),
+}
+BUFS = dict(SCRATCH)
+PLACE = {}
+_end = {}
+for _n, (_w, _s, _d) in BUFS.items():
+    if _w == "sbuf" and _s[1] <= 48:
+        _a = "short_" + _d
+        PLACE[_n] = (_a, _end.get(_a, 0))
+        _end[_a] = _end.get(_a, 0) + (_s[1] + 15) // 16 * 16
+        del SCRATCH[_n]
+        SCRATCH[_a] = _sb(_end[_a], _d)
+    else:
+        PLACE[_n] = (_n, 0)
+NDMA = 24
+SEMAPHORES = (["qv", "qa", "qp", "qg", "sent"] + ["d%d" % i for i in range(NDMA)]
+              + ["ra%d" % t for t in range(ST)] + ["rb%d" % t for t in range(ST)])
+PSUM = ("Q0", "Q1", "Q2", "Q3", "P1", "P2", "MA", "MB")
+WIDTH = {F32: 4, I32: 4, BF: 2, F16: 2, U16: 2}
+CYC, PEC, GAT, SCA, HOP, FAR, FIX = 0.83, 0.42, 1.5, 3.5, 90.0, 2500.0, 50.0
+PLAN = {}
+SENT = [("Q3", "v"), ("P1", "a"), ("P2", "v")]
+ROUNDS, NOISE = 400, 1500.0
+VGAT = (1,)
+
+
+def plan(ops):
+    n = len(ops)
+    cost = [o["cost"] + 0.001 for o in ops]
+    pred = [[] for _ in range(n)]
+    succ = [[] for _ in range(n)]
+    for i, o in enumerate(ops):
+        for d in o["deps"] | o["order"]:
+            lag = ops[d]["lat"] + (HOP if d in o["deps"] else 0.0)
+            pred[i].append((d, lag))
+            succ[d].append((i, lag))
+    tail = [o["lat"] for o in ops]
+
+    def fill(seq, before, first):
+        st = [0.0] * n
+        busy = {}
+        for i in seq:
+            t = max([st[d] + cost[d] + lag for d, lag in before[i]] + [first[i]])
+            q = ops[i]["q"]
+            if q != "x":
+                a, b = busy.setdefault(q, ([], []))
+                lo, hi = 0, len(b)
+                while lo < hi:
+                    m = (lo + hi) // 2
+                    if b[m] <= t:
+                        lo = m + 1
+                    else:
+                        hi = m
+                while lo < len(a) and a[lo] < t + cost[i]:
+                    t = max(t, b[lo])
+                    lo += 1
+                a.insert(lo, t)
+                b.insert(lo, t + cost[i])
+            st[i] = t
+        return st
+
+    far = [0.0] * n
+    for i in range(n - 1, -1, -1):
+        far[i] = cost[i] + max([far[s] + lag for s, lag in succ[i]] + [tail[i]])
+    zero = [0.0] * n
+    rng = np.random.default_rng(7)
+
+    def ranked(key, before, after):
+        key = list(key)
+        left = [len(b) for b in before]
+        ready = [i for i in range(n) if not left[i]]
+        seq = []
+        while ready:
+            i = min(ready, key=lambda k: key[k])
+            ready.remove(i)
+            seq.append(i)
+            for s, _ in after[i]:
+                left[s] -= 1
+                if not left[s]:
+                    ready.append(s)
+        return seq
+
+    best = None
+    st = fill(sorted(range(n), key=lambda i: -far[i]), pred, zero)
+    for k in range(ROUNDS):
+        span = max(st[i] + cost[i] + tail[i] for i in range(n))
+        if best is None or span < best[0]:
+            best = (span, st)
+        noise = rng.random(n) * (NOISE if k % 3 == 2 else 0.0)
+        if k % 3 == 2:
+            st = best[1]
+        back = fill(ranked([-(st[i] + cost[i]) + noise[i] for i in range(n)], succ, pred), succ, tail)
+        st = fill(sorted(range(n), key=lambda i: -(back[i] + cost[i])), pred, zero)
+    st = best[1]
+    PLAN["end"] = [st[i] + cost[i] + tail[i] for i in range(n)]
+    return sorted(range(n), key=lambda i: st[i])
+
+
+def rank_program(g, core, T, topo):
+    rank = T.rank_of(core)
+    if rank is None:
+        return
+    A, AF = AluOpType, ActivationFunctionType
+    N = len(T.cores)
+    ops = []
+    seen = {}
+    bank = {}
+    ndma = [0]
+
+    def R(name, lo=0, hi=None, step=1, p0=0, p1=128, ps=1):
+        w = BUFS[name][1][1]
+        hi = w if hi is None else hi
+        t, o = T[PLACE[name][0]], PLACE[name][1]
+        if (p0, p1, ps) == (0, 128, 1):
+            ap = t[:, o + lo:o + hi] if step == 1 else t[:, o + lo:o + hi:step]
+        else:
+            ap = t[p0:p1:ps, o + lo:o + hi]
+        return (ap, [(name, lo, hi)], [], len(range(lo, hi, step)), WIDTH[BUFS[name][2]], name in PSUM)
+
+    def G(win, off):
+        return (win[0].indirect(off[0]), win[1], off[1], 16 * off[3], win[4], False)
+
+    def add(q, call, outs, ins, cost, kind="c", sem=None, lat=0.0, after=()):
+        me = len(ops)
+        acc = []
+        for o in outs:
+            acc += [(r, True) for r in o[1]] + [(r, False) for r in o[2]]
+        for o in ins:
+            if isinstance(o, tuple):
+                acc += [(r, False) for r in o[1] + o[2]]
+        deps, order = set(), set(after)
+        for (name, lo, hi), wr in acc:
+            ps = name in PSUM
+            if ps and name in bank:
+                order.add(bank[name])
+            for a in seen.get(name, []):
+                other = ops[a[2]]
+                same = other["q"] == q and other["kind"] == "c" and kind == "c"
+                if ps and not same:
+                    deps.add(a[2])
+                elif wr and a[3] and kind == "d" and other["kind"] == "d":
+                    continue
+                elif a[0] < hi and lo < a[1] and (wr or a[3]) and not (same and q == "p" and ps):
+                    deps.add(a[2])
+        for (name, lo, hi), wr in acc:
+            lst = seen.setdefault(name, [])
+            if name in PSUM:
+                lst[:] = [a for a in lst if ops[a[2]]["q"] == q]
+                bank[name] = me
+            if wr:
+                lst[:] = [a for a in lst if not (lo <= a[0] and a[1] <= hi and a[2] in deps)]
+        ops.append({"q": q, "call": call, "deps": deps, "order": order - deps, "sem": sem, "kind": kind, "cost": cost, "lat": lat,
+                    "tag": (outs[0][1][0][0] if outs else kind)})
+        for (name, lo, hi), wr in acc:
+            seen[name].append([lo, hi, me, wr])
+        return me
+
+    def a0(x):
+        return x[0] if isinstance(x, tuple) else x
+
+    def vcost(o, ins, two=False):
+        n = o[3]
+        if o[2]:
+            return FIX + n * SCA * CYC
+        if ins and ins[0][2]:
+            return FIX + n * GAT * CYC
+        if two:
+            return FIX + n * CYC * (1 if (ins[0][5] or ins[1][5]) else 2)
+        return FIX + n * CYC * (0.5 if max([o[4]] + [i[4] for i in ins]) == 2 else 1)
+
+    def cp(o, i):
+        add("v", lambda: g.vector.tensor_copy(o[0], i[0]), [o], [i], vcost(o, [i]))
+
+    def tt(o, i0, i1, op):
+        add("v", lambda: g.vector.tensor_tensor(o[0], i0[0], i1[0], op), [o], [i0, i1], vcost(o, [i0, i1], True))
+
+    def ts(o, i, s1, op0, s2=None, op1=None):
+        if op1 is None:
+            add("v", lambda: g.vector.tensor_scalar(o[0], i[0], a0(s1), None, op0), [o], [i, s1], vcost(o, [i]))
+        else:
+            add("v", lambda: g.vector.tensor_scalar(o[0], i[0], a0(s1), a0(s2), op0, op1), [o], [i, s1, s2], vcost(o, [i]))
+
+    def scan(o, d0, d1, init, op0, op1):
+        add("v", lambda: g.vector.tensor_tensor_scan(o[0], d0[0], d1[0], init, op0, op1), [o], [d0, d1], vcost(o, [d0, d1]))
+
+    def red(o, i):
+        add("v", lambda: g.vector.tensor_reduce(o[0], i[0], AxisListType.X, A.add), [o], [i], FIX + i[3] * CYC)
+
+    def ms(o, c):
+        add("v", lambda: g.vector.memset(o[0], c), [o], [], vcost(o, []))
+
+    def act(o, i, func=None, bias=0.0, scale=1.0, acc=None):
+        f = AF.Identity if func is None else func
+        c = 65.0 + o[3] * CYC * (GAT if i[2] else 1)
+        if acc is None:
+            add("a", lambda: g.scalar.activation(o[0], i[0], f, bias=a0(bias), scale=a0(scale)), [o], [i, bias, scale], c)
+        else:
+            add("a", lambda: g.scalar.activation(o[0], i[0], f, bias=a0(bias), scale=scale, accum_out=acc[0]), [o, acc], [i, bias], c + 20)
+
+    def mm(o, l, r, start, stop):
+        add("p", lambda: g.tensor.matmul(o[0], l[0], r[0], start, stop), [o], [l, r], max(64, r[3]) * PEC * (4 if r[4] == 4 else 1))
+
+    def iota(o, pat, base, cm):
+        c = 130.0 + 2 * CYC * o[3]
+        if BUFS[o[1][0][0]][2] == I32:
+            add("g", lambda: g.iota(o[0], pat, base, cm), [o], [], c)
+        else:
+            add("g", lambda: g.iota(o[0], pat, base, cm, allow_small_or_imprecise_dtypes=True), [o], [], c)
+
+    def dma(q, o, i):
+        e = {"s": g.sync, "a": g.scalar, "g": g}[q]
+        sem = "d%d" % ndma[0]
+        ndma[0] += 1
+        sb = o if isinstance(o, tuple) else i
+        add(q, lambda: e.dma_start(a0(o), a0(i)), [o] if isinstance(o, tuple) else [], [i], 100.0, kind="d", sem=sem,
+            lat=2000.0 + 128 * sb[3] * sb[4] / 150.0)
+
+    def engines_to(dst):
+        es = topo.engines(core, dst)
+        n = min(len(topo.engines(a, b)) for a in T.cores for b in T.cores if a != b)
+        m = 0
+        for e in es[:n]:
+            m |= 1 << e
+        return m, n
+
+    nsent = [0]
+
+    def send(src, dst, sem, to):
+        rid, pid = topo.addr(to)[:2]
+        m, n = engines_to(to)
+        nsent[0] += n
+        me = add("g", lambda: g.remote_dma(dst[0], src[0], T.sem[sem], T.sem.sent, pid, rid, m), [], [src], 300.0, kind="r", lat=FAR)
+        add("x", None, [dst], [], 0.0, kind="x", sem=sem, after=[me])
+
+    def Sr(r, name="Wd"):
+        return R(name, 16 - r, 144 - r)
+
+    def Rr(r):
+        return R("RR", 128 * r, 128 * r + 128)
+
+    def toN(o, src, last, rot=0, at=0):
+        for r in range(16):
+            mm(o, Sr((r + rot) % 16), R(src, at + 12 * r, at + 12 * r + 12), False, last and r == 15)
+
+    def toA(o, src, last):
+        for r in range(16):
+            mm(o, Sr(r), R(src, r, None, 16), False, last and r == 15)
+
+    def toLanes(ob, src, at=0, js=range(12)):
+        for j in js:
+            mm(R(ob, 16 * j, 16 * j + 16), R("BO"), R(src, at + j, at + L, 12), True, True)
+
+    PC, PK, PR0, PPI, PNI, P32, PX, PB = [R("pc", i, i + 1) for i in range(8)]
+    PV1, PC1 = R("pr1", 0, L), R("pr1", L, 2 * L)
+
+    ms(R("li"), 0)
+    dma("s", R("li", 0, L, ps=16), T.lc[:])
+    dma("g", R("li", L, 2 * L, ps=16), T.lv[:])
+    dma("s", R("li", 2 * L, 3 * L, ps=16), T.ld[:])
+    dma("s", R("Bi"), T.bnd[:])
+    dma("a", R("xin", 0, S // 2), T.x[:, 0:S // 2])
+    dma("a", R("xin", S // 2, S), T.x[:, S // 2:S])
+    dma("s", R("k1"), T.kt[:])
+    iota(R("pi", 0, 1), [[0, 1]], 0, 1)
+    iota(R("it4"), [[1, 144]], -16, -1)
+    iota(R("it5"), [[16, 8], [0, 16]], 0, -1)
+    iota(R("it6"), [[1, 128]], 0, -1)
+    iota(R("it7"), [[1, 16]], 0, 0)
+    iota(R("it2"), [[0, 13], [1, 16]], 0, 0)
+    iota(R("it"), [[1, 64], [0, 16]], 0, 0)
+    iota(R("TT", 2048, 4096), [[0, 2048]], 0, 0)
+    ts(R("pj", 0, 1), R("pi", 0, 1), 15, A.bitwise_and)
+    ts(R("pj", 1, 2), R("pi", 0, 1), 5, A.arith_shift_right)
+    ts(R("pj", 2, 3), R("pi", 0, 1), 1, A.bitwise_and)
+    cp(PC, R("pj", 0, 1))
+    cp(PPI, R("pj", 2, 3))
+    ts(PK, PC, -1.0, A.mult, 15.0, A.add)
+    ts(PR0, PC, 0.0, A.is_equal)
+    ts(PNI, PPI, -2.0, A.mult, 1.0, A.add)
+    ts(P32, R("pj", 1, 2), 16.0, A.mult, PC, A.add)
+    cp(R("cJ"), R("it7", 0, 12))
+    ts(R("nid"), R("it7", 0, 12), 16.0, A.mult, PC, A.add)
+    ts(R("nq"), R("nid"), -5.5, A.add, 1.0 / 12, A.mult)
+    ts(R("nf"), R("nq"), -191.0 / 16, A.mult)
+    tt(R("nf"), R("nf"), R("nid"), A.add)
+    ts(R("perm"), R("nf"), 16.0, A.mult)
+    ts(R("nid16", 0, 12), R("nid"), float(L), A.add)
+    ts(PX, PC, float(S), A.add)
+    ts(PB, PC, float(NV), A.add)
+    ts(R("Wd"), R("it4"), PC, A.add, 0.0, A.is_equal)
+    ts(R("Wd10"), R("Wd"), 2.0 ** -10, A.mult)
+    ts(R("BO"), R("it5"), PC, A.add, 0.0, A.is_equal)
+    ts(R("Ib"), R("it6"), 0.0, A.is_equal)
+    ms(R("cst"), 1536.0)
+    ms(R("cst", 0, 12), 0.0)
+    ms(R("cst", 24, 48), 0.0)
+    ts(R("DG"), R("it2"), PC, A.is_equal)
+    ts(R("NDG"), R("it2"), PC, A.not_equal)
+    ts(R("sc1"), R("it2", 0, L), 0.0, A.not_equal, 65536.0 + 1.0 / 32, A.mult)
+    ts(R("sc1"), R("sc1"), -65536.0, A.add)
+    ts(R("Sel"), R("it"), P32, A.is_equal)
+    ms(R("th"), 1.0 / 32)
+    for w in ("sw2", "swo", "swp", "pl"):
+        ms(R(w, 12, 16), 0.0)
+    for r in range(16):
+        ts(Rr(r), R("BO"), R("DG", r, r + 1), A.mult)
+        act(R("EE", 128 * r, 128 * r + 128), R("Ib"), scale=R("DG", r, r + 1))
+    act(R("DGc"), R("DG"), scale=1536.0)
+    act(R("I9"), R("Ib"), scale=2.0 ** -9)
+    act(R("I192"), R("Ib"), scale=-float(L))
+    act(R("If"), R("Ib"))
+    act(R("I10"), R("Ib"), scale=2.0 ** -10)
+    act(R("Ih"), R("Ib"), scale=0.5)
+    act(R("In"), R("Ib"), scale=-1.0)
+    act(R("BOf"), R("BO"))
+    ms(R("sc3"), 0.0)
+    ms(R("row"), 0.0)
+    for k in "2op":
+        ms(R("eq" + k), 4096.0)
+    for a in range(MB):
+        e = SEG[a + 1] - 1
+        act(R("sc3", SEG[a], SEG[a] + 1), PC, scale=0.0, bias=8192.0)
+        act(R("sc3", e, e + 1), PC, scale=0.0, bias=8192.0 - 16 * a)
+        act(R("sc3", e - 16, e), R("DG", 0, 16), scale=-8192.0)
+        act(R("row", a, 12, MB), R("it7", 0, NS), scale=float(SL), bias=float(e))
+    for s in range(NS):
+        cp(R("sc2", SL * s, SL * s + SL), R("sc3"))
+    tt(R("rowd"), R("row"), R("DG", 0, 16), A.mult)
+    red(R("col", 1, 2), R("rowd"))
+    cp(R("cOff", 0, 1), R("col", 1, 2))
+    cp(R("B", 0, NV // 2), R("Bi", 0, NV // 2))
+    cp(R("B", NV // 2, NV), R("Bi", NV // 2, NV))
+    ms(R("B", NV, BS), 0.0)
+    ts(R("ka"), R("k1"), 1023, A.bitwise_and)
+    ts(R("TT", 0, 512), R("ka"), 2.0, A.mult, PPI, A.add)
+    act(R("TT", 4096, 4608), R("TT", 0, 512), bias=PNI)
+    ts(R("TT", 1024, 1536), R("k1"), -1536.0, A.add)
+    for o in (0, 1024, 4096):
+        dma("s", R("TT", o + 512, o + 1024, ps=2), R("TT", o, o + 512, p0=1, ps=2))
+        dma("s", R("TT", o + 512, o + 1024, p0=1, ps=2), R("TT", o, o + 512, ps=2))
+    ts(R("X", 0, 1536), R("xin", 0, 1536), -127.5, A.add)
+    ts(R("X", 1536, S), R("xin", 1536, S), -127.5, A.add)
+    ms(R("X", S, XS), 0.0)
+    ms(R("X", XS, XS + 1), -0.0625)
+    ms(R("X", XS + 1, XS + 16), 0.0625)
+    ts(R("lcol"), R("li", L, 2 * L), 2.0, A.mult)
+    tt(R("lcol"), R("lcol"), R("li", 2 * L, 3 * L), A.add)
+    ts(PC1, G(R("li", 0, L), R("perm")), -1536.0, A.add, PR0, A.mult)
+    ts(PV1, G(R("lcol"), R("perm")), PR0, A.mult)
+
+    def lanes(t):
+        s = (5 * t) % 16
+        mm(R("Q0", 0, 48), R("Ib"), R("cst", 12, 60), True, False)
+        toA(R("Q0", 24, 48), "pr1", False)
+        toN(R("Q0", 12, 24), "pr1", False)
+        toN(R("Q0", 0, 12), "pr1", True, at=L)
+        toLanes("Q1", "pr1")
+        mm(R("Q2", 0, L), R("Ib"), R("DGc", s, s + L), True, False)
+        for r in range(16):
+            mm(R("Q2", r, L, 16), Sr((r + s) % 16), R("pr1", L + 12 * r, L + 12 * r + 12), False, r == 15)
+        cp(R("I"), R("Q0", 0, 48))
+        act(R("cN"), R("Q0", 0, 12))
+        rivals("o", ("Q0", 12), [("Q1", "a")] * NS, R("oo"), PB)
+        act(R("t4"), R("Q2", 0, L))
+        ts(R("D"), R("I", 12, 36), 1, A.bitwise_and)
+        cp(R("nu"), R("I", 0, 24))
+        cp(R("QO", 0, 24, 2), R("I", 36, 48))
+        ts(R("QO", 1, 24, 2), R("D", 12, 24), float(XS), A.add)
+        ts(R("sg", 0, 24), R("D"), -2.0, A.mult, 1.0, A.add)
+        ts(R("cm"), R("I", 36, 48), KW - 1, A.bitwise_and)
+        ts(R("d4", 0, 12), R("D", 12, 24), 4096.0, A.mult, 1536.0, A.add)
+        tt(R("oq"), R("I", 24, 36), R("sg", 12, 24), A.add)
+        cp(R("cu"), R("cm"))
+        cp(R("ou"), R("oq"))
+        act(R("sb", 0, 12), R("sg", 0, 12), scale=-1.0)
+        act(R("SX"), G(R("sg", 0, 12), R("cJ")), scale=2.0 ** -7)
+        act(R("QS"), G(R("X"), R("QO")))
+        act(R("qN"), G(R("X"), R("nu", 0, 12)))
+        for b in range(3):
+            mm(R("MA", 128 * b, 128 * b + 128), R("QS", 128 * b, 128 * b + 128), R("Ib"), True, True)
+        mm(R("MB", 0, 12), R("Ib"), R("sb", 0, 12), True, False)
+        for r in range(16):
+            mm(R("MB", 0, 12), Sr(r), R("qN", r, L, 16), False, r == 15)
+        act(R("QT"), R("MA", 0, 384))
+        act(R("LN", 0, 12), R("MB", 0, 12), scale=-1.0)
+        act(R("LX"), G(R("LN", 0, 12), R("cJ")))
+        for c in range(4):
+            spread(c)
+        mm(R("P1", 0, L), R("If"), R("LX"), True, False)
+        mm(R("P2", 0, L), R("I10"), R("LX"), True, False)
+        act(R("f4"), R("qN"), scale=0.25, bias=31.5 + 192.0)
+
+    def spread(c):
+        b, h = divmod(c, 2)
+        mm(R("Q%d" % (c % 4)), R("QT", 128 * b, 128 * b + 128), R("Sel", 512 * h, 512 * h + 512), True, True)
+
+    def rivals(k, w, bk, off, spare, shift=0.0):
+        wt = R(w[0], w[1], w[1] + 12)
+        if any(e == "a" for _, e in bk):
+            act(R("nw" + k, 0, 12), wt, scale=-4096.0, bias=4096.0 * shift)
+        act(R("sw" + k, 0, 12), wt, scale=-1.0, bias=spare)
+        for j in range(12):
+            s, a = divmod(j, MB)
+            o = R("eq" + k, SL * s + SEG[a] + 1, SL * s + SEG[a + 1] - 1)
+            i = R(bk[s][0], 16 * MB * s, 16 * j + 16)
+            if bk[s][1] == "a":
+                act(o, i, AF.Abs, scale=4096.0, bias=R("nw" + k, j, j + 1))
+            else:
+                ts(o, i, R(w[0], w[1] + j, w[1] + j + 1), A.not_equal, 4096.0, A.mult)
+        scan(R("ds" + k), R("sc2"), R("eq" + k), 0.0, A.add, A.min)
+        tt(R("of" + k), G(R("ds" + k), R("cOff", 0, 1)), R("sw" + k), A.min)
+        ts(off, R("of" + k), -1.0, A.mult, spare, A.add)
+
+    def append(cols, t, name, base, t1, t2):
+        s = (5 * t) % 16
+        tt(R(t1), G(R("B"), cols), R("NDG", s, s + L), A.mult)
+        for j in range(NS - 1, -1, -1):
+            a, b = 16 * MB * j, 16 * MB * (j + 1)
+            tt(G(R("B"), R(name, base + PS * j, base + PS * j + MB)), R(t1, a, b), R(t2, a, b), A.add)
+
+    lanes(0)
+    for t in range(ST):
+        last = t == ST - 1
+        to = T.cores[(rank + 1 + t % (N - 1)) % N]
+        cp(R("E"), G(R("Bi") if t == 0 else R("B"), R("ou")))
+        done, prev = [0, 0], []
+
+        def sums(c, which):
+            src, wt, o = (("xe", "Wd10", "P2"), ("H", "Wd", "P1"))[which]
+            while 192 * (done[which] + 1) <= 512 * (c + 1):
+                r = done[which]
+                mm(R(o, 0, L), Sr(r, wt), R(src, 192 * r, 192 * r + 192), False, r == 15)
+                done[which] += 1
+
+        for c in range(6):
+            o, i = R("xe", 512 * c, 512 * c + 512), G(R("X"), R("E", 32 * c, 32 * c + 32))
+            if c in VGAT:
+                cp(o, i)
+            else:
+                act(o, i)
+                if prev:
+                    ops[-1]["order"].add(prev[-1])
+                prev.append(len(ops) - 1)
+            sums(c, 0)
+        ts(R("Ec"), R("E"), -1536.0, A.add)
+        append(R("nu", 12, 24), t, "oo", 0, "t3", "t4")
+        for c in range(6):
+            tt(R("H", 512 * c, 512 * c + 512), R("xe", 512 * c, 512 * c + 512), R("Q%d" % (c % 4)), A.min)
+            sums(c, 1)
+            if c + 4 < 6:
+                spread(c + 4)
+        act(R("a1"), R("P2", 0, L), bias=196608.0)
+        act(R("Y"), R("P2", 0, L), scale=512.0, bias=4096.0)
+        act(R("a2"), R("a1"), scale=-1.0, bias=196600.0)
+        mm(R("MB", 0, L), R("I9"), R("Y"), True, False)
+        mm(R("MB", 0, L), R("If"), R("a2"), False, True)
+        tt(R("tt"), R("SX"), R("P2", 0, L), A.mult)
+        ts(R("R1"), R("P1", 0, L), R("th", 0, 1), A.add)
+        tt(R("P1", 256, 256 + L), R("R1"), R("P1", 0, L), A.subtract)
+        tt(R("R2"), R("R1"), R("MB", 0, L), A.add)
+        tt(R("P1", 256, 256 + L), R("P1", 256, 256 + L), R("tt"), A.is_gt)
+        tt(R("P1", 256, 256 + L), R("P1", 256, 256 + L), R("Y"), A.mult)
+        tt(R("key"), R("R2"), R("P1", 256, 256 + L), A.subtract)
+        scan(R("scn"), R("sc1"), R("key"), 0.0, A.add, A.max)
+        best = R("scn", 15, L, 16)
+        ts(R("Z"), best, 1024.0, A.mult, float(2 ** 23 - 512 + 8), A.add)
+        ts(R("hit"), best, -4090.0, A.is_gt)
+        ts(R("kk"), R("Z"), 5, A.arith_shift_right, 15, A.bitwise_and)
+        ts(R("lo"), R("Z"), 31, A.bitwise_and)
+        cp(R("kb", 0, 12), R("kk"))
+        for r in range(16):
+            mm(R("MA", 12 * r, 12 * r + 12), Rr(r), R("kb", 0, 12), True, True)
+        ts(R("pa"), R("lo"), -10.0, A.add)
+        ts(R("z2"), R("Z"), 9, A.arith_shift_right)
+        tt(R("pb"), R("pa"), R("hit"), A.mult)
+        tt(R("pd"), R("pb"), R("z2"), A.subtract)
+        ts(R("pe"), R("pd"), 15, A.bitwise_and)
+        cp(R("pf", 0, 12), R("pe"))
+        for r in range(16):
+            mm(R("MB", 12 * r, 12 * r + 12), Rr(r), R("pf", 0, 12), True, True)
+        act(R("ms"), R("hit"), scale=-1.0, bias=1.0, acc=R("mc", 0, 1))
+        ts(R("MA", 0, L), R("MA", 0, L), PK, A.is_equal)
+        tt(R("prE"), R("Ec"), R("MA", 0, L), A.mult)
+        mm(R("Q0", 0, 12), R("Ib"), R("d4", 0, 12), True, False)
+        toA(R("Q0", 0, 12), "prE", True)
+        mm(R("Q1", 0, 12), R("Ib"), R("cst", 12, 24), True, False)
+        toN(R("Q1", 0, 12), "prE", True)
+        mm(R("P2", 0, 1), R("BOf"), R("mc", 0, 1), True, True)
+        mm(R("P1", 0, 12), R("Ib"), R("nid16", 0, 12), True, False)
+        mm(R("P1", 0, 12), R("I192"), R("hit"), False, True)
+        cp(R("su"), R("P1", 0, 12))
+        ts(R("mp"), R("MB", 0, L), PC, A.is_equal)
+        tt(R("pc2"), G(R("TT", 1536, 2048), R("cu")), R("mp"), A.mult)
+        cp(R("ei"), R("Q0", 0, 12))
+        ts(R("ej"), R("ei"), 4096 + KW - 1, A.bitwise_and)
+        cp(R("eo"), R("ej"))
+        tt(R("pv2"), G(R("TT", 512, 5120), R("eo")), R("mp"), A.mult)
+        mm(R("Q2", 0, 24), R("Ib"), R("cst", 0, 24), True, False)
+        toN(R("Q2", 12, 24), "pc2", False, rot=5 * t)
+        toN(R("Q2", 0, 12), "pv2", True)
+        for s in range(NS):
+            toLanes(SENT[s][0], "pv2", js=range(MB * s, MB * s + MB))
+        cp(R("eN"), R("Q1", 0, 12))
+        tt(R("pm"), R("Q1", 0, 12), R("cN"), A.subtract)
+        act(R("yN"), G(R("X"), R("eN")))
+        act(R("ymt", t, t + 1), R("P2", 0, 1))
+        tt(PV1, G(R("TT", 0, 4608), R("eo")), R("mp"), A.mult)
+        tt(R("pn"), R("pm"), R("hit"), A.mult)
+        tt(R("pl", 0, 12), R("pn"), R("cN"), A.add)
+        rivals("2", ("Q2", 0), SENT, R("m2", 16 * t, 16 * t + 16), PB)
+        cp(R("m1", 24 * t, 24 * t + 24), R("Q2", 0, 24))
+        send(R("m1", 24 * t, 24 * t + 24), R("r1", 24 * t, 24 * t + 24), "ra%d" % t, to)
+        send(R("m2", 16 * t, 16 * t + 16), R("r2", 16 * t, 16 * t + 16), "rb%d" % t, to)
+        s = (5 * t) % 16
+        ts(R("V", 0, 12), R("r1", 24 * t + 12, 24 * t + 24), -1536.0, A.add)
+        mm(R("P2", 0, L), R("Ib"), R("DGc", s, s + L), True, False)
+        for r in range(16):
+            e = (r + s) % 16
+            mm(R("P2", r, L, 16), R("EE", 128 * e, 128 * e + 128), R("V", 0, 12), False, r == 15)
+        act(R("t2"), R("P2", 0, L))
+        mm(R("MA", 0, L), R("Ib"), R("yN"), True, False)
+        mm(R("MA", 0, L), R("In"), R("f4"), False, True)
+        mm(R("MA", L, 2 * L), R("Ih"), R("yN"), True, False)
+        mm(R("MA", L, 2 * L), R("Ih"), R("qN"), False, True)
+        ts(R("p16", 0, 12), R("pl", 0, 12), -1536.0, A.add)
+        tt(PC1, G(R("TT", 1024, 1536), R("cu")), R("mp"), A.mult)
+        for r in range(16):
+            mm(R("MB", r, L, 16), Rr(r), R("p16", 0, 12), True, True)
+        act(R("zr"), R("MA", L, 2 * L), bias=127.25)
+        act(R("vals", 0, L), R("MA", 0, L), AF.Abs, bias=127.5 + 192.0)
+        act(R("zs"), R("zr"), bias=1.5 * 2 ** 23)
+        act(R("vals", L, 2 * L), R("zs"), bias=-1.5 * 2 ** 23)
+        act(R("nv"), G(R("vals"), R("su")), bias=-127.5)
+        rivals("p", ("pl", 0), [("MB", "a")] * NS, R("op"), PX, shift=1536.0)
+        for j in range(NS - 1, -1, -1):
+            cp(G(R("X"), R("op", PS * j, PS * j + MB)), R("nv", 16 * MB * j, 16 * MB * (j + 1)))
+        if not last:
+            act(R("hb", 0, 1), R("ymt", t, t + 1), scale=0.5, bias=143.75)
+            act(R("ab", 0, 1), R("ymt", t, t + 1), scale=1.0 / 16, bias=18.0 + 1.0 / 32)
+            act(R("th", 0, 1), R("hb", 0, 1), scale=-0.125, bias=R("ab", 0, 1))
+            lanes(t + 1)
+        else:
+            toLanes("Q0", "pr1", at=L)
+            toLanes("Q1", "pr1")
+            for b in range(8):
+                act(R("junk", 384 * b, 384 * b + 384), R("X", 384 * b, 384 * b + 384), bias=127.5, acc=R("yst", b, b + 1))
+        append(R("r1", 24 * t, 24 * t + 12), t, "r2", 16 * t, "t1", "t2")
+
+    dma("s", T.yb[:, 0:1024], R("B", 0, 1024))
+    dma("a", T.yb[:, 1024:2048], R("B", 1024, 2048))
+    ts(R("oc", 0, L), R("Q0", 0, L), 1536.0, A.add)
+    cp(R("oi"), R("Q1", 0, L))
+    ts(R("oj", 0, L), R("oi"), 1, A.arith_shift_right)
+    ts(R("oj", L, 2 * L), R("oi"), 1, A.bitwise_and)
+    cp(R("oc", L, 3 * L), R("oj"))
+    dma("s", T.yc[:], R("oc", 0, L, ps=16))
+    dma("s", T.ys[:], R("yst"))
+    dma("s", T.ym[:], R("ymt", 0, ST, ps=16))
+    dma("s", T.yv[:], R("oc", L, 2 * L, ps=16))
+    dma("s", T.yd[:], R("oc", 2 * L, 3 * L, ps=16))
+
+    if "order" not in PLAN:
+        PLAN["order"] = plan(ops)
+        PLAN["ops"] = ops
+    order = PLAN["order"]
+    where = {i: k for k, i in enumerate(order)}
+    queue = {"v": g.vector, "a": g.scalar, "p": g.tensor, "g": g, "s": g.sync}
+    qsem = {"v": "qv", "a": "qa", "p": "qp", "g": "qg"}
+    narr = engines_to(T.cores[(rank + 1) % N])[1]
+    need, waits = set(), {}
+    for i, o in enumerate(ops):
+        latest = {}
+        for d in o["deps"]:
+            if ops[d]["kind"] == "c":
+                q = ops[d]["q"]
+                if q not in latest or where[d] > where[latest[q]]:
+                    latest[q] = d
+        waits[i] = set(d for d in o["deps"] if ops[d]["kind"] in "dx") | set(latest.values())
+        need |= waits[i]
+    count, mark, clock, known = {}, {}, {}, {q: {} for q in queue}
+    for i in order:
+        q, sem, kind = ops[i]["q"], ops[i]["sem"], ops[i]["kind"]
+        if kind == "x":
+            mark[i] = (sem, narr)
+            clock[i] = {sem: narr}
+            continue
+        kn = known[q]
+        for d in sorted(waits[i], key=lambda k: -where[k]):
+            s, v = mark[d]
+            if kn.get(s, 0) < v:
+                queue[q].wait_ge(T.sem[s], v)
+            for s2, v2 in clock[d].items():
+                if kn.get(s2, 0) < v2:
+                    kn[s2] = v2
+        ins = ops[i]["call"]()
+        if kind == "d":
+            ins.then_inc(T.sem[sem], 16)
+            mark[i] = (sem, 16)
+            count[sem] = 16
+        elif kind == "c" and i in need:
+            s = qsem[q]
+            count[s] = count.get(s, 0) + 1
+            ins.then_inc(T.sem[s], 1)
+            mark[i] = (s, count[s])
+        if i in mark:
+            clock[i] = dict(kn)
+            clock[i][mark[i][0]] = mark[i][1]
+    for s, v in count.items():
+        if max(kn.get(s, 0) for kn in known.values()) < v:
+            g.wait_ge(T.sem[s], v)
+    g.wait_ge(T.sem.sent, nsent[0])

@@ -19,7 +19,7 @@ def _sb(n, d):
 
 SCRATCH = {
     "xin": _sb(S, BF), "X": _sb(XS + 16, BF), "Bi": _sb(NV, I32), "B": _sb(BS, F32),
-    "k1": _sb(KW, I32), "ka": _sb(KW, I32), "TT": _sb(5120, F32),
+    "k1": _sb(KW, I32), "ka": _sb(KW, I32), "TT": _sb(4608, F32), "TW": _sb(4096 + S, F32), "ew": _sb(12, U16),
     "li": _sb(3 * L, I32), "lcol": _sb(L, F32),
     "pi": _sb(4, I32), "pj": _sb(4, I32), "pc": _sb(16, F32), "it": _sb(1024, F32), "it2": _sb(208, F32),
     "it4": _sb(144, F32), "it5": _sb(128, F32), "it6": _sb(128, F32), "it7": _sb(16, F32),
@@ -66,16 +66,17 @@ for _n, (_w, _s, _d) in BUFS.items():
         SCRATCH[_a] = _sb(_end[_a], _d)
     else:
         PLACE[_n] = (_n, 0)
-NDMA = 24
+NDMA = 32
 SEMAPHORES = (["qv", "qa", "qp", "qg", "sent"] + ["d%d" % i for i in range(NDMA)]
               + ["ra%d" % t for t in range(ST)] + ["rb%d" % t for t in range(ST)])
 PSUM = ("Q0", "Q1", "Q2", "Q3", "P1", "P2", "MA", "MB")
 WIDTH = {F32: 4, I32: 4, BF: 2, F16: 2, U16: 2}
-CYC, PEC, GAT, SCA, HOP, FAR, FIX = 0.83, 0.42, 1.5, 3.5, 90.0, 2500.0, 50.0
+CYC, PEC, GAT, SCA, HOP, FAR, FIX = 0.83, 0.42, 1.5, 3.5, 140.0, 3000.0, 50.0
 PLAN = {}
 SENT = [("Q3", "v"), ("P1", "a"), ("P2", "v")]
-ROUNDS, NOISE = 400, 1500.0
-VGAT = (1,)
+ROUNDS, NOISE = 200, 1500.0
+PIECES = [(0, 512, "a"), (512, 1152, "v"), (1152, 1536, "a"), (1536, 2048, "a"), (2048, 2560, "a"), (2560, 2880, "a"),
+          (2880, 3072, "a")]
 
 
 def plan(ops):
@@ -309,7 +310,7 @@ def rank_program(g, core, T, topo):
 
     ms(R("li"), 0)
     dma("s", R("li", 0, L, ps=16), T.lc[:])
-    dma("g", R("li", L, 2 * L, ps=16), T.lv[:])
+    dma("a", R("li", L, 2 * L, ps=16), T.lv[:])
     dma("s", R("li", 2 * L, 3 * L, ps=16), T.ld[:])
     dma("s", R("Bi"), T.bnd[:])
     dma("a", R("xin", 0, S // 2), T.x[:, 0:S // 2])
@@ -389,9 +390,14 @@ def rank_program(g, core, T, topo):
     ts(R("TT", 0, 512), R("ka"), 2.0, A.mult, PPI, A.add)
     act(R("TT", 4096, 4608), R("TT", 0, 512), bias=PNI)
     ts(R("TT", 1024, 1536), R("k1"), -1536.0, A.add)
-    for o in (0, 1024, 4096):
-        dma("s", R("TT", o + 512, o + 1024, ps=2), R("TT", o, o + 512, p0=1, ps=2))
-        dma("s", R("TT", o + 512, o + 1024, p0=1, ps=2), R("TT", o, o + 512, ps=2))
+    act(R("TT", 512, 1024), R("TT", 0, 512))
+    for nm, o, k in (("TW", 0, 0), ("TW", 4096, 4096), ("TT", 1024, 1536)):
+        dma("s", R(nm, k, k + 512, ps=2), R("TT", o, o + 512, p0=1, ps=2))
+        dma("s", R(nm, k, k + 512, p0=1, ps=2), R("TT", o, o + 512, ps=2))
+    for o in (0, 4096):
+        for k in range(1, 6):
+            dma("s", R("TW", o + 512 * k, o + 512 * k + 512), R("TW", o, o + 512))
+    iota(R("TW", S, 4096), [[0, 4096 - S]], 0, 0)
     ts(R("X", 0, 1536), R("xin", 0, 1536), -127.5, A.add)
     ts(R("X", 1536, S), R("xin", 1536, S), -127.5, A.add)
     ms(R("X", S, XS), 0.0)
@@ -422,7 +428,7 @@ def rank_program(g, core, T, topo):
         ts(R("QO", 1, 24, 2), R("D", 12, 24), float(XS), A.add)
         ts(R("sg", 0, 24), R("D"), -2.0, A.mult, 1.0, A.add)
         ts(R("cm"), R("I", 36, 48), KW - 1, A.bitwise_and)
-        ts(R("d4", 0, 12), R("D", 12, 24), 4096.0, A.mult, 1536.0, A.add)
+        act(R("d4", 0, 12), R("sg", 12, 24), scale=-2048.0, bias=3584.0)
         tt(R("oq"), R("I", 24, 36), R("sg", 12, 24), A.add)
         cp(R("cu"), R("cm"))
         cp(R("ou"), R("oq"))
@@ -450,9 +456,12 @@ def rank_program(g, core, T, topo):
 
     def rivals(k, w, bk, off, spare, shift=0.0):
         wt = R(w[0], w[1], w[1] + 12)
-        if any(e == "a" for _, e in bk):
+        if any(e == "v" for _, e in bk):
+            ts(R("nw" + k, 0, 12), wt, -4096.0, A.mult)
+            act(R("sw" + k, 0, 12), R("nw" + k, 0, 12), scale=2.0 ** -12, bias=spare)
+        else:
             act(R("nw" + k, 0, 12), wt, scale=-4096.0, bias=4096.0 * shift)
-        act(R("sw" + k, 0, 12), wt, scale=-1.0, bias=spare)
+            act(R("sw" + k, 0, 12), wt, scale=-1.0, bias=spare)
         for j in range(12):
             s, a = divmod(j, MB)
             o = R("eq" + k, SL * s + SEG[a] + 1, SL * s + SEG[a + 1] - 1)
@@ -481,26 +490,27 @@ def rank_program(g, core, T, topo):
 
         def sums(c, which):
             src, wt, o = (("xe", "Wd10", "P2"), ("H", "Wd", "P1"))[which]
-            while 192 * (done[which] + 1) <= 512 * (c + 1):
+            while 192 * (done[which] + 1) <= c:
                 r = done[which]
                 mm(R(o, 0, L), Sr(r, wt), R(src, 192 * r, 192 * r + 192), False, r == 15)
                 done[which] += 1
 
-        for c in range(6):
-            o, i = R("xe", 512 * c, 512 * c + 512), G(R("X"), R("E", 32 * c, 32 * c + 32))
-            if c in VGAT:
+        for lo, hi, e in PIECES:
+            o, i = R("xe", lo, hi), G(R("X"), R("E", lo // 16, hi // 16))
+            if e == "v":
                 cp(o, i)
             else:
                 act(o, i)
                 if prev:
                     ops[-1]["order"].add(prev[-1])
                 prev.append(len(ops) - 1)
-            sums(c, 0)
+            sums(hi, 0)
         ts(R("Ec"), R("E"), -1536.0, A.add)
         append(R("nu", 12, 24), t, "oo", 0, "t3", "t4")
         for c in range(6):
-            tt(R("H", 512 * c, 512 * c + 512), R("xe", 512 * c, 512 * c + 512), R("Q%d" % (c % 4)), A.min)
-            sums(c, 1)
+            for lo, hi in ([(0, 512)] if c < 5 else [(0, 320), (320, 512)]):
+                tt(R("H", 512 * c + lo, 512 * c + hi), R("xe", 512 * c + lo, 512 * c + hi), R("Q%d" % (c % 4), lo, hi), A.min)
+                sums(512 * c + hi, 1)
             if c + 4 < 6:
                 spread(c + 4)
         act(R("a1"), R("P2", 0, L), bias=196608.0)
@@ -517,16 +527,15 @@ def rank_program(g, core, T, topo):
         tt(R("key"), R("R2"), R("P1", 256, 256 + L), A.subtract)
         scan(R("scn"), R("sc1"), R("key"), 0.0, A.add, A.max)
         best = R("scn", 15, L, 16)
-        ts(R("Z"), best, 1024.0, A.mult, float(2 ** 23 - 512 + 8), A.add)
+        ts(R("Z"), best, 1024.0, A.mult, float(2 ** 23 - 512 + 14), A.add)
         ts(R("hit"), best, -4090.0, A.is_gt)
         ts(R("kk"), R("Z"), 5, A.arith_shift_right, 15, A.bitwise_and)
         ts(R("lo"), R("Z"), 31, A.bitwise_and)
         cp(R("kb", 0, 12), R("kk"))
         for r in range(16):
             mm(R("MA", 12 * r, 12 * r + 12), Rr(r), R("kb", 0, 12), True, True)
-        ts(R("pa"), R("lo"), -10.0, A.add)
         ts(R("z2"), R("Z"), 9, A.arith_shift_right)
-        tt(R("pb"), R("pa"), R("hit"), A.mult)
+        tt(R("pb"), R("lo"), R("hit"), A.mult)
         tt(R("pd"), R("pb"), R("z2"), A.subtract)
         ts(R("pe"), R("pd"), 15, A.bitwise_and)
         cp(R("pf", 0, 12), R("pe"))
@@ -545,10 +554,11 @@ def rank_program(g, core, T, topo):
         cp(R("su"), R("P1", 0, 12))
         ts(R("mp"), R("MB", 0, L), PC, A.is_equal)
         tt(R("pc2"), G(R("TT", 1536, 2048), R("cu")), R("mp"), A.mult)
+        cp(R("ew"), R("Q0", 0, 12))
         cp(R("ei"), R("Q0", 0, 12))
         ts(R("ej"), R("ei"), 4096 + KW - 1, A.bitwise_and)
         cp(R("eo"), R("ej"))
-        tt(R("pv2"), G(R("TT", 512, 5120), R("eo")), R("mp"), A.mult)
+        tt(R("pv2"), G(R("TW"), R("ew")), R("mp"), A.mult)
         mm(R("Q2", 0, 24), R("Ib"), R("cst", 0, 24), True, False)
         toN(R("Q2", 12, 24), "pc2", False, rot=5 * t)
         toN(R("Q2", 0, 12), "pv2", True)
@@ -561,9 +571,9 @@ def rank_program(g, core, T, topo):
         tt(PV1, G(R("TT", 0, 4608), R("eo")), R("mp"), A.mult)
         tt(R("pn"), R("pm"), R("hit"), A.mult)
         tt(R("pl", 0, 12), R("pn"), R("cN"), A.add)
-        rivals("2", ("Q2", 0), SENT, R("m2", 16 * t, 16 * t + 16), PB)
         cp(R("m1", 24 * t, 24 * t + 24), R("Q2", 0, 24))
         send(R("m1", 24 * t, 24 * t + 24), R("r1", 24 * t, 24 * t + 24), "ra%d" % t, to)
+        rivals("2", ("Q2", 0), SENT, R("m2", 16 * t, 16 * t + 16), PB)
         send(R("m2", 16 * t, 16 * t + 16), R("r2", 16 * t, 16 * t + 16), "rb%d" % t, to)
         s = (5 * t) % 16
         ts(R("V", 0, 12), R("r1", 24 * t + 12, 24 * t + 24), -1536.0, A.add)

@@ -4,61 +4,59 @@ from concourse.mybir import dt, AluOpType, AxisListType, ActivationFunctionType
 
 S, NV, KW, L, ST = 3072, 2048, 512, 192, 7
 F32, BF, F16, I32, U16 = "float32", "bfloat16", "float16", "int32", "uint16"
-MB = 4
-NS = 12 // MB
-PS = MB
-SEG = [sum(16 * (b + 1) + 2 for b in range(a)) for a in range(MB + 1)]
+MB, NS = 4, 3
+SEG = [8 * a * (a + 1) for a in range(MB + 1)]
 SL = SEG[MB]
-NE = SL * NS
 XS, BS = S + 16 * MB, NV + 16 * MB
+C0 = 512.0 * 12288
 
 
 def _sb(n, d):
-    return ("sbuf", [128, n], d)
+    return ("sbuf", [128] + (n if isinstance(n, list) else [n]), d)
+
+
+def _ps(n):
+    return ("psum", [128] + n, F32)
 
 
 SCRATCH = {
-    "xin": _sb(S, BF), "X": _sb(XS + 16, BF), "Bi": _sb(NV, I32), "B": _sb(BS, F32),
-    "k1": _sb(KW, I32), "ka": _sb(KW, I32), "TT": _sb(4608, F32), "TW": _sb(4096 + S, F32), "ew": _sb(12, U16),
-    "li": _sb(3 * L, I32), "lcol": _sb(L, F32),
-    "pi": _sb(4, I32), "pj": _sb(4, I32), "pc": _sb(16, F32), "it": _sb(1024, F32), "it2": _sb(208, F32),
-    "it4": _sb(144, F32), "it5": _sb(128, F32), "it6": _sb(128, F32), "it7": _sb(16, F32),
-    "Wd": _sb(144, BF), "Wd10": _sb(144, BF), "BO": _sb(128, BF), "BOf": _sb(128, F32), "RR": _sb(2048, BF),
-    "Ib": _sb(128, BF), "Ih": _sb(128, BF), "In": _sb(128, BF), "If": _sb(128, F32), "I10": _sb(128, F32), "Sel": _sb(1024, BF),
-    "DG": _sb(208, F32), "NDG": _sb(208, F32), "sc1": _sb(L, F32), "sc2": _sb(NE, F16), "sc3": _sb(SL, F32),
-    "EE": _sb(2048, BF), "DGc": _sb(208, BF), "I9": _sb(128, F32), "I192": _sb(128, BF), "nid16": _sb(16, F16),
-    "cJ": _sb(12, U16), "perm": _sb(12, U16), "nid": _sb(12, F32), "nq": _sb(12, I32), "nf": _sb(12, F32), "cst": _sb(64, BF),
-    "row": _sb(16, F32), "rowd": _sb(16, F32), "col": _sb(8, F32), "cOff": _sb(2, U16),
-    "E": _sb(L, U16), "Ec": _sb(L, F16), "xe": _sb(S, BF), "H": _sb(S, F16),
-    "QS": _sb(2 * L, BF), "QT": _sb(2 * L, BF), "qN": _sb(L, BF), "f4": _sb(L, BF), "yN": _sb(L, BF),
-    "LN": _sb(16, F32), "LX": _sb(L, F32), "SX": _sb(L, F32), "th": _sb(4, F32), "hb": _sb(4, BF), "ab": _sb(4, F32),
-    "Y": _sb(L, F32), "a1": _sb(L, F32), "a2": _sb(L, F32), "tt": _sb(L, F32), "R1": _sb(L, I32), "R2": _sb(L, F32),
-    "key": _sb(L, F32), "scn": _sb(L, F32),
-    "Z": _sb(12, I32), "kk": _sb(12, I32), "kb": _sb(16, BF), "z2": _sb(12, I32), "lo": _sb(12, I32), "hit": _sb(12, BF),
-    "pa": _sb(12, F32), "pb": _sb(12, F32), "pd": _sb(12, I32), "pe": _sb(12, I32), "pf": _sb(16, BF),
+    "xin": _sb(S, BF), "X": _sb(XS + NV, BF), "Bi": _sb(NV, I32), "B": _sb(BS, F32),
+    "K": _sb(S, I32), "ka": _sb(KW, I32), "TT": _sb(3 * S, F32),
+    "li": _sb(3 * L, I32), "lcol": _sb(L, F32), "ld0": _sb(L, BF),
+    "pi": _sb(16, I32), "pj": _sb(16, I32), "pc": _sb(16, F32), "pt": _sb(16, F32), "it": _sb(1024, BF), "it2": _sb(208, F32),
+    "it4": _sb(144, F32), "it5": _sb(128, F32), "it6": _sb(128, F32), "it7": _sb(16, F32), "it8": _sb(16, F32),
+    "Wd": _sb(144, BF), "BO": _sb(128, BF), "BOf": _sb(128, F32), "BO8": _sb(128, BF), "RR": _sb(2048, BF),
+    "Ib": _sb(128, BF), "Ih": _sb(128, BF), "In": _sb(128, BF), "I8": _sb(128, BF), "I192": _sb(128, BF), "I2": _sb(128, BF),
+    "I2n": _sb(128, BF), "I9": _sb(128, F32), "I16": _sb(128, BF), "Ie": _sb(128, BF), "Sw": _sb(128, BF),
+    "Sel": _sb(1024, BF), "DG": _sb(208, F32), "NDG": _sb(208, F32), "NDm": _sb(208, BF), "sc1": _sb(L, F32),
+    "DK": _sb(16, BF), "DP": _sb(48, BF), "MK": _sb(SL, BF), "AJ": _sb(NS * SL, BF), "MJ": _sb(NS * SL, BF),
+    "SP": _sb(12 * (ST + 1), F32), "n8": _sb(16, BF), "cJ": _sb(12, U16), "nid16": _sb(16, F16), "cst": _sb(24, BF),
+    "E": _sb(L, U16), "Ec": _sb(L, F16), "xe": _sb(S, BF), "H": _sb(S, F16), "LT": _sb(128, F16), "cT": _sb(128, F16),
+    "QS": _sb(2 * L, BF), "QT": _sb(256, F16), "qN": _sb(L, BF), "f4": _sb(L, BF), "yN": _sb(L, BF), "kc": _sb(L, F16), "ke": _sb(L, F16),
+    "SX": _sb(L, F32), "th": _sb(4, F32), "hb": _sb(4, BF), "ab": _sb(4, F32),
+    "Y": _sb(L, F32), "h16": _sb(L, F16), "tt": _sb(L, BF), "R1": _sb(L, I32), "R1k": _sb(L, F32), "R2": _sb(L, F32),
+    "key": _sb(L, F32), "scn": _sb(L, I32),
+    "kk": _sb(12, I32), "ku": _sb(12, U16), "z2": _sb(12, I32), "lo": _sb(12, I32), "hit": _sb(12, BF),
+    "pb": _sb(12, F32), "pd": _sb(12, I32), "pe": _sb(12, I32), "pu": _sb(12, U16),
     "ms": _sb(12, F32), "mc": _sb(4, F32), "ymt": _sb(8, F32),
-    "prE": _sb(L, F16), "mp": _sb(L, F32), "pr1": _sb(2 * L, F16), "pv2": _sb(L, F16), "pc2": _sb(L, F16),
-    "ei": _sb(12, I32), "ej": _sb(12, I32), "eo": _sb(12, U16), "eN": _sb(12, U16),
+    "prE": _sb(L, F16), "mp": _sb(L, F32), "pr1": _sb([2 * NS, 64], F16), "pr2": _sb(2 * L, F16), "Lp": _sb([NS, 64], F16),
+    "ew": _sb(12, U16), "eN": _sb(12, U16), "c32": _sb(16, F32),
     "m1": _sb(24 * ST, U16), "m2": _sb(16 * ST, U16), "r1": _sb(24 * ST, U16), "r2": _sb(16 * ST, U16),
-    "pl": _sb(16, F32), "oo": _sb(16, U16), "op": _sb(16, U16), "V": _sb(16, F16),
-    "nw2": _sb(16, F32), "nwo": _sb(16, F32), "nwp": _sb(16, F32), "sw2": _sb(16, F32), "swo": _sb(16, F32), "swp": _sb(16, F32),
-    "eq2": _sb(NE, BF), "eqo": _sb(NE, BF), "eqp": _sb(NE, BF),
-    "ds2": _sb(NE, BF), "dso": _sb(NE, BF), "dsp": _sb(NE, BF),
-    "of2": _sb(16, F32), "ofo": _sb(16, F32), "ofp": _sb(16, F32),
+    "oo": _sb(16, U16), "op": _sb(16, U16), "aT2": _sb(128 * ST, F16), "aTo": _sb(128, F16), "aTp": _sb(128, F16),
+    "ds2": _sb(16, F32), "dso": _sb(16, F32), "dsp": _sb(16, F32),
     "t1": _sb(L, F32), "t2": _sb(L, F32), "t3": _sb(L, F32), "t4": _sb(L, F32),
-    "pm": _sb(12, F32), "pn": _sb(12, F32), "p16": _sb(32, F16), "so": _sb(12, F32), "sq": _sb(12, F32), "su": _sb(12, U16),
-    "zr": _sb(L, F32), "zs": _sb(L, F32), "vals": _sb(2 * L, F32), "nv": _sb(L, BF),
-    "I": _sb(48, I32), "D": _sb(24, I32), "cm": _sb(12, I32), "cu": _sb(12, U16), "nu": _sb(24, U16), "QO": _sb(24, U16),
-    "d4": _sb(16, BF), "sg": _sb(32, F32), "sb": _sb(16, BF), "oq": _sb(12, F32), "ou": _sb(12, U16), "cN": _sb(12, F32), "cR": _sb(12, F32),
-    "yst": _sb(8, F32), "junk": _sb(S, BF), "oc": _sb(3 * L, F32), "oi": _sb(L, I32), "oj": _sb(2 * L, I32),
-    "Q0": ("psum", [128, 512], F32), "Q1": ("psum", [128, 512], F32), "Q2": ("psum", [128, 512], F32), "Q3": ("psum", [128, 512], F32),
-    "P1": ("psum", [128, 512], F32), "P2": ("psum", [128, 512], F32), "MA": ("psum", [128, 512], F32), "MB": ("psum", [128, 512], F32),
+    "pm": _sb(12, F32), "pn": _sb(12, F32), "p16": _sb(16, F16), "su": _sb(12, U16), "cc": _sb(12, F32),
+    "vals": _sb(2 * L, I32), "nv": _sb(L, BF),
+    "D0": _sb(12, BF), "D1": _sb(12, BF), "oN": _sb(12, U16), "cu": _sb(12, U16), "QO": _sb(24, U16), "ou": _sb(12, U16), "Sd": _sb(12, F32),
+    "yst": _sb(8, F32), "ysv": _sb(8, F32), "oc": _sb(3 * L, F32), "oi": _sb(L, I32), "oj": _sb(2 * L, I32),
+    "Q0": _ps([512]), "Q1": _ps([512]), "Q2": _ps([512]), "P1": _ps([512]), "P2": _ps([512]), "MA": _ps([512]), "MB": _ps([512]),
+    "RV": _ps([NS, 170]),
 }
 BUFS = dict(SCRATCH)
 PLACE = {}
 _end = {}
 for _n, (_w, _s, _d) in BUFS.items():
-    if _w == "sbuf" and _s[1] <= 48:
+    if _w == "sbuf" and len(_s) == 2 and _s[1] <= 48:
         _a = "short_" + _d
         PLACE[_n] = (_a, _end.get(_a, 0))
         _end[_a] = _end.get(_a, 0) + (_s[1] + 15) // 16 * 16
@@ -66,17 +64,19 @@ for _n, (_w, _s, _d) in BUFS.items():
         SCRATCH[_a] = _sb(_end[_a], _d)
     else:
         PLACE[_n] = (_n, 0)
-NDMA = 32
+SCRATCH["RV"] = SCRATCH.pop("RV")
+NDMA = 44
 SEMAPHORES = (["qv", "qa", "qp", "qg", "sent"] + ["d%d" % i for i in range(NDMA)]
               + ["ra%d" % t for t in range(ST)] + ["rb%d" % t for t in range(ST)])
-PSUM = ("Q0", "Q1", "Q2", "Q3", "P1", "P2", "MA", "MB")
+PSUM = ("Q0", "Q1", "Q2", "P1", "P2", "MA", "MB", "RV")
 WIDTH = {F32: 4, I32: 4, BF: 2, F16: 2, U16: 2}
-CYC, PEC, GAT, SCA, HOP, FAR, FIX = 0.83, 0.42, 1.5, 3.5, 140.0, 3000.0, 50.0
+CYC, PEC, GAT, SCA, HOP, FAR, FIX, DL, DB = 0.83, 0.42, 1.5, 3.5, 170.0, 2300.0, 50.0, 1500.0, 200.0
 PLAN = {}
-SENT = [("Q3", "v"), ("P1", "a"), ("P2", "v")]
 ROUNDS, NOISE = 200, 1500.0
-PIECES = [(0, 512, "a"), (512, 1152, "v"), (1152, 1536, "a"), (1536, 2048, "a"), (2048, 2560, "a"), (2560, 2880, "a"),
-          (2880, 3072, "a")]
+PIECES = [(0, 32, "a"), (32, 72, "v"), (72, 96, "a"), (96, 128, "a"), (128, 160, "a"), (160, 180, "a"), (180, 192, "a")]
+MINS = [0, 32, 64, 96, 128, 160, 180, 192]
+ESPLIT, YSA = 32, 5
+ON = dict(cT="a", ku="v", pu="a", ew="v", aT2="a", aTo="a", aTp="a", m1="a", ou="a", R1="v")
 
 
 def plan(ops):
@@ -166,16 +166,21 @@ def rank_program(g, core, T, topo):
         w = BUFS[name][1][1]
         hi = w if hi is None else hi
         t, o = T[PLACE[name][0]], PLACE[name][1]
-        if (p0, p1, ps) == (0, 128, 1):
-            ap = t[:, o + lo:o + hi] if step == 1 else t[:, o + lo:o + hi:step]
-        else:
-            ap = t[p0:p1:ps, o + lo:o + hi]
-        return (ap, [(name, lo, hi)], [], len(range(lo, hi, step)), WIDTH[BUFS[name][2]], name in PSUM)
+        rows = slice(None) if (p0, p1, ps) == (0, 128, 1) else slice(p0, p1, ps)
+        ap = t[rows, o + lo:o + hi] if step == 1 else t[rows, o + lo:o + hi:step]
+        cols = sum(1 << c for c in range(lo, hi, step)) if step > 1 else (1 << hi) - (1 << lo)
+        return (ap, [(name, cols)], [], len(range(lo, hi, step)), WIDTH[BUFS[name][2]], name in PSUM)
+
+    def M(name, *idx):
+        shape = BUFS[name][1][1:]
+        flat = np.arange(int(np.prod(shape))).reshape(shape)[idx]
+        return (T[name][(slice(None),) + idx], [(name, sum(1 << int(c) for c in flat.flat))], [], int(flat.size),
+                WIDTH[BUFS[name][2]], name in PSUM)
 
     def G(win, off):
         return (win[0].indirect(off[0]), win[1], off[1], 16 * off[3], win[4], False)
 
-    def add(q, call, outs, ins, cost, kind="c", sem=None, lat=0.0, after=()):
+    def add(q, call, outs, ins, cost, kind="c", sem=None, lat=0.0, after=(), wait=()):
         me = len(ops)
         acc = []
         for o in outs:
@@ -183,31 +188,31 @@ def rank_program(g, core, T, topo):
         for o in ins:
             if isinstance(o, tuple):
                 acc += [(r, False) for r in o[1] + o[2]]
-        deps, order = set(), set(after)
-        for (name, lo, hi), wr in acc:
+        deps, order = set(wait), set(after)
+        for (name, cols), wr in acc:
             ps = name in PSUM
             if ps and name in bank:
                 order.add(bank[name])
             for a in seen.get(name, []):
-                other = ops[a[2]]
+                other = ops[a[1]]
                 same = other["q"] == q and other["kind"] == "c" and kind == "c"
                 if ps and not same:
-                    deps.add(a[2])
-                elif wr and a[3] and kind == "d" and other["kind"] == "d":
+                    deps.add(a[1])
+                elif wr and a[2] and kind == "d" and other["kind"] == "d":
                     continue
-                elif a[0] < hi and lo < a[1] and (wr or a[3]) and not (same and q == "p" and ps):
-                    deps.add(a[2])
-        for (name, lo, hi), wr in acc:
+                elif a[0] & cols and (wr or a[2]) and not (same and q == "p" and ps):
+                    deps.add(a[1])
+        for (name, cols), wr in acc:
             lst = seen.setdefault(name, [])
             if name in PSUM:
-                lst[:] = [a for a in lst if ops[a[2]]["q"] == q]
+                lst[:] = [a for a in lst if ops[a[1]]["q"] == q]
                 bank[name] = me
             if wr:
-                lst[:] = [a for a in lst if not (lo <= a[0] and a[1] <= hi and a[2] in deps)]
+                lst[:] = [a for a in lst if not (a[0] & ~cols == 0 and a[1] in deps)]
         ops.append({"q": q, "call": call, "deps": deps, "order": order - deps, "sem": sem, "kind": kind, "cost": cost, "lat": lat,
                     "tag": (outs[0][1][0][0] if outs else kind)})
-        for (name, lo, hi), wr in acc:
-            seen[name].append([lo, hi, me, wr])
+        for (name, cols), wr in acc:
+            seen[name].append([cols, me, wr])
         return me
 
     def a0(x):
@@ -238,7 +243,10 @@ def rank_program(g, core, T, topo):
     def scan(o, d0, d1, init, op0, op1):
         add("v", lambda: g.vector.tensor_tensor_scan(o[0], d0[0], d1[0], init, op0, op1), [o], [d0, d1], vcost(o, [d0, d1]))
 
-    def red(o, i):
+    def least(o, i):
+        add("v", lambda: g.vector.tensor_reduce(o[0], i[0], AxisListType.X, A.min, apply_absolute_value=True), [o], [i], FIX + i[3] * CYC)
+
+    def total(o, i):
         add("v", lambda: g.vector.tensor_reduce(o[0], i[0], AxisListType.X, A.add), [o], [i], FIX + i[3] * CYC)
 
     def ms(o, c):
@@ -252,8 +260,15 @@ def rank_program(g, core, T, topo):
         else:
             add("a", lambda: g.scalar.activation(o[0], i[0], f, bias=a0(bias), scale=scale, accum_out=acc[0]), [o, acc], [i, bias], c + 20)
 
+    def plus(k, o, i, bias=0.0):
+        if ON[k] == "a":
+            act(o, i, bias=bias)
+        else:
+            ts(o, i, bias, A.add)
+
     def mm(o, l, r, start, stop):
-        add("p", lambda: g.tensor.matmul(o[0], l[0], r[0], start, stop), [o], [l, r], max(64, r[3]) * PEC * (4 if r[4] == 4 else 1))
+        add("p", lambda: g.tensor.matmul(o[0], l[0], r[0], start, stop), [o], [l, r],
+            max(min(64, l[3]), r[3]) * PEC * (4 if r[4] == 4 else 1))
 
     def iota(o, pat, base, cm):
         c = 130.0 + 2 * CYC * o[3]
@@ -262,13 +277,16 @@ def rank_program(g, core, T, topo):
         else:
             add("g", lambda: g.iota(o[0], pat, base, cm, allow_small_or_imprecise_dtypes=True), [o], [], c)
 
-    def dma(q, o, i):
+    def select(o, pat):
+        add("g", lambda: g.affine_select(o[0], o[0], pat, A.is_equal, 0.0, 0, 1), [o], [o], 170.0 + 2 * CYC * o[3])
+
+    def dma(q, o, i, wait=()):
         e = {"s": g.sync, "a": g.scalar, "g": g}[q]
         sem = "d%d" % ndma[0]
         ndma[0] += 1
         sb = o if isinstance(o, tuple) else i
-        add(q, lambda: e.dma_start(a0(o), a0(i)), [o] if isinstance(o, tuple) else [], [i], 100.0, kind="d", sem=sem,
-            lat=2000.0 + 128 * sb[3] * sb[4] / 150.0)
+        return add(q, lambda: e.dma_start(a0(o), a0(i)), [o] if isinstance(o, tuple) else [], [i], 100.0, kind="d", sem=sem,
+                   lat=DL + 128 * sb[3] * sb[4] / DB, wait=wait)
 
     def engines_to(dst):
         es = topo.engines(core, dst)
@@ -287,216 +305,216 @@ def rank_program(g, core, T, topo):
         me = add("g", lambda: g.remote_dma(dst[0], src[0], T.sem[sem], T.sem.sent, pid, rid, m), [], [src], 300.0, kind="r", lat=FAR)
         add("x", None, [dst], [], 0.0, kind="x", sem=sem, after=[me])
 
-    def Sr(r, name="Wd"):
-        return R(name, 16 - r, 144 - r)
+    def Sr(r):
+        return R("Wd", 16 - r, 144 - r)
 
-    def Rr(r):
-        return R("RR", 128 * r, 128 * r + 128)
+    def every(a, b, step=None):
+        return slice(a, b, step)
 
-    def toN(o, src, last, rot=0, at=0):
-        for r in range(16):
-            mm(o, Sr((r + rot) % 16), R(src, at + 12 * r, at + 12 * r + 12), False, last and r == 15)
-
-    def toA(o, src, last):
-        for r in range(16):
-            mm(o, Sr(r), R(src, r, None, 16), False, last and r == 15)
-
-    def toLanes(ob, src, at=0, js=range(12)):
-        for j in js:
-            mm(R(ob, 16 * j, 16 * j + 16), R("BO"), R(src, at + j, at + L, 12), True, True)
-
-    PC, PK, PR0, PPI, PNI, P32, PX, PB = [R("pc", i, i + 1) for i in range(8)]
-    PV1, PC1 = R("pr1", 0, L), R("pr1", L, 2 * L)
+    ALL = slice(None)
+    PC, PK, PR0, PPI, PNI, P64, PG, PX1, PLT, PU, PB16, PS16, PB17, PG0, PW = [R("pc", i, i + 1) for i in range(15)]
+    SJ = R("Sel", 0, L, p1=12)
+    PV1, PC1 = M("pr1", every(0, NS)), M("pr1", every(NS, 2 * NS))
 
     ms(R("li"), 0)
     dma("s", R("li", 0, L, ps=16), T.lc[:])
     dma("a", R("li", L, 2 * L, ps=16), T.lv[:])
     dma("s", R("li", 2 * L, 3 * L, ps=16), T.ld[:])
-    dma("s", R("Bi"), T.bnd[:])
-    dma("a", R("xin", 0, S // 2), T.x[:, 0:S // 2])
-    dma("a", R("xin", S // 2, S), T.x[:, S // 2:S])
-    dma("s", R("k1"), T.kt[:])
+    big = [dma("a", R("xin", 0, S // 2), T.x[:, 0:S // 2]), dma("s", R("xin", S // 2, S), T.x[:, S // 2:S]), dma("s", R("Bi"), T.bnd[:])]
+    dma("s", R("K", 0, KW), T.kt[:], wait=big[:2])
     iota(R("pi", 0, 1), [[0, 1]], 0, 1)
+    iota(R("pi", 8, 8 + ST), [[-5, ST]], 48, 1)
     iota(R("it4"), [[1, 144]], -16, -1)
     iota(R("it5"), [[16, 8], [0, 16]], 0, -1)
     iota(R("it6"), [[1, 128]], 0, -1)
     iota(R("it7"), [[1, 16]], 0, 0)
+    iota(R("it8", 0, 12), [[0, NS], [16, MB]], NV, 0)
     iota(R("it2"), [[0, 13], [1, 16]], 0, 0)
     iota(R("it"), [[1, 64], [0, 16]], 0, 0)
-    iota(R("TT", 2048, 4096), [[0, 2048]], 0, 0)
     ts(R("pj", 0, 1), R("pi", 0, 1), 15, A.bitwise_and)
-    ts(R("pj", 1, 2), R("pi", 0, 1), 5, A.arith_shift_right)
+    ts(R("pj", 1, 2), R("pi", 0, 1), 63, A.bitwise_and)
     ts(R("pj", 2, 3), R("pi", 0, 1), 1, A.bitwise_and)
+    ts(R("pj", 8, 8 + ST), R("pi", 8, 8 + ST), 15, A.bitwise_and)
     cp(PC, R("pj", 0, 1))
+    cp(P64, R("pj", 1, 2))
     cp(PPI, R("pj", 2, 3))
-    ts(PK, PC, -1.0, A.mult, 15.0, A.add)
+    act(PG, R("pi", 0, 1), bias=-12.0)
+    act(R("pt", 0, ST), R("pj", 8, 8 + ST))
+    act(PK, PC, scale=-1.0, bias=15.0)
     ts(PR0, PC, 0.0, A.is_equal)
-    ts(PNI, PPI, -2.0, A.mult, 1.0, A.add)
-    ts(P32, R("pj", 1, 2), 16.0, A.mult, PC, A.add)
-    cp(R("cJ"), R("it7", 0, 12))
-    ts(R("nid"), R("it7", 0, 12), 16.0, A.mult, PC, A.add)
-    ts(R("nq"), R("nid"), -5.5, A.add, 1.0 / 12, A.mult)
-    ts(R("nf"), R("nq"), -191.0 / 16, A.mult)
-    tt(R("nf"), R("nf"), R("nid"), A.add)
-    ts(R("perm"), R("nf"), 16.0, A.mult)
-    ts(R("nid16", 0, 12), R("nid"), float(L), A.add)
-    ts(PX, PC, float(S), A.add)
-    ts(PB, PC, float(NV), A.add)
+    act(PNI, PPI, scale=-2.0, bias=1.0)
+    act(PX1, PC, bias=PNI)
+    ts(PLT, PG, 16.0, A.is_lt)
+    ts(PW, PG, 0.0, A.is_ge, PLT, A.mult)
+    ts(PU, PG, PW, A.mult)
+    ts(PU, PG, 16.0, A.is_ge, PU, A.add)
+    ts(PB16, PG, 16.0, A.is_equal, float(NV), A.mult)
+    act(PS16, PB16, scale=0.75)
+    ts(PB17, PG, 17.0, A.is_equal, PB16, A.add)
+    act(R("cJ"), R("it7", 0, 12))
+    ts(R("nid16", 0, 12), R("it7", 0, 12), 16.0, A.mult, PC, A.add)
     ts(R("Wd"), R("it4"), PC, A.add, 0.0, A.is_equal)
-    ts(R("Wd10"), R("Wd"), 2.0 ** -10, A.mult)
     ts(R("BO"), R("it5"), PC, A.add, 0.0, A.is_equal)
     ts(R("Ib"), R("it6"), 0.0, A.is_equal)
-    ms(R("cst"), 1536.0)
+    ts(R("Sw"), R("it6"), PNI, A.is_equal)
     ms(R("cst", 0, 12), 0.0)
-    ms(R("cst", 24, 48), 0.0)
+    ms(R("cst", 12, 24), 1536.0)
     ts(R("DG"), R("it2"), PC, A.is_equal)
     ts(R("NDG"), R("it2"), PC, A.not_equal)
-    ts(R("sc1"), R("it2", 0, L), 0.0, A.not_equal, 65536.0 + 1.0 / 32, A.mult)
-    ts(R("sc1"), R("sc1"), -65536.0, A.add)
-    ts(R("Sel"), R("it"), P32, A.is_equal)
+    ts(R("DK"), R("it7"), PK, A.is_equal)
+    ts(R("DP"), R("it2", 1, 49), PX1, A.is_equal)
+    ts(R("sc1"), R("it2", 0, L), 0.0, A.not_equal, 2.0 ** 24, A.mult)
+    ts(R("sc1"), R("sc1"), 32.0 - 2.0 ** 24, A.add)
+    ts(R("Sel"), R("it"), P64, A.is_equal)
     ms(R("th"), 1.0 / 32)
-    for w in ("sw2", "swo", "swp", "pl"):
-        ms(R(w, 12, 16), 0.0)
-    for r in range(16):
-        ts(Rr(r), R("BO"), R("DG", r, r + 1), A.mult)
-        act(R("EE", 128 * r, 128 * r + 128), R("Ib"), scale=R("DG", r, r + 1))
-    act(R("DGc"), R("DG"), scale=1536.0)
-    act(R("I9"), R("Ib"), scale=2.0 ** -9)
-    act(R("I192"), R("Ib"), scale=-float(L))
-    act(R("If"), R("Ib"))
-    act(R("I10"), R("Ib"), scale=2.0 ** -10)
-    act(R("Ih"), R("Ib"), scale=0.5)
-    act(R("In"), R("Ib"), scale=-1.0)
+    iota(R("RR"), [[0, 2048]], 1, 0)
+    select(R("RR"), [[-1, 16], [-16, 8], [0, 16]])
+    act(R("NDm"), R("NDG"), scale=-4096.0)
+    for nm, k in (("I192", -float(L)), ("Ih", 0.5), ("In", -1.0), ("I8", 8192.0), ("I2", 2.0), ("I2n", -2.0), ("I9", 2.0 ** -9),
+                  ("I16", -16.0), ("Ie", 0.0625)):
+        act(R(nm), R("Ib"), scale=k)
     act(R("BOf"), R("BO"))
-    ms(R("sc3"), 0.0)
-    ms(R("row"), 0.0)
-    for k in "2op":
-        ms(R("eq" + k), 4096.0)
+    act(R("BO8"), R("BO"), scale=8192.0)
+    for t in range(ST):
+        s = (5 * t) % 16
+        ts(R("aT2", 128 * t, 128 * t + 128), R("it2", 16 - s, 144 - s), PG, A.is_equal, PB16, A.add)
+    ts(R("aTo"), R("it2", 0, 128), PG, A.is_equal, PB17, A.add)
+    ts(R("aTp"), R("it2", 0, 128), PG, A.is_equal, PS16, A.add)
+    act(PG0, PW, scale=4096.0)
+    act(R("n8", 0, 12), R("Ib", 0, 12), scale=-8192.0)
+    ms(R("MK"), 0.0)
     for a in range(MB):
         e = SEG[a + 1] - 1
-        act(R("sc3", SEG[a], SEG[a] + 1), PC, scale=0.0, bias=8192.0)
-        act(R("sc3", e, e + 1), PC, scale=0.0, bias=8192.0 - 16 * a)
-        act(R("sc3", e - 16, e), R("DG", 0, 16), scale=-8192.0)
-        act(R("row", a, 12, MB), R("it7", 0, NS), scale=float(SL), bias=float(e))
+        ts(R("MK", e - 15, e), R("it7", 0, 15), PG, A.is_ge, PG0, A.mult)
+        ts(R("MK", e, e + 1), PW, 16.0 * a, A.mult, PU, A.add)
+        for s in range(NS):
+            act(R("AJ", SL * s + SEG[a], SL * s + e), R("it2", 0, e - SEG[a]), scale=0.0, bias=R("n8", MB * s + a, MB * s + a + 1))
+        act(R("AJ", e, None, SL), R("Ib", a, 12, MB), scale=-1.0)
     for s in range(NS):
-        cp(R("sc2", SL * s, SL * s + SL), R("sc3"))
-    tt(R("rowd"), R("row"), R("DG", 0, 16), A.mult)
-    red(R("col", 1, 2), R("rowd"))
-    cp(R("cOff", 0, 1), R("col", 1, 2))
-    cp(R("B", 0, NV // 2), R("Bi", 0, NV // 2))
+        tt(R("MJ", SL * s, SL * s + SL), R("AJ", SL * s, SL * s + SL), R("MK"), A.add)
+    for t in range(ST):
+        act(R("SP", 12 * t, 12 * t + 12), R("it8", 0, 12), bias=R("pt", t, t + 1))
+    act(R("SP", 12 * ST, 12 * ST + 12), R("SP", 0, 12), bias=float(S - NV))
+    act(R("B", 0, NV // 2), R("Bi", 0, NV // 2))
     cp(R("B", NV // 2, NV), R("Bi", NV // 2, NV))
     ms(R("B", NV, BS), 0.0)
-    ts(R("ka"), R("k1"), 1023, A.bitwise_and)
-    ts(R("TT", 0, 512), R("ka"), 2.0, A.mult, PPI, A.add)
-    act(R("TT", 4096, 4608), R("TT", 0, 512), bias=PNI)
-    ts(R("TT", 1024, 1536), R("k1"), -1536.0, A.add)
-    act(R("TT", 512, 1024), R("TT", 0, 512))
-    for nm, o, k in (("TW", 0, 0), ("TW", 4096, 4096), ("TT", 1024, 1536)):
-        dma("s", R(nm, k, k + 512, ps=2), R("TT", o, o + 512, p0=1, ps=2))
-        dma("s", R(nm, k, k + 512, p0=1, ps=2), R("TT", o, o + 512, ps=2))
-    for o in (0, 4096):
-        for k in range(1, 6):
-            dma("s", R("TW", o + 512 * k, o + 512 * k + 512), R("TW", o, o + 512))
-    iota(R("TW", S, 4096), [[0, 4096 - S]], 0, 0)
+    ts(R("ka"), R("K", 0, KW), 1023, A.bitwise_and)
+    ts(R("TT", 0, KW), R("ka"), 2.0, A.mult, PPI, A.add)
+    act(R("TT", S, S + KW), R("TT", 0, KW), bias=PNI)
+    for k in range(1, S // KW):
+        dma("s", R("K", KW * k, KW * k + KW), T.kt[:], wait=big)
+    for o in (0, S):
+        for k in range(1, S // KW):
+            dma("s", R("TT", o + KW * k, o + KW * k + KW), R("TT", o, o + KW), wait=big)
+    dma("s", R("TT", 2 * S, 3 * S), R("TT", 0, S))
     ts(R("X", 0, 1536), R("xin", 0, 1536), -127.5, A.add)
     ts(R("X", 1536, S), R("xin", 1536, S), -127.5, A.add)
     ms(R("X", S, XS), 0.0)
-    ms(R("X", XS, XS + 1), -0.0625)
-    ms(R("X", XS + 1, XS + 16), 0.0625)
-    ts(R("lcol"), R("li", L, 2 * L), 2.0, A.mult)
-    tt(R("lcol"), R("lcol"), R("li", 2 * L, 3 * L), A.add)
-    ts(PC1, G(R("li", 0, L), R("perm")), -1536.0, A.add, PR0, A.mult)
-    ts(PV1, G(R("lcol"), R("perm")), PR0, A.mult)
+    iota(R("X", XS, XS + 512), [[0, 256], [-2, 2]], 1, 0)
+    for k in range(1, NV // 512):
+        dma("s", R("X", XS + 512 * k, XS + 512 * k + 512), R("X", XS, XS + 512))
+    act(R("lcol"), R("li", L, 2 * L), scale=2.0, bias=PR0)
+    tt(PV1, R("lcol"), R("li", 2 * L, 3 * L), A.subtract)
+    ts(PC1, R("li", 0, L), -1536.0, A.add, PR0, A.mult)
+    act(R("ld0"), R("li", 2 * L, 3 * L))
+    for r in range(16):
+        mm(R("Q2", 0, 12), Sr(r), R("ld0", r, L, 16), r == 0, r == 15)
+    act(R("D0"), R("Q2", 0, 12))
 
     def lanes(t):
         s = (5 * t) % 16
-        mm(R("Q0", 0, 48), R("Ib"), R("cst", 12, 60), True, False)
-        toA(R("Q0", 24, 48), "pr1", False)
-        toN(R("Q0", 12, 24), "pr1", False)
-        toN(R("Q0", 0, 12), "pr1", True, at=L)
-        toLanes("Q1", "pr1")
-        mm(R("Q2", 0, L), R("Ib"), R("DGc", s, s + L), True, False)
+        D = "D%d" % (t % 2)
+        for a in range(16):
+            at = 16 * (a % 4) + a // 4
+            mm(R("Q0", 0, 24), Sr(a), M("pr1", ALL, every(at, at + 13, 4)), a == 0, a == 15)
+        plus("ou", R("ou"), R("Q0", 0, 12))
+        act(R("QO", 0, 12), R("Q0", 12, 24), bias=1536.0)
+        act(R("QO", 12, 24), R("Q0", 0, 12), bias=float(XS))
         for r in range(16):
-            mm(R("Q2", r, L, 16), Sr((r + s) % 16), R("pr1", L + 12 * r, L + 12 * r + 12), False, r == 15)
-        cp(R("I"), R("Q0", 0, 48))
-        act(R("cN"), R("Q0", 0, 12))
-        rivals("o", ("Q0", 12), [("Q1", "a")] * NS, R("oo"), PB)
-        act(R("t4"), R("Q2", 0, L))
-        ts(R("D"), R("I", 12, 36), 1, A.bitwise_and)
-        cp(R("nu"), R("I", 0, 24))
-        cp(R("QO", 0, 24, 2), R("I", 36, 48))
-        ts(R("QO", 1, 24, 2), R("D", 12, 24), float(XS), A.add)
-        ts(R("sg", 0, 24), R("D"), -2.0, A.mult, 1.0, A.add)
-        ts(R("cm"), R("I", 36, 48), KW - 1, A.bitwise_and)
-        act(R("d4", 0, 12), R("sg", 12, 24), scale=-2048.0, bias=3584.0)
-        tt(R("oq"), R("I", 24, 36), R("sg", 12, 24), A.add)
-        cp(R("cu"), R("cm"))
-        cp(R("ou"), R("oq"))
-        act(R("sb", 0, 12), R("sg", 0, 12), scale=-1.0)
-        act(R("SX"), G(R("sg", 0, 12), R("cJ")), scale=2.0 ** -7)
+            mm(R("Q1", 0, 24), Sr(r), M("pr1", ALL, every(r, 64, 16)), r == 0, r == 15)
+        act(R("oN"), R("Q1", 0, 12))
+        act(R("cu"), R("Q1", 12, 24), bias=1536.0)
+        act(R("cc"), R("Q1", 12, 24))
+        act(R("Sd"), R(D), scale=float(S), bias=1536.0)
         act(R("QS"), G(R("X"), R("QO")))
-        act(R("qN"), G(R("X"), R("nu", 0, 12)))
-        for b in range(3):
-            mm(R("MA", 128 * b, 128 * b + 128), R("QS", 128 * b, 128 * b + 128), R("Ib"), True, True)
-        mm(R("MB", 0, 12), R("Ib"), R("sb", 0, 12), True, False)
+        for b in range(2):
+            mm(R("MA", 128 * b, 128 * b + 128), R("QS", 64 * b, 64 * b + 128), R("Ib"), True, False)
+            mm(R("MA", 128 * b, 128 * b + 128), R("QS", L + 64 * b, L + 64 * b + 128), R("Ie"), False, True)
+        act(R("QT"), R("MA", 0, 256))
+        act(R("qN"), G(R("X", 0, XS), R("cu")))
+        mm(R("MB", 256, 384, p1=12), R(D), R("I2"), True, False)
         for r in range(16):
-            mm(R("MB", 0, 12), Sr(r), R("qN", r, L, 16), False, r == 15)
-        act(R("QT"), R("MA", 0, 384))
-        act(R("LN", 0, 12), R("MB", 0, 12), scale=-1.0)
-        act(R("LX"), G(R("LN", 0, 12), R("cJ")))
-        for c in range(4):
+            mm(R("MB", 256 + r, 384, 16, p1=12), R("qN", r, L, 16), R("BO", 0, 128, 16), False, r == 15)
+        act(R("LT", p1=12), R("MB", 256, 384, p1=12), scale=-1.0, bias=1.0)
+        act(R("SX"), G(R(D), R("cJ")), scale=-2.0 ** -17, bias=2.0 ** -18)
+        for c in range(3):
             spread(c)
-        mm(R("P1", 0, L), R("If"), R("LX"), True, False)
-        mm(R("P2", 0, L), R("I10"), R("LX"), True, False)
+        mm(R("P1", 0, L), R("LT", p1=12), SJ, True, False)
+        mm(R("P2", 0, L), R("LT", p1=12), SJ, True, False)
         act(R("f4"), R("qN"), scale=0.25, bias=31.5 + 192.0)
+        act(R("kc"), G(R("K"), R("cu")), bias=-1536.0)
+        rivals("o", "pr1", "BO8", 0, 0, R("SP", 0, 12), R("oo", 0, 12), "MB", D)
+        for r in range(16):
+            mm(R("MB", 128 + (r + s) % 16, 256, 16, p1=12), M("pr1", every(NS, 2 * NS), every(r, 64, 16)), R("BO", 0, 128, 16), True, True)
+        plus("cT", R("cT", p1=12), R("MB", 128, 256, p1=12))
+        mm(R("MB", 0, L), R("Ib"), R("NDm", s, s + L), True, False)
+        mm(R("MB", 0, L), R("cT", p1=12), SJ, False, True)
+        act(R("t4"), R("MB", 0, L), AF.Relu, bias=1536.0)
+        mm(R("MA", 0, L), R("Ib"), R("kc"), True, True)
+        mm(R("MA", L, 2 * L), R("Sw"), R("kc"), True, True)
 
     def spread(c):
-        b, h = divmod(c, 2)
-        mm(R("Q%d" % (c % 4)), R("QT", 128 * b, 128 * b + 128), R("Sel", 512 * h, 512 * h + 512), True, True)
+        b, p = (0, 0) if c < 2 else ((0, 64) if c < 4 else (1, 64))
+        mm(R("Q%d" % (c % 3)), R("QT", 128 * b, 128 * b + 128, p0=p, p1=p + 64), R("Sel", 512 * (c % 2), 512 * (c % 2) + 512, p0=p, p1=p + 64),
+           True, True)
 
-    def rivals(k, w, bk, off, spare, shift=0.0):
-        wt = R(w[0], w[1], w[1] + 12)
-        if any(e == "v" for _, e in bk):
-            ts(R("nw" + k, 0, 12), wt, -4096.0, A.mult)
-            act(R("sw" + k, 0, 12), R("nw" + k, 0, 12), scale=2.0 ** -12, bias=spare)
+    def rivals(k, src, lw, s, at, spare, off, bk, side=None):
+        rv = M("RV", ALL, every(0, SL))
+        if k == "p":
+            mm(R(bk, 0, 128, p1=12), R("p16", 0, 12), R("Ib"), True, True)
         else:
-            act(R("nw" + k, 0, 12), wt, scale=-4096.0, bias=4096.0 * shift)
-            act(R("sw" + k, 0, 12), wt, scale=-1.0, bias=spare)
-        for j in range(12):
-            s, a = divmod(j, MB)
-            o = R("eq" + k, SL * s + SEG[a] + 1, SL * s + SEG[a + 1] - 1)
-            i = R(bk[s][0], 16 * MB * s, 16 * j + 16)
-            if bk[s][1] == "a":
-                act(o, i, AF.Abs, scale=4096.0, bias=R("nw" + k, j, j + 1))
+            for r in range(16):
+                row = R(src, r, L, 16) if k == "2" else M(src, every(0, NS), every(r, 64, 16))
+                mm(R(bk, (r + s) % 16, 128, 16, p1=12), row, R("BO", 0, 128, 16), True, True)
+        plus("aT" + k, R("aT" + k, at, at + 128, p1=12), R(bk, 0, 128, p1=12))
+        for a in range(MB):
+            if k == "2":
+                for c in range(NS):
+                    mm(M("RV", c, every(SEG[a], SEG[a + 1] - 1)), R(lw), R(src, 64 * c, 64 * c + 16 * a + 15), a + c == 0, False)
             else:
-                ts(o, i, R(w[0], w[1] + j, w[1] + j + 1), A.not_equal, 4096.0, A.mult)
-        scan(R("ds" + k), R("sc2"), R("eq" + k), 0.0, A.add, A.min)
-        tt(R("of" + k), G(R("ds" + k), R("cOff", 0, 1)), R("sw" + k), A.min)
-        ts(off, R("of" + k), -1.0, A.mult, spare, A.add)
+                mm(M("RV", ALL, every(SEG[a], SEG[a + 1] - 1)), R(lw), M(src, every(0, NS), every(0, 16 * a + 15)), a == 0, False)
+            mm(M("RV", ALL, SEG[a + 1] - 1), R("I2n"), R(side or "cst", a, 12, MB), False, False)
+        mm(rv, R("aT" + k, at, at + 128, p1=30), R("MJ", p1=30), False, True)
+        for a in range(MB - 1, -1, -1):
+            least(R("ds" + k, a, 12, MB), M("RV", ALL, every(SEG[a], SEG[a + 1])))
+        tt(off, spare, R("ds" + k, 0, 12), A.subtract)
 
-    def append(cols, t, name, base, t1, t2):
-        s = (5 * t) % 16
+    def append(cols, s, name, base, t1, t2):
         tt(R(t1), G(R("B"), cols), R("NDG", s, s + L), A.mult)
         for j in range(NS - 1, -1, -1):
             a, b = 16 * MB * j, 16 * MB * (j + 1)
-            tt(G(R("B"), R(name, base + PS * j, base + PS * j + MB)), R(t1, a, b), R(t2, a, b), A.add)
+            tt(G(R("B"), R(name, base + MB * j, base + MB * j + MB)), R(t1, a, b), R(t2, a, b), A.add)
 
     lanes(0)
     for t in range(ST):
         last = t == ST - 1
         to = T.cores[(rank + 1 + t % (N - 1)) % N]
-        cp(R("E"), G(R("Bi") if t == 0 else R("B"), R("ou")))
+        s = (5 * t) % 16
+        D, Dn = "D%d" % (t % 2), "D%d" % (1 - t % 2)
+        Bt = R("Bi") if t == 0 else R("B")
+        act(R("E", 0, ESPLIT), G(Bt, R("ou", 0, ESPLIT // 16)))
+        cp(R("E", ESPLIT, L), G(Bt, R("ou", ESPLIT // 16, 12)))
         done, prev = [0, 0], []
 
-        def sums(c, which):
-            src, wt, o = (("xe", "Wd10", "P2"), ("H", "Wd", "P1"))[which]
-            while 192 * (done[which] + 1) <= c:
-                r = done[which]
-                mm(R(o, 0, L), Sr(r, wt), R(src, 192 * r, 192 * r + 192), False, r == 15)
+        def sums(n, which):
+            src, o = (("xe", "P2"), ("H", "P1"))[which]
+            while 4 * (done[which] + 1) <= n:
+                c, r = divmod(done[which], 16)
+                mm(R(o, 64 * c, 64 * c + 64), Sr(r), R(src, 64 * done[which], 64 * done[which] + 64), False, (which, c, r) == (0, 2, 15))
                 done[which] += 1
 
         for lo, hi, e in PIECES:
-            o, i = R("xe", lo, hi), G(R("X"), R("E", lo // 16, hi // 16))
+            o, i = R("xe", 16 * lo, 16 * hi), G(R("X", 0, XS), R("E", lo, hi))
             if e == "v":
                 cp(o, i)
             else:
@@ -505,118 +523,105 @@ def rank_program(g, core, T, topo):
                     ops[-1]["order"].add(prev[-1])
                 prev.append(len(ops) - 1)
             sums(hi, 0)
-        ts(R("Ec"), R("E"), -1536.0, A.add)
-        append(R("nu", 12, 24), t, "oo", 0, "t3", "t4")
-        for c in range(6):
-            for lo, hi in ([(0, 512)] if c < 5 else [(0, 320), (320, 512)]):
-                tt(R("H", 512 * c + lo, 512 * c + hi), R("xe", 512 * c + lo, 512 * c + hi), R("Q%d" % (c % 4), lo, hi), A.min)
-                sums(512 * c + hi, 1)
-            if c + 4 < 6:
-                spread(c + 4)
-        act(R("a1"), R("P2", 0, L), bias=196608.0)
-        act(R("Y"), R("P2", 0, L), scale=512.0, bias=4096.0)
-        act(R("a2"), R("a1"), scale=-1.0, bias=196600.0)
-        mm(R("MB", 0, L), R("I9"), R("Y"), True, False)
-        mm(R("MB", 0, L), R("If"), R("a2"), False, True)
+        act(R("Ec"), G(Bt, R("oN")), bias=-1536.0)
+        append(R("oo", 0, 12), s, "oo", 0, "t3", "t4")
         tt(R("tt"), R("SX"), R("P2", 0, L), A.mult)
-        ts(R("R1"), R("P1", 0, L), R("th", 0, 1), A.add)
-        tt(R("P1", 256, 256 + L), R("R1"), R("P1", 0, L), A.subtract)
-        tt(R("R2"), R("R1"), R("MB", 0, L), A.add)
-        tt(R("P1", 256, 256 + L), R("P1", 256, 256 + L), R("tt"), A.is_gt)
+        act(R("Y"), R("P2", 0, L), scale=512.0, bias=512.0 * 8192)
+        act(R("h16"), R("P2", 0, L), scale=1.0 / 16, bias=1536.0)
+        for a, b in zip(MINS, MINS[1:]):
+            c = a // 32
+            tt(R("H", 16 * a, 16 * b), R("xe", 16 * a, 16 * b), R("Q%d" % (c % 3), 16 * (a - 32 * c), 16 * (b - 32 * c)), A.min)
+            sums(b, 1)
+            if b % 32 == 0 and c + 3 < 6:
+                spread(c + 3)
+        mm(R("P1", 0, L), R("Ib"), R("tt"), False, True)
+        mm(R("Q1", 0, L), R("I9"), R("Y"), True, False)
+        mm(R("Q1", 0, L), R("I16"), R("h16"), False, True)
+        plus("R1", R("R1"), R("P1", 0, L), R("th", 0, 1))
+        act(R("R1k"), R("R1"), scale=1024.0, bias=C0 + 16 * 1536.0 - 8192 + 14)
+        tt(R("P1", 256, 256 + L), R("R1"), R("P1", 0, L), A.is_gt)
+        tt(R("R2"), R("R1k"), R("Q1", 0, L), A.add)
         tt(R("P1", 256, 256 + L), R("P1", 256, 256 + L), R("Y"), A.mult)
         tt(R("key"), R("R2"), R("P1", 256, 256 + L), A.subtract)
         scan(R("scn"), R("sc1"), R("key"), 0.0, A.add, A.max)
         best = R("scn", 15, L, 16)
-        ts(R("Z"), best, 1024.0, A.mult, float(2 ** 23 - 512 + 14), A.add)
-        ts(R("hit"), best, -4090.0, A.is_gt)
-        ts(R("kk"), R("Z"), 5, A.arith_shift_right, 15, A.bitwise_and)
-        ts(R("lo"), R("Z"), 31, A.bitwise_and)
-        cp(R("kb", 0, 12), R("kk"))
-        for r in range(16):
-            mm(R("MA", 12 * r, 12 * r + 12), Rr(r), R("kb", 0, 12), True, True)
-        ts(R("z2"), R("Z"), 9, A.arith_shift_right)
+        ts(R("kk"), best, 5, A.arith_shift_right, 15, A.bitwise_and)
+        plus("ku", R("ku"), R("kk"))
+        tt(R("prE"), G(R("DK"), R("ku")), R("Ec"), A.mult)
+        ts(R("hit"), best, 512.0 * 4100, A.is_gt)
+        ts(R("lo"), best, 31, A.bitwise_and)
+        ts(R("z2"), best, 9, A.arith_shift_right, 15, A.bitwise_and)
         tt(R("pb"), R("lo"), R("hit"), A.mult)
         tt(R("pd"), R("pb"), R("z2"), A.subtract)
-        ts(R("pe"), R("pd"), 15, A.bitwise_and)
-        cp(R("pf", 0, 12), R("pe"))
-        for r in range(16):
-            mm(R("MB", 12 * r, 12 * r + 12), Rr(r), R("pf", 0, 12), True, True)
+        plus("pu", R("pu"), R("pd"), 16.0)
+        act(R("mp"), G(R("DP"), R("pu")))
         act(R("ms"), R("hit"), scale=-1.0, bias=1.0, acc=R("mc", 0, 1))
-        ts(R("MA", 0, L), R("MA", 0, L), PK, A.is_equal)
-        tt(R("prE"), R("Ec"), R("MA", 0, L), A.mult)
-        mm(R("Q0", 0, 12), R("Ib"), R("d4", 0, 12), True, False)
-        toA(R("Q0", 0, 12), "prE", True)
-        mm(R("Q1", 0, 12), R("Ib"), R("cst", 12, 24), True, False)
-        toN(R("Q1", 0, 12), "prE", True)
-        mm(R("P2", 0, 1), R("BOf"), R("mc", 0, 1), True, True)
-        mm(R("P1", 0, 12), R("Ib"), R("nid16", 0, 12), True, False)
-        mm(R("P1", 0, 12), R("I192"), R("hit"), False, True)
-        cp(R("su"), R("P1", 0, 12))
-        ts(R("mp"), R("MB", 0, L), PC, A.is_equal)
-        tt(R("pc2"), G(R("TT", 1536, 2048), R("cu")), R("mp"), A.mult)
-        cp(R("ew"), R("Q0", 0, 12))
-        cp(R("ei"), R("Q0", 0, 12))
-        ts(R("ej"), R("ei"), 4096 + KW - 1, A.bitwise_and)
-        cp(R("eo"), R("ej"))
-        tt(R("pv2"), G(R("TW"), R("ew")), R("mp"), A.mult)
-        mm(R("Q2", 0, 24), R("Ib"), R("cst", 0, 24), True, False)
-        toN(R("Q2", 12, 24), "pc2", False, rot=5 * t)
-        toN(R("Q2", 0, 12), "pv2", True)
-        for s in range(NS):
-            toLanes(SENT[s][0], "pv2", js=range(MB * s, MB * s + MB))
-        cp(R("eN"), R("Q1", 0, 12))
-        tt(R("pm"), R("Q1", 0, 12), R("cN"), A.subtract)
-        act(R("yN"), G(R("X"), R("eN")))
-        act(R("ymt", t, t + 1), R("P2", 0, 1))
-        tt(PV1, G(R("TT", 0, 4608), R("eo")), R("mp"), A.mult)
-        tt(R("pn"), R("pm"), R("hit"), A.mult)
-        tt(R("pl", 0, 12), R("pn"), R("cN"), A.add)
-        cp(R("m1", 24 * t, 24 * t + 24), R("Q2", 0, 24))
+        for r in range(16):
+            mm(R("Q0", 0, 12), Sr(r), R("prE", r, L, 16), r == 0, r == 15)
+        tt(R("ew"), R("Q0", 0, 12), R("Sd"), A.add)
+        tt(R("pr2", L, 2 * L), R("mp"), R("MA", 0, L), A.mult)
+        tt(R("pr2", 0, L), G(R("TT", 0, 2 * S), R("ew")), R("mp"), A.mult)
+        rivals("2", "pr2", "BO8", s, 128 * t, R("SP", 12 * t, 12 * t + 12), R("m2", 16 * t, 16 * t + 12), "Q2")
+        mm(R("Q1", 0, 24), R("Ib"), R("cst"), True, False)
+        for r in range(16):
+            mm(R("Q1", 0, 24), Sr((r + s) % 16), R("pr2", r, 2 * L, 16), False, r == 15)
+        plus("m1", R("m1", 24 * t, 24 * t + 24), R("Q1", 0, 24))
         send(R("m1", 24 * t, 24 * t + 24), R("r1", 24 * t, 24 * t + 24), "ra%d" % t, to)
-        rivals("2", ("Q2", 0), SENT, R("m2", 16 * t, 16 * t + 16), PB)
-        send(R("m2", 16 * t, 16 * t + 16), R("r2", 16 * t, 16 * t + 16), "rb%d" % t, to)
-        s = (5 * t) % 16
-        ts(R("V", 0, 12), R("r1", 24 * t + 12, 24 * t + 24), -1536.0, A.add)
-        mm(R("P2", 0, L), R("Ib"), R("DGc", s, s + L), True, False)
+        send(R("m2", 16 * t, 16 * t + 12), R("r2", 16 * t, 16 * t + 12), "rb%d" % t, to)
+        act(R("eN"), R("Q0", 0, 12), bias=1536.0)
+        tt(R("pm"), R("Q0", 0, 12), R("cc"), A.subtract)
+        act(R("yN"), G(R("X", 0, XS), R("eN")))
+        act(R("ke"), G(R("TT", S, 3 * S), R("ew")))
+        tt(R("pn"), R("pm"), R("hit"), A.mult)
+        tt(R("p16", 0, 12), R("pn"), R("cc"), A.add)
+        mm(R("MB", 0, L), R("Sw"), R("ke"), True, True)
+        tt(PV1, R("mp"), R("MB", 0, L), A.mult)
+        tt(PC1, R("mp"), R("MA", L, 2 * L), A.mult)
+        if not last:
+            ts(R("pe"), R("pd"), 1, A.bitwise_and)
+            tt(R(Dn), R(D), R("pe"), A.is_equal)
+        mm(R("Q1", 32, 33), R("BOf"), R("mc", 0, 1), True, True)
+        mm(R("Q1", 48, 60), R("Ib"), R("nid16", 0, 12), True, False)
+        mm(R("Q1", 48, 60), R("I192"), R("hit"), False, True)
+        act(R("su"), R("Q1", 48, 60), bias=float(L))
+        act(R("ymt", t, t + 1), R("Q1", 32, 33))
+        mm(R("P1", 0, L), R("Ib"), R("yN"), True, False)
+        mm(R("P1", 0, L), R("In"), R("f4"), False, True)
+        mm(R("P1", L, 2 * L), R("Ih"), R("yN"), True, False)
+        mm(R("P1", L, 2 * L), R("Ih"), R("qN"), False, True)
         for r in range(16):
-            e = (r + s) % 16
-            mm(R("P2", r, L, 16), R("EE", 128 * e, 128 * e + 128), R("V", 0, 12), False, r == 15)
-        act(R("t2"), R("P2", 0, L))
-        mm(R("MA", 0, L), R("Ib"), R("yN"), True, False)
-        mm(R("MA", 0, L), R("In"), R("f4"), False, True)
-        mm(R("MA", L, 2 * L), R("Ih"), R("yN"), True, False)
-        mm(R("MA", L, 2 * L), R("Ih"), R("qN"), False, True)
-        ts(R("p16", 0, 12), R("pl", 0, 12), -1536.0, A.add)
-        tt(PC1, G(R("TT", 1024, 1536), R("cu")), R("mp"), A.mult)
-        for r in range(16):
-            mm(R("MB", r, L, 16), Rr(r), R("p16", 0, 12), True, True)
-        act(R("zr"), R("MA", L, 2 * L), bias=127.25)
-        act(R("vals", 0, L), R("MA", 0, L), AF.Abs, bias=127.5 + 192.0)
-        act(R("zs"), R("zr"), bias=1.5 * 2 ** 23)
-        act(R("vals", L, 2 * L), R("zs"), bias=-1.5 * 2 ** 23)
+            mm(R("P2", r, L, 16), R("RR", 128 * r, 128 * r + 128), R("p16", 0, 12), True, True)
+        act(M("Lp", ALL), R("P2", 0, L))
+        act(R("vals", 0, L), R("P1", 0, L), AF.Abs, bias=127.5 + 192.0)
+        act(R("vals", L, 2 * L), R("P1", L, 2 * L), bias=127.25)
         act(R("nv"), G(R("vals"), R("su")), bias=-127.5)
-        rivals("p", ("pl", 0), [("MB", "a")] * NS, R("op"), PX, shift=1536.0)
+        rivals("p", "Lp", "I8", 0, 0, R("SP", 12 * ST, 12 * ST + 12), R("op", 0, 12), "Q2")
         for j in range(NS - 1, -1, -1):
-            cp(G(R("X"), R("op", PS * j, PS * j + MB)), R("nv", 16 * MB * j, 16 * MB * (j + 1)))
+            cp(G(R("X", 0, XS), R("op", MB * j, MB * j + MB)), R("nv", 16 * MB * j, 16 * MB * (j + 1)))
+        act(R("c32", 0, 12), R("r1", 24 * t + 12, 24 * t + 24))
+        tt(R("t2"), G(R("c32", 0, 12), R("cJ")), R("DG", 0, L), A.mult)
         if not last:
             act(R("hb", 0, 1), R("ymt", t, t + 1), scale=0.5, bias=143.75)
             act(R("ab", 0, 1), R("ymt", t, t + 1), scale=1.0 / 16, bias=18.0 + 1.0 / 32)
             act(R("th", 0, 1), R("hb", 0, 1), scale=-0.125, bias=R("ab", 0, 1))
             lanes(t + 1)
         else:
-            toLanes("Q0", "pr1", at=L)
-            toLanes("Q1", "pr1")
-            for b in range(8):
-                act(R("junk", 384 * b, 384 * b + 384), R("X", 384 * b, 384 * b + 384), bias=127.5, acc=R("yst", b, b + 1))
-        append(R("r1", 24 * t, 24 * t + 12), t, "r2", 16 * t, "t1", "t2")
+            mm(R("Q0", 0, 2 * L), R("BO"), M("pr1", ALL), True, True)
+            for b in range(YSA):
+                act(R("xin", 384 * b, 384 * b + 384), R("X", 384 * b, 384 * b + 384), bias=127.5, acc=R("yst", b, b + 1))
+            for b in range(YSA, 8):
+                total(R("ysv", b, b + 1), R("X", 384 * b, 384 * b + 384))
+            ts(R("yst", YSA, 8), R("ysv", YSA, 8), 127.5 * 384, A.add)
+        append(R("r1", 24 * t, 24 * t + 12), 0, "r2", 16 * t, "t1", "t2")
 
     dma("s", T.yb[:, 0:1024], R("B", 0, 1024))
     dma("a", T.yb[:, 1024:2048], R("B", 1024, 2048))
-    ts(R("oc", 0, L), R("Q0", 0, L), 1536.0, A.add)
-    cp(R("oi"), R("Q1", 0, L))
+    ts(R("oc", 0, L), R("Q0", L, 2 * L), 1536.0, A.add)
+    cp(R("oi"), R("Q0", 0, L))
     ts(R("oj", 0, L), R("oi"), 1, A.arith_shift_right)
     ts(R("oj", L, 2 * L), R("oi"), 1, A.bitwise_and)
-    cp(R("oc", L, 3 * L), R("oj"))
+    cp(R("oc", L, 2 * L), R("oj", 0, L))
+    ts(R("oc", 2 * L, 3 * L), R("oj", L, 2 * L), -1.0, A.mult, 1.0, A.add)
     dma("s", T.yc[:], R("oc", 0, L, ps=16))
     dma("s", T.ys[:], R("yst"))
     dma("s", T.ym[:], R("ymt", 0, ST, ps=16))

@@ -21,41 +21,40 @@ def _ps(n):
 
 SCRATCH = {
     "xin": _sb(S, BF), "X": _sb(XS + NV, BF), "Bi": _sb(NV, I32), "B": _sb(BS, F32),
-    "K": _sb(S, I32), "ka": _sb(KW, I32), "TT": _sb(3 * S, F32),
-    "li": _sb(3 * L, I32), "lcol": _sb(L, F32), "ld0": _sb(L, BF),
-    "pi": _sb(16, I32), "pj": _sb(16, I32), "pc": _sb(16, F32), "pt": _sb(16, F32), "it": _sb(1024, BF), "it2": _sb(208, F32),
-    "it4": _sb(144, F32), "it5": _sb(128, F32), "it6": _sb(128, F32), "it7": _sb(16, F32), "it8": _sb(16, F32),
+    "K": _sb(S, I32), "ka": _sb(KW, I32), "TT": _sb(2 * S, F32), "li": _sb(3 * L, I32), "lcol": _sb(L, F32),
+    "pi": _sb(16, I32), "pj": _sb(16, I32), "pc": _sb(16, F32), "it": _sb(1024, BF), "it2": _sb(208, F32),
+    "it4": _sb(144, F32), "it5": _sb(128, F32), "it6": _sb(128, F32), "it7": _sb(16, F32),
     "Wd": _sb(144, BF), "BO": _sb(128, BF), "BOf": _sb(128, F32), "BO8": _sb(128, BF), "RR": _sb(2048, BF),
-    "Ib": _sb(128, BF), "Ih": _sb(128, BF), "In": _sb(128, BF), "I8": _sb(128, BF), "I192": _sb(128, BF), "I2": _sb(128, BF),
-    "I2n": _sb(128, BF), "I9": _sb(128, F32), "I16": _sb(128, BF), "Ie": _sb(128, BF), "Sw": _sb(128, BF),
-    "Sel": _sb(1024, BF), "DG": _sb(208, F32), "NDG": _sb(208, F32), "NDm": _sb(208, BF), "sc1": _sb(L, F32),
-    "DK": _sb(16, BF), "DP": _sb(48, BF), "MK": _sb(SL, BF), "AJ": _sb(NS * SL, BF), "MJ": _sb(NS * SL, BF),
-    "SP": _sb(12 * (ST + 1), F32), "n8": _sb(16, BF), "cJ": _sb(12, U16), "nid16": _sb(16, F16), "cst": _sb(24, BF),
-    "E": _sb(L, U16), "Ec": _sb(L, F16), "xe": _sb(S, BF), "H": _sb(S, F16), "LT": _sb(128, F16), "cT": _sb(128, F16),
+    "Ib": _sb(128, BF), "In": _sb(128, BF), "I8": _sb(128, BF), "I192": _sb(128, BF), "I9": _sb(128, F32), "I16": _sb(128, BF),
+    "Sw": _sb(128, BF), "Sel": _sb(1024, BF), "DG": _sb(208, F32), "NDG": _sb(208, F32), "NDm": _sb(208, BF), "sc1": _sb(L, F32),
+    "DK": _sb(16, BF), "DP": _sb(48, BF), "DQ": _sb(48, BF), "MJ": _sb([NS, SL], BF), "CR": _sb(144, F16),
+    "sa": _sb(12 * ST, I32), "sb": _sb(12 * ST, I32), "SP": _sb(12 * (ST + 1), F32), "w3": _sb(16, BF),
+    "cJ": _sb(12, U16), "nid16": _sb(16, F16), "cst": _sb(24, BF),
+    "E": _sb(L, U16), "Ec": _sb(L, F16), "xe": _sb(S, BF), "H": _sb(S, F16), "LT": _sb(128, F16), "cT": _sb(256, F16),
     "QS": _sb(2 * L, BF), "QT": _sb(256, F16), "qN": _sb(L, BF), "f4": _sb(L, BF), "yN": _sb(L, BF), "kc": _sb(L, F16), "ke": _sb(L, F16),
     "SX": _sb(L, F32), "th": _sb(4, F32), "hb": _sb(4, BF), "ab": _sb(4, F32),
     "Y": _sb(L, F32), "h16": _sb(L, F16), "tt": _sb(L, BF), "R1": _sb(L, I32), "R1k": _sb(L, F32), "R2": _sb(L, F32),
     "key": _sb(L, F32), "scn": _sb(L, I32),
-    "kk": _sb(12, I32), "ku": _sb(12, U16), "z2": _sb(12, I32), "lo": _sb(12, I32), "hit": _sb(12, BF),
-    "pb": _sb(12, F32), "pd": _sb(12, I32), "pe": _sb(12, I32), "pu": _sb(12, U16),
-    "ms": _sb(12, F32), "mc": _sb(4, F32), "ymt": _sb(8, F32),
+    "kk": _sb(12, I32), "ku": _sb(12, U16), "z2": _sb(12, I32), "lo": _sb(12, I32), "hit": _sb(12, BF), "pb": _sb(12, F32),
+    "pu": _sb(12, U16), "ms": _sb(12, F32), "mc": _sb(4, F32), "ymt": _sb(8, F32),
     "prE": _sb(L, F16), "mp": _sb(L, F32), "pr1": _sb([2 * NS, 64], F16), "pr2": _sb(2 * L, F16), "Lp": _sb([NS, 64], F16),
-    "ew": _sb(12, U16), "eN": _sb(12, U16), "c32": _sb(16, F32),
-    "m1": _sb(24 * ST, U16), "m2": _sb(16 * ST, U16), "r1": _sb(24 * ST, U16), "r2": _sb(16 * ST, U16),
+    "ew": _sb(12, U16), "ex": _sb(12, U16), "eN": _sb(12, U16), "ei": _sb(12, I32), "ej": _sb(12, I32), "c32": _sb(16, F32),
+    "m1": _sb(24 * ST, U16), "m2": _sb(16 * ST, U16), "r1": _sb(24 * ST, U16), "r2": _sb(16 * ST, U16), "c2T": _sb(128, F16),
     "oo": _sb(16, U16), "op": _sb(16, U16), "aT2": _sb(128 * ST, F16), "aTo": _sb(128, F16), "aTp": _sb(128, F16),
     "ds2": _sb(16, F32), "dso": _sb(16, F32), "dsp": _sb(16, F32),
     "t1": _sb(L, F32), "t2": _sb(L, F32), "t3": _sb(L, F32), "t4": _sb(L, F32),
     "pm": _sb(12, F32), "pn": _sb(12, F32), "p16": _sb(16, F16), "su": _sb(12, U16), "cc": _sb(12, F32),
     "vals": _sb(2 * L, I32), "nv": _sb(L, BF),
-    "D0": _sb(12, BF), "D1": _sb(12, BF), "oN": _sb(12, U16), "cu": _sb(12, U16), "QO": _sb(24, U16), "ou": _sb(12, U16), "Sd": _sb(12, F32),
+    "D": _sb(12, BF), "Di": _sb(12, I32), "Dj": _sb(12, I32), "Sd": _sb(24, F32), "oN": _sb(12, U16), "ou": _sb(12, U16),
+    "cu": _sb(12, U16), "QO": _sb(24, U16), "ci": _sb(12, I32), "cj": _sb(12, I32), "cw": _sb(12, U16),
     "yst": _sb(8, F32), "ysv": _sb(8, F32), "oc": _sb(3 * L, F32), "oi": _sb(L, I32), "oj": _sb(2 * L, I32),
-    "Q0": _ps([512]), "Q1": _ps([512]), "Q2": _ps([512]), "P1": _ps([512]), "P2": _ps([512]), "MA": _ps([512]), "MB": _ps([512]),
-    "RV": _ps([NS, 170]),
+    "Q0": _ps([512]), "Q1": _ps([512]), "Q2": _ps([512]), "P1": _ps([512]), "MA": _ps([512]), "MB": _ps([512]),
+    "P2": _ps([NS, 170]), "RV": _ps([NS, 170]),
 }
-BUFS = dict(SCRATCH)
+BUFS = dict(SCRATCH, MK=SCRATCH["MJ"])
 PLACE = {}
 _end = {}
-for _n, (_w, _s, _d) in BUFS.items():
+for _n, (_w, _s, _d) in list(SCRATCH.items()):
     if _w == "sbuf" and len(_s) == 2 and _s[1] <= 48:
         _a = "short_" + _d
         PLACE[_n] = (_a, _end.get(_a, 0))
@@ -64,19 +63,19 @@ for _n, (_w, _s, _d) in BUFS.items():
         SCRATCH[_a] = _sb(_end[_a], _d)
     else:
         PLACE[_n] = (_n, 0)
-SCRATCH["RV"] = SCRATCH.pop("RV")
-NDMA = 44
+NDMA = 48
 SEMAPHORES = (["qv", "qa", "qp", "qg", "sent"] + ["d%d" % i for i in range(NDMA)]
               + ["ra%d" % t for t in range(ST)] + ["rb%d" % t for t in range(ST)])
 PSUM = ("Q0", "Q1", "Q2", "P1", "P2", "MA", "MB", "RV")
 WIDTH = {F32: 4, I32: 4, BF: 2, F16: 2, U16: 2}
-CYC, PEC, GAT, SCA, HOP, FAR, FIX, DL, DB = 0.83, 0.42, 1.5, 3.5, 170.0, 2300.0, 50.0, 1500.0, 200.0
+CYC, PEC, GAT, SCA, HOP, FAR, FIX, DL, DB = 0.83, 0.42, 1.5, 3.5, 170.0, 2300.0, 50.0, 1300.0, 330.0
 PLAN = {}
-ROUNDS, NOISE = 200, 1500.0
+ROUNDS, NOISE, SHARE, SLACK = 500, 1500.0, (0.05, 0.2, 0.5), 300.0
+NT, NK = 1, 2
 PIECES = [(0, 32, "a"), (32, 72, "v"), (72, 96, "a"), (96, 128, "a"), (128, 160, "a"), (160, 180, "a"), (180, 192, "a")]
 MINS = [0, 32, 64, 96, 128, 160, 180, 192]
 ESPLIT, YSA = 32, 5
-ON = dict(cT="a", ku="v", pu="a", ew="v", aT2="a", aTo="a", aTp="a", m1="a", ou="a", R1="v")
+ON = dict(aT2="a", aTp="a", m1="a", ou="a", R1="v")
 
 
 def plan(ops):
@@ -86,7 +85,7 @@ def plan(ops):
     succ = [[] for _ in range(n)]
     for i, o in enumerate(ops):
         for d in o["deps"] | o["order"]:
-            lag = ops[d]["lat"] + (HOP if d in o["deps"] else 0.0)
+            lag = ops[d]["lat"] + HOP if d in o["deps"] else (ops[d]["lat"] if o["kind"] == "x" else 0.0)
             pred[i].append((d, lag))
             succ[d].append((i, lag))
     tail = [o["lat"] for o in ops]
@@ -119,33 +118,25 @@ def plan(ops):
         far[i] = cost[i] + max([far[s] + lag for s, lag in succ[i]] + [tail[i]])
     zero = [0.0] * n
     rng = np.random.default_rng(7)
+    names = {}
+    kin = np.array([names.setdefault((o["q"], o["tag"], o["nth"]), len(names)) for o in ops])
 
-    def ranked(key, before, after):
-        key = list(key)
-        left = [len(b) for b in before]
-        ready = [i for i in range(n) if not left[i]]
-        seq = []
-        while ready:
-            i = min(ready, key=lambda k: key[k])
-            ready.remove(i)
-            seq.append(i)
-            for s, _ in after[i]:
-                left[s] -= 1
-                if not left[s]:
-                    ready.append(s)
-        return seq
-
-    best = None
-    st = fill(sorted(range(n), key=lambda i: -far[i]), pred, zero)
-    for k in range(ROUNDS):
-        span = max(st[i] + cost[i] + tail[i] for i in range(n))
-        if best is None or span < best[0]:
-            best = (span, st)
-        noise = rng.random(n) * (NOISE if k % 3 == 2 else 0.0)
-        if k % 3 == 2:
-            st = best[1]
-        back = fill(ranked([-(st[i] + cost[i]) + noise[i] for i in range(n)], succ, pred), succ, tail)
+    def both(st, shift):
+        key = [shift[i] - st[i] - cost[i] for i in range(n)]
+        for i in range(n - 1, -1, -1):
+            for d, _ in succ[i]:
+                if key[i] <= key[d]:
+                    key[i] = key[d] + 0.001
+        back = fill(sorted(range(n), key=lambda i: key[i]), succ, tail)
         st = fill(sorted(range(n), key=lambda i: -(back[i] + cost[i])), pred, zero)
+        return max(st[i] + cost[i] + tail[i] for i in range(n)), st
+
+    best = both(fill(sorted(range(n), key=lambda i: -far[i]), pred, zero), zero)
+    for k in range(ROUNDS):
+        some = rng.random(n) < SHARE[k % len(SHARE)]
+        new = both(best[1], ((rng.random(n) - 0.5) * some)[kin] * NOISE)
+        if new[0] < best[0] + SLACK * (1 - k / ROUNDS):
+            best = new
     st = best[1]
     PLAN["end"] = [st[i] + cost[i] + tail[i] for i in range(n)]
     return sorted(range(n), key=lambda i: st[i])
@@ -161,6 +152,7 @@ def rank_program(g, core, T, topo):
     seen = {}
     bank = {}
     ndma = [0]
+    nth = {}
 
     def R(name, lo=0, hi=None, step=1, p0=0, p1=128, ps=1):
         w = BUFS[name][1][1]
@@ -171,10 +163,10 @@ def rank_program(g, core, T, topo):
         cols = sum(1 << c for c in range(lo, hi, step)) if step > 1 else (1 << hi) - (1 << lo)
         return (ap, [(name, cols)], [], len(range(lo, hi, step)), WIDTH[BUFS[name][2]], name in PSUM)
 
-    def M(name, *idx):
+    def M(name, *idx, p0=0, p1=128):
         shape = BUFS[name][1][1:]
         flat = np.arange(int(np.prod(shape))).reshape(shape)[idx]
-        return (T[name][(slice(None),) + idx], [(name, sum(1 << int(c) for c in flat.flat))], [], int(flat.size),
+        return (T[{"MK": "MJ"}.get(name, name)][(slice(p0, p1),) + idx], [(name, sum(1 << int(c) for c in flat.flat))], [], int(flat.size),
                 WIDTH[BUFS[name][2]], name in PSUM)
 
     def G(win, off):
@@ -209,8 +201,10 @@ def rank_program(g, core, T, topo):
                 bank[name] = me
             if wr:
                 lst[:] = [a for a in lst if not (a[0] & ~cols == 0 and a[1] in deps)]
+        tag = outs[0][1][0][0] if outs else kind
         ops.append({"q": q, "call": call, "deps": deps, "order": order - deps, "sem": sem, "kind": kind, "cost": cost, "lat": lat,
-                    "tag": (outs[0][1][0][0] if outs else kind)})
+                    "tag": tag, "nth": nth.get((q, tag), 0) if q != "p" else 0})
+        nth[(q, tag)] = ops[-1]["nth"] + 1
         for (name, cols), wr in acc:
             seen[name].append([cols, me, wr])
         return me
@@ -277,16 +271,16 @@ def rank_program(g, core, T, topo):
         else:
             add("g", lambda: g.iota(o[0], pat, base, cm, allow_small_or_imprecise_dtypes=True), [o], [], c)
 
-    def select(o, pat):
-        add("g", lambda: g.affine_select(o[0], o[0], pat, A.is_equal, 0.0, 0, 1), [o], [o], 170.0 + 2 * CYC * o[3])
+    def select(o, i, pat, cm):
+        add("g", lambda: g.affine_select(o[0], i[0], pat, A.is_equal, 0.0, 0, cm), [o], [i], 170.0 + 2 * CYC * o[3])
 
-    def dma(q, o, i, wait=()):
+    def dma(q, o, i, wait=(), after=(), ahead=0):
         e = {"s": g.sync, "a": g.scalar, "g": g}[q]
         sem = "d%d" % ndma[0]
         ndma[0] += 1
         sb = o if isinstance(o, tuple) else i
         return add(q, lambda: e.dma_start(a0(o), a0(i)), [o] if isinstance(o, tuple) else [], [i], 100.0, kind="d", sem=sem,
-                   lat=DL + 128 * sb[3] * sb[4] / DB, wait=wait)
+                   lat=DL + 128 * (ahead + sb[3] * sb[4]) / DB, wait=wait, after=after)
 
     def engines_to(dst):
         es = topo.engines(core, dst)
@@ -312,34 +306,31 @@ def rank_program(g, core, T, topo):
         return slice(a, b, step)
 
     ALL = slice(None)
-    PC, PK, PR0, PPI, PNI, P64, PG, PX1, PLT, PU, PB16, PS16, PB17, PG0, PW = [R("pc", i, i + 1) for i in range(15)]
-    SJ = R("Sel", 0, L, p1=12)
+    PC, PK, PR0, PPI, PNI, P64, PG, PX1, PLT, PU, PB16, PS16, PB17, PW = [R("pc", i, i + 1) for i in range(14)]
+    SJ, GS, I12 = R("Sel", 0, L, p1=12), R("BO", 0, 128, 16), R("Ib", 0, 12, p1=12)
+    U = M("P2", ALL, every(0, 64))
     PV1, PC1 = M("pr1", every(0, NS)), M("pr1", every(NS, 2 * NS))
 
     ms(R("li"), 0)
-    dma("s", R("li", 0, L, ps=16), T.lc[:])
-    dma("a", R("li", L, 2 * L, ps=16), T.lv[:])
-    dma("s", R("li", 2 * L, 3 * L, ps=16), T.ld[:])
-    big = [dma("a", R("xin", 0, S // 2), T.x[:, 0:S // 2]), dma("s", R("xin", S // 2, S), T.x[:, S // 2:S]), dma("s", R("Bi"), T.bnd[:])]
-    dma("s", R("K", 0, KW), T.kt[:], wait=big[:2])
+    big = [dma("a", R("xin", 0, S // 2), T.x[:, 0:S // 2])]
+    small = [dma("s", R("li", L * k, L * k + L, ps=16), src[:]) for k, src in enumerate((T.lv, T.ld, T.lc))]
+    big.append(dma("s", R("xin", S // 2, S), T.x[:, S // 2:S], after=small, ahead=S // 2))
+    big.append(dma("s", R("Bi"), T.bnd[:], after=big[1:], ahead=3 * S // 2))
+    dma("s", R("K", 0, KW), T.kt[:], after=big[2:], ahead=3 * S // 2 + 4 * NV)
     iota(R("pi", 0, 1), [[0, 1]], 0, 1)
-    iota(R("pi", 8, 8 + ST), [[-5, ST]], 48, 1)
     iota(R("it4"), [[1, 144]], -16, -1)
     iota(R("it5"), [[16, 8], [0, 16]], 0, -1)
     iota(R("it6"), [[1, 128]], 0, -1)
     iota(R("it7"), [[1, 16]], 0, 0)
-    iota(R("it8", 0, 12), [[0, NS], [16, MB]], NV, 0)
     iota(R("it2"), [[0, 13], [1, 16]], 0, 0)
     iota(R("it"), [[1, 64], [0, 16]], 0, 0)
     ts(R("pj", 0, 1), R("pi", 0, 1), 15, A.bitwise_and)
     ts(R("pj", 1, 2), R("pi", 0, 1), 63, A.bitwise_and)
     ts(R("pj", 2, 3), R("pi", 0, 1), 1, A.bitwise_and)
-    ts(R("pj", 8, 8 + ST), R("pi", 8, 8 + ST), 15, A.bitwise_and)
     cp(PC, R("pj", 0, 1))
     cp(P64, R("pj", 1, 2))
     cp(PPI, R("pj", 2, 3))
-    act(PG, R("pi", 0, 1), bias=-12.0)
-    act(R("pt", 0, ST), R("pj", 8, 8 + ST))
+    act(PG, R("pi", 0, 1), bias=-32.0)
     act(PK, PC, scale=-1.0, bias=15.0)
     ts(PR0, PC, 0.0, A.is_equal)
     act(PNI, PPI, scale=-2.0, bias=1.0)
@@ -362,103 +353,109 @@ def rank_program(g, core, T, topo):
     ts(R("DG"), R("it2"), PC, A.is_equal)
     ts(R("NDG"), R("it2"), PC, A.not_equal)
     ts(R("DK"), R("it7"), PK, A.is_equal)
-    ts(R("DP"), R("it2", 1, 49), PX1, A.is_equal)
-    ts(R("sc1"), R("it2", 0, L), 0.0, A.not_equal, 2.0 ** 24, A.mult)
-    ts(R("sc1"), R("sc1"), 32.0 - 2.0 ** 24, A.add)
+    ts(R("DP"), R("it2", 15, 63), PX1, A.add, 0.0, A.is_equal)
+    ts(R("DQ"), R("it2", 15, 63), PX1, A.add, 16.0, A.is_equal)
+    tt(R("DP"), R("DP"), R("DQ"), A.add)
+    ms(R("sc1"), 32.0)
+    ms(R("sc1", 0, L, 16), -2.0 ** 24)
     ts(R("Sel"), R("it"), P64, A.is_equal)
     ms(R("th"), 1.0 / 32)
     iota(R("RR"), [[0, 2048]], 1, 0)
-    select(R("RR"), [[-1, 16], [-16, 8], [0, 16]])
+    select(R("RR"), R("RR"), [[-1, 16], [-16, 8], [0, 16]], 1)
     act(R("NDm"), R("NDG"), scale=-4096.0)
-    for nm, k in (("I192", -float(L)), ("Ih", 0.5), ("In", -1.0), ("I8", 8192.0), ("I2", 2.0), ("I2n", -2.0), ("I9", 2.0 ** -9),
-                  ("I16", -16.0), ("Ie", 0.0625)):
+    for nm, k in (("I192", -float(L)), ("In", -1.0), ("I8", 8192.0), ("I9", -2.0 ** -9), ("I16", 16.0)):
         act(R(nm), R("Ib"), scale=k)
     act(R("BOf"), R("BO"))
     act(R("BO8"), R("BO"), scale=8192.0)
+    ts(R("CR"), R("it2", 0, 144), PG, A.is_equal, PB16, A.add)
     for t in range(ST):
         s = (5 * t) % 16
-        ts(R("aT2", 128 * t, 128 * t + 128), R("it2", 16 - s, 144 - s), PG, A.is_equal, PB16, A.add)
+        dma("s", R("aT2", 128 * t, 128 * t + 128, p0=12, p1=50), R("CR", 16 - s, 144 - s, p0=12, p1=50))
     ts(R("aTo"), R("it2", 0, 128), PG, A.is_equal, PB17, A.add)
     ts(R("aTp"), R("it2", 0, 128), PG, A.is_equal, PS16, A.add)
-    act(PG0, PW, scale=4096.0)
-    act(R("n8", 0, 12), R("Ib", 0, 12), scale=-8192.0)
-    ms(R("MK"), 0.0)
+    UP = dict(p0=32, p1=64)
+    for a in range(MB):
+        iota(M("MJ", ALL, every(SEG[a], SEG[a + 1]), p1=32), [[MB, NS], [0, 16 * a + 16]], a, -1)
+    ts(M("MJ", ALL, p1=32), M("MJ", ALL, p1=32), 0.0, A.is_equal, -8192.0, A.mult)
+    ms(M("MK", ALL, **UP), 0.0)
+    ts(R("w3", 0, NS, **UP), R("it2", 0, 48, 16, **UP), R("pc", 13, 14, **UP), A.add)
     for a in range(MB):
         e = SEG[a + 1] - 1
-        ts(R("MK", e - 15, e), R("it7", 0, 15), PG, A.is_ge, PG0, A.mult)
-        ts(R("MK", e, e + 1), PW, 16.0 * a, A.mult, PU, A.add)
-        for s in range(NS):
-            act(R("AJ", SL * s + SEG[a], SL * s + e), R("it2", 0, e - SEG[a]), scale=0.0, bias=R("n8", MB * s + a, MB * s + a + 1))
-        act(R("AJ", e, None, SL), R("Ib", a, 12, MB), scale=-1.0)
-    for s in range(NS):
-        tt(R("MJ", SL * s, SL * s + SL), R("AJ", SL * s, SL * s + SL), R("MK"), A.add)
-    for t in range(ST):
-        act(R("SP", 12 * t, 12 * t + 12), R("it8", 0, 12), bias=R("pt", t, t + 1))
+        act(M("MJ", ALL, e, p1=32), M("MJ", ALL, e, p1=32), scale=2.0 ** -13)
+        ts(M("MK", ALL, every(e - 15, e + 1), **UP), R("it2", 0, 48, **UP), R("pc", 6, 7, **UP), A.is_ge, 4096.0, A.mult)
+        ts(M("MK", ALL, e, **UP), R("w3", 0, NS, **UP), 16.0 * a, A.mult, R("pc", 9, 10, **UP), A.add)
+    iota(R("sa"), [[-5, ST], [0, 12]], 48, 1)
+    iota(R("sb"), [[0, ST * NS], [16, MB]], NV, 0)
+    ts(R("sa"), R("sa"), 15, A.bitwise_and)
+    tt(R("SP", 0, 12 * ST), R("sa"), R("sb"), A.add)
     act(R("SP", 12 * ST, 12 * ST + 12), R("SP", 0, 12), bias=float(S - NV))
-    act(R("B", 0, NV // 2), R("Bi", 0, NV // 2))
-    cp(R("B", NV // 2, NV), R("Bi", NV // 2, NV))
+    select(R("B", 0, NV), R("Bi"), [[0, NV]], 0)
     ms(R("B", NV, BS), 0.0)
     ts(R("ka"), R("K", 0, KW), 1023, A.bitwise_and)
-    ts(R("TT", 0, KW), R("ka"), 2.0, A.mult, PPI, A.add)
-    act(R("TT", S, S + KW), R("TT", 0, KW), bias=PNI)
+    act(R("TT", S - KW, S), R("ka"), scale=2.0, bias=PPI)
+    act(R("TT", S, S + KW), R("TT", S - KW, S), bias=PNI)
     for k in range(1, S // KW):
-        dma("s", R("K", KW * k, KW * k + KW), T.kt[:], wait=big)
-    for o in (0, S):
-        for k in range(1, S // KW):
-            dma("s", R("TT", o + KW * k, o + KW * k + KW), R("TT", o, o + KW), wait=big)
-    dma("s", R("TT", 2 * S, 3 * S), R("TT", 0, S))
+        dma("s", R("TT", S - KW * (k + 1), S - KW * k), R("TT", S - KW, S), ahead=8 * KW * (k - 1))
+        more = dma("s", R("TT", S + KW * k, S + KW * (k + 1)), R("TT", S, S + KW), ahead=8 * KW * k - 4 * KW)
+    for k in range(1, S // KW):
+        dma("s", R("K", KW * k, KW * k + KW), T.kt[:], wait=[more], ahead=4 * KW * (k - 1))
     ts(R("X", 0, 1536), R("xin", 0, 1536), -127.5, A.add)
     ts(R("X", 1536, S), R("xin", 1536, S), -127.5, A.add)
     ms(R("X", S, XS), 0.0)
-    iota(R("X", XS, XS + 512), [[0, 256], [-2, 2]], 1, 0)
-    for k in range(1, NV // 512):
-        dma("s", R("X", XS + 512 * k, XS + 512 * k + 512), R("X", XS, XS + 512))
-    act(R("lcol"), R("li", L, 2 * L), scale=2.0, bias=PR0)
-    tt(PV1, R("lcol"), R("li", 2 * L, 3 * L), A.subtract)
-    ts(PC1, R("li", 0, L), -1536.0, A.add, PR0, A.mult)
-    act(R("ld0"), R("li", 2 * L, 3 * L))
-    for r in range(16):
-        mm(R("Q2", 0, 12), Sr(r), R("ld0", r, L, 16), r == 0, r == 15)
-    act(R("D0"), R("Q2", 0, 12))
+    ms(R("X", XS, XS + NV, 2), 0.0625)
+    ms(R("X", XS + 1, XS + NV, 2), -0.0625)
+    act(R("lcol"), R("li", 0, L), scale=2.0, bias=PR0)
+    tt(PV1, R("lcol"), R("li", L, 2 * L), A.subtract)
+    ts(PC1, R("li", 2 * L, 3 * L), -1536.0, A.add, PR0, A.mult)
 
     def lanes(t):
         s = (5 * t) % 16
-        D = "D%d" % (t % 2)
         for a in range(16):
             at = 16 * (a % 4) + a // 4
             mm(R("Q0", 0, 24), Sr(a), M("pr1", ALL, every(at, at + 13, 4)), a == 0, a == 15)
         plus("ou", R("ou"), R("Q0", 0, 12))
         act(R("QO", 0, 12), R("Q0", 12, 24), bias=1536.0)
         act(R("QO", 12, 24), R("Q0", 0, 12), bias=float(XS))
-        for r in range(16):
-            mm(R("Q1", 0, 24), Sr(r), M("pr1", ALL, every(r, 64, 16)), r == 0, r == 15)
+        for o, k, w in ((0, 0, 0), (128, s, NS), (256, 0, NS)):
+            for r in range(16):
+                mm(R("MB", o + (r + k) % 16, o + 128, 16, p1=12), M("pr1", every(w, w + NS), every(r, 64, 16)), GS, True, True)
+        act(R("aTo", p1=12), R("MB", 0, 128, p1=12))
+        act(R("cT", p1=12), R("MB", 128, 384, p1=12))
+        mm(R("Q1", 0, 12), R("aTo", p1=12), I12, True, True)
+        mm(R("Q1", 12, 24), R("cT", 128, 256, p1=12), I12, True, True)
         act(R("oN"), R("Q1", 0, 12))
         act(R("cu"), R("Q1", 12, 24), bias=1536.0)
         act(R("cc"), R("Q1", 12, 24))
-        act(R("Sd"), R(D), scale=float(S), bias=1536.0)
+        act(R("Di"), R("Q1", 0, 12))
+        ts(R("Dj"), R("Di"), 1, A.bitwise_and)
+        act(R("D"), R("Dj"), scale=-2.0, bias=2.0)
+        w, b = (float(KW), 0.0) if t < NT else (float(S), 1536.0)
+        act(R("Sd", 0, 12), R("Dj"), scale=-w, bias=b + w)
+        act(R("Sd", 12, 24), R("Dj"), scale=w, bias=b)
         act(R("QS"), G(R("X"), R("QO")))
         for b in range(2):
             mm(R("MA", 128 * b, 128 * b + 128), R("QS", 64 * b, 64 * b + 128), R("Ib"), True, False)
-            mm(R("MA", 128 * b, 128 * b + 128), R("QS", L + 64 * b, L + 64 * b + 128), R("Ie"), False, True)
+            mm(R("MA", 128 * b, 128 * b + 128), R("QS", L + 64 * b, L + 64 * b + 128), R("Ib"), False, True)
         act(R("QT"), R("MA", 0, 256))
         act(R("qN"), G(R("X", 0, XS), R("cu")))
-        mm(R("MB", 256, 384, p1=12), R(D), R("I2"), True, False)
+        mm(M("P2", 0, every(0, 128), p1=12), R("D"), R("Ib"), True, False)
         for r in range(16):
-            mm(R("MB", 256 + r, 384, 16, p1=12), R("qN", r, L, 16), R("BO", 0, 128, 16), False, r == 15)
-        act(R("LT", p1=12), R("MB", 256, 384, p1=12), scale=-1.0, bias=1.0)
-        act(R("SX"), G(R(D), R("cJ")), scale=-2.0 ** -17, bias=2.0 ** -18)
+            mm(M("P2", 0, every(r, 128, 16), p1=12), R("qN", r, L, 16), GS, False, r == 15)
+        act(R("LT", p1=12), M("P2", 0, every(0, 128), p1=12), scale=-1.0, bias=1.0)
+        act(R("SX"), G(R("D"), R("cJ")), scale=-2.0 ** -18, bias=2.0 ** -18)
         for c in range(3):
             spread(c)
         mm(R("P1", 0, L), R("LT", p1=12), SJ, True, False)
-        mm(R("P2", 0, L), R("LT", p1=12), SJ, True, False)
-        act(R("f4"), R("qN"), scale=0.25, bias=31.5 + 192.0)
-        act(R("kc"), G(R("K"), R("cu")), bias=-1536.0)
-        rivals("o", "pr1", "BO8", 0, 0, R("SP", 0, 12), R("oo", 0, 12), "MB", D)
-        for r in range(16):
-            mm(R("MB", 128 + (r + s) % 16, 256, 16, p1=12), M("pr1", every(NS, 2 * NS), every(r, 64, 16)), R("BO", 0, 128, 16), True, True)
-        plus("cT", R("cT", p1=12), R("MB", 128, 256, p1=12))
+        mm(U, R("LT", p1=12), SJ, True, False)
+        act(R("f4"), R("qN"), scale=-0.25, bias=-31.5 - 192.0)
+        if t < NK:
+            act(R("ci"), R("cc"), bias=1536.0)
+            ts(R("cj"), R("ci"), KW - 1, A.bitwise_and)
+            act(R("cw"), R("cj"))
+        act(R("kc"), G(R("K", 0, KW), R("cw")) if t < NK else G(R("K"), R("cu")), bias=-1536.0)
+        rivals("o", "RV", "pr1", "BO8", 0, R("SP", 0, 12), R("oo", 0, 12), "D")
         mm(R("MB", 0, L), R("Ib"), R("NDm", s, s + L), True, False)
-        mm(R("MB", 0, L), R("cT", p1=12), SJ, False, True)
+        mm(R("MB", 0, L), R("cT", 0, 128, p1=12), SJ, False, True)
         act(R("t4"), R("MB", 0, L), AF.Relu, bias=1536.0)
         mm(R("MA", 0, L), R("Ib"), R("kc"), True, True)
         mm(R("MA", L, 2 * L), R("Sw"), R("kc"), True, True)
@@ -468,25 +465,19 @@ def rank_program(g, core, T, topo):
         mm(R("Q%d" % (c % 3)), R("QT", 128 * b, 128 * b + 128, p0=p, p1=p + 64), R("Sel", 512 * (c % 2), 512 * (c % 2) + 512, p0=p, p1=p + 64),
            True, True)
 
-    def rivals(k, src, lw, s, at, spare, off, bk, side=None):
-        rv = M("RV", ALL, every(0, SL))
-        if k == "p":
-            mm(R(bk, 0, 128, p1=12), R("p16", 0, 12), R("Ib"), True, True)
-        else:
-            for r in range(16):
-                row = R(src, r, L, 16) if k == "2" else M(src, every(0, NS), every(r, 64, 16))
-                mm(R(bk, (r + s) % 16, 128, 16, p1=12), row, R("BO", 0, 128, 16), True, True)
-        plus("aT" + k, R("aT" + k, at, at + 128, p1=12), R(bk, 0, 128, p1=12))
+    def rivals(k, RV, src, lw, at, spare, off, side="cst"):
+        for a in range(MB):
+            mm(M(RV, ALL, SEG[a + 1] - 1), R("In"), R(side, a, 12, MB), a == 0, False)
         for a in range(MB):
             if k == "2":
                 for c in range(NS):
-                    mm(M("RV", c, every(SEG[a], SEG[a + 1] - 1)), R(lw), R(src, 64 * c, 64 * c + 16 * a + 15), a + c == 0, False)
+                    mm(M(RV, c, every(SEG[a], SEG[a + 1] - 1)), R(lw), R(src, 64 * c, 64 * c + 16 * a + 15), False, False)
             else:
-                mm(M("RV", ALL, every(SEG[a], SEG[a + 1] - 1)), R(lw), M(src, every(0, NS), every(0, 16 * a + 15)), a == 0, False)
-            mm(M("RV", ALL, SEG[a + 1] - 1), R("I2n"), R(side or "cst", a, 12, MB), False, False)
-        mm(rv, R("aT" + k, at, at + 128, p1=30), R("MJ", p1=30), False, True)
+                mm(M(RV, ALL, every(SEG[a], SEG[a + 1] - 1)), R(lw), M(src, every(0, NS), every(0, 16 * a + 15)), False, False)
+        mj = M("MJ", ALL, p1=50)
+        mm(M(RV, ALL, every(0, SL)), R("aT" + k, at, at + 128, p1=50), (mj[0], mj[1] + M("MK", ALL)[1]) + mj[2:], False, True)
         for a in range(MB - 1, -1, -1):
-            least(R("ds" + k, a, 12, MB), M("RV", ALL, every(SEG[a], SEG[a + 1])))
+            least(R("ds" + k, a, 12, MB), M(RV, ALL, every(SEG[a], SEG[a + 1])))
         tt(off, spare, R("ds" + k, 0, 12), A.subtract)
 
     def append(cols, s, name, base, t1, t2):
@@ -500,17 +491,17 @@ def rank_program(g, core, T, topo):
         last = t == ST - 1
         to = T.cores[(rank + 1 + t % (N - 1)) % N]
         s = (5 * t) % 16
-        D, Dn = "D%d" % (t % 2), "D%d" % (1 - t % 2)
         Bt = R("Bi") if t == 0 else R("B")
+        nth.clear()
         act(R("E", 0, ESPLIT), G(Bt, R("ou", 0, ESPLIT // 16)))
         cp(R("E", ESPLIT, L), G(Bt, R("ou", ESPLIT // 16, 12)))
         done, prev = [0, 0], []
 
         def sums(n, which):
-            src, o = (("xe", "P2"), ("H", "P1"))[which]
             while 4 * (done[which] + 1) <= n:
                 c, r = divmod(done[which], 16)
-                mm(R(o, 64 * c, 64 * c + 64), Sr(r), R(src, 64 * done[which], 64 * done[which] + 64), False, (which, c, r) == (0, 2, 15))
+                o = R("P1", 64 * c, 64 * c + 64) if which else M("P2", c, every(0, 64))
+                mm(o, Sr(r), R(("xe", "H")[which], 64 * done[which], 64 * done[which] + 64), False, (which, c, r) == (0, 2, 15))
                 done[which] += 1
 
         for lo, hi, e in PIECES:
@@ -525,9 +516,9 @@ def rank_program(g, core, T, topo):
             sums(hi, 0)
         act(R("Ec"), G(Bt, R("oN")), bias=-1536.0)
         append(R("oo", 0, 12), s, "oo", 0, "t3", "t4")
-        tt(R("tt"), R("SX"), R("P2", 0, L), A.mult)
-        act(R("Y"), R("P2", 0, L), scale=512.0, bias=512.0 * 8192)
-        act(R("h16"), R("P2", 0, L), scale=1.0 / 16, bias=1536.0)
+        tt(R("tt"), R("SX"), U, A.mult)
+        act(R("Y"), U, scale=512.0, bias=512.0 * 8192)
+        act(R("h16"), U, scale=1.0 / 16, bias=1536.0)
         for a, b in zip(MINS, MINS[1:]):
             c = a // 32
             tt(R("H", 16 * a, 16 * b), R("xe", 16 * a, 16 * b), R("Q%d" % (c % 3), 16 * (a - 32 * c), 16 * (b - 32 * c)), A.min)
@@ -538,7 +529,7 @@ def rank_program(g, core, T, topo):
         mm(R("Q1", 0, L), R("I9"), R("Y"), True, False)
         mm(R("Q1", 0, L), R("I16"), R("h16"), False, True)
         plus("R1", R("R1"), R("P1", 0, L), R("th", 0, 1))
-        act(R("R1k"), R("R1"), scale=1024.0, bias=C0 + 16 * 1536.0 - 8192 + 14)
+        act(R("R1k"), R("R1"), scale=1024.0, bias=C0 - 16 * 1536.0 + 8192 + 18)
         tt(R("P1", 256, 256 + L), R("R1"), R("P1", 0, L), A.is_gt)
         tt(R("R2"), R("R1k"), R("Q1", 0, L), A.add)
         tt(R("P1", 256, 256 + L), R("P1", 256, 256 + L), R("Y"), A.mult)
@@ -546,56 +537,65 @@ def rank_program(g, core, T, topo):
         scan(R("scn"), R("sc1"), R("key"), 0.0, A.add, A.max)
         best = R("scn", 15, L, 16)
         ts(R("kk"), best, 5, A.arith_shift_right, 15, A.bitwise_and)
-        plus("ku", R("ku"), R("kk"))
+        cp(R("ku"), R("kk"))
         tt(R("prE"), G(R("DK"), R("ku")), R("Ec"), A.mult)
         ts(R("hit"), best, 512.0 * 4100, A.is_gt)
         ts(R("lo"), best, 31, A.bitwise_and)
         ts(R("z2"), best, 9, A.arith_shift_right, 15, A.bitwise_and)
         tt(R("pb"), R("lo"), R("hit"), A.mult)
-        tt(R("pd"), R("pb"), R("z2"), A.subtract)
-        plus("pu", R("pu"), R("pd"), 16.0)
+        tt(R("pu"), R("pb"), R("z2"), A.add)
         act(R("mp"), G(R("DP"), R("pu")))
         act(R("ms"), R("hit"), scale=-1.0, bias=1.0, acc=R("mc", 0, 1))
         for r in range(16):
             mm(R("Q0", 0, 12), Sr(r), R("prE", r, L, 16), r == 0, r == 15)
-        tt(R("ew"), R("Q0", 0, 12), R("Sd"), A.add)
+        if t < NT:
+            ts(R("ei"), R("Q0", 0, 12), 1536.0, A.add)
+            ts(R("ej"), R("ei"), KW - 1, A.bitwise_and)
+        eS, TW = (R("ej"), R("TT", S - KW, S + KW)) if t < NT else (R("Q0", 0, 12), R("TT"))
+        tt(R("ew"), eS, R("Sd", 0, 12), A.add)
         tt(R("pr2", L, 2 * L), R("mp"), R("MA", 0, L), A.mult)
-        tt(R("pr2", 0, L), G(R("TT", 0, 2 * S), R("ew")), R("mp"), A.mult)
-        rivals("2", "pr2", "BO8", s, 128 * t, R("SP", 12 * t, 12 * t + 12), R("m2", 16 * t, 16 * t + 12), "Q2")
-        mm(R("Q1", 0, 24), R("Ib"), R("cst"), True, False)
+        tt(R("pr2", 0, L), G(TW, R("ew")), R("mp"), A.mult)
         for r in range(16):
-            mm(R("Q1", 0, 24), Sr((r + s) % 16), R("pr2", r, 2 * L, 16), False, r == 15)
+            mm(R("Q2", (r + s) % 16, 128, 16, p1=12), R("pr2", r, L, 16), GS, True, True)
+        plus("aT2", R("aT2", 128 * t, 128 * t + 128, p1=12), R("Q2", 0, 128, p1=12))
+        rivals("2", "RV", "pr2", "BO8", 128 * t, R("SP", 12 * t, 12 * t + 12), R("m2", 16 * t, 16 * t + 12))
+        for r in range(16):
+            mm(R("MB", 256 + (r + s) % 16, 384, 16, p1=12), R("pr2", L + r, 2 * L, 16), GS, True, True)
+        act(R("c2T", p1=12), R("MB", 256, 384, p1=12))
+        mm(R("Q1", 12, 24), R("Ib"), R("cst", 12, 24), True, False)
+        mm(R("Q1", 12, 24), R("c2T", p1=12), I12, False, True)
+        mm(R("Q1", 0, 12), R("aT2", 128 * t, 128 * t + 128, p1=12), I12, True, True)
         plus("m1", R("m1", 24 * t, 24 * t + 24), R("Q1", 0, 24))
         send(R("m1", 24 * t, 24 * t + 24), R("r1", 24 * t, 24 * t + 24), "ra%d" % t, to)
         send(R("m2", 16 * t, 16 * t + 12), R("r2", 16 * t, 16 * t + 12), "rb%d" % t, to)
         act(R("eN"), R("Q0", 0, 12), bias=1536.0)
-        tt(R("pm"), R("Q0", 0, 12), R("cc"), A.subtract)
+        tt(R("pm"), R("ms"), R("cc"), A.mult)
+        tt(R("pn"), R("Q0", 0, 12), R("hit"), A.mult)
         act(R("yN"), G(R("X", 0, XS), R("eN")))
-        act(R("ke"), G(R("TT", S, 3 * S), R("ew")))
-        tt(R("pn"), R("pm"), R("hit"), A.mult)
-        tt(R("p16", 0, 12), R("pn"), R("cc"), A.add)
+        tt(R("ex"), eS, R("Sd", 12, 24), A.add)
+        act(R("ke"), G(TW, R("ex")))
+        tt(R("p16", 0, 12), R("pn"), R("pm"), A.add)
         mm(R("MB", 0, L), R("Sw"), R("ke"), True, True)
         tt(PV1, R("mp"), R("MB", 0, L), A.mult)
         tt(PC1, R("mp"), R("MA", L, 2 * L), A.mult)
-        if not last:
-            ts(R("pe"), R("pd"), 1, A.bitwise_and)
-            tt(R(Dn), R(D), R("pe"), A.is_equal)
         mm(R("Q1", 32, 33), R("BOf"), R("mc", 0, 1), True, True)
         mm(R("Q1", 48, 60), R("Ib"), R("nid16", 0, 12), True, False)
         mm(R("Q1", 48, 60), R("I192"), R("hit"), False, True)
         act(R("su"), R("Q1", 48, 60), bias=float(L))
         act(R("ymt", t, t + 1), R("Q1", 32, 33))
         mm(R("P1", 0, L), R("Ib"), R("yN"), True, False)
-        mm(R("P1", 0, L), R("In"), R("f4"), False, True)
-        mm(R("P1", L, 2 * L), R("Ih"), R("yN"), True, False)
-        mm(R("P1", L, 2 * L), R("Ih"), R("qN"), False, True)
+        mm(R("P1", 0, L), R("Ib"), R("f4"), False, True)
+        mm(R("P1", L, 2 * L), R("Ib"), R("yN"), True, False)
+        mm(R("P1", L, 2 * L), R("Ib"), R("qN"), False, True)
         for r in range(16):
-            mm(R("P2", r, L, 16), R("RR", 128 * r, 128 * r + 128), R("p16", 0, 12), True, True)
-        act(M("Lp", ALL), R("P2", 0, L))
+            mm(R("Q0", r, L, 16), R("RR", 128 * r, 128 * r + 128), R("p16", 0, 12), True, True)
+        act(M("Lp", ALL), R("Q0", 0, L))
         act(R("vals", 0, L), R("P1", 0, L), AF.Abs, bias=127.5 + 192.0)
-        act(R("vals", L, 2 * L), R("P1", L, 2 * L), bias=127.25)
+        act(R("vals", L, 2 * L), R("P1", L, 2 * L), scale=0.5, bias=127.25)
         act(R("nv"), G(R("vals"), R("su")), bias=-127.5)
-        rivals("p", "Lp", "I8", 0, 0, R("SP", 12 * ST, 12 * ST + 12), R("op", 0, 12), "Q2")
+        mm(R("Q2", 0, 128, p1=12), R("p16", 0, 12), R("Ib"), True, True)
+        plus("aTp", R("aTp", p1=12), R("Q2", 0, 128, p1=12))
+        rivals("p", "P2", "Lp", "I8", 0, R("SP", 12 * ST, 12 * ST + 12), R("op", 0, 12))
         for j in range(NS - 1, -1, -1):
             cp(G(R("X", 0, XS), R("op", MB * j, MB * j + MB)), R("nv", 16 * MB * j, 16 * MB * (j + 1)))
         act(R("c32", 0, 12), R("r1", 24 * t + 12, 24 * t + 24))
@@ -615,7 +615,7 @@ def rank_program(g, core, T, topo):
         append(R("r1", 24 * t, 24 * t + 12), 0, "r2", 16 * t, "t1", "t2")
 
     dma("s", T.yb[:, 0:1024], R("B", 0, 1024))
-    dma("a", T.yb[:, 1024:2048], R("B", 1024, 2048))
+    dma("a", T.yb[:, 1024:2048], R("B", 1024, 2048), ahead=4096)
     ts(R("oc", 0, L), R("Q0", L, 2 * L), 1536.0, A.add)
     cp(R("oi"), R("Q0", 0, L))
     ts(R("oj", 0, L), R("oi"), 1, A.arith_shift_right)

import numpy as np
from concourse.bass import DstId, RemoteDMATransfer
from concourse.mybir import dt, AluOpType, AxisListType, ActivationFunctionType

S, NV, KW, L, ST = 3072, 2048, 512, 192, 7
F32, BF, F16, I32, U16 = "float32", "bfloat16", "float16", "int32", "uint16"
MB, NS = 4, 3
SEG = [8 * a * (a + 1) for a in range(MB + 1)]
SL = SEG[MB]
XS, BS = S + 16 * MB, NV + 16 * MB
C0 = 512.0 * 12288


def _sb(n, d):
    return ("sbuf", [128] + (n if isinstance(n, list) else [n]), d)


def _ps(n):
    return ("psum", [128] + n, F32)


SCRATCH = {
    "xin": _sb(S, BF), "X": _sb(XS + NV, BF), "Bi": _sb(NV, I32), "B": _sb(BS, F32),
    "K": _sb(S, I32), "ka": _sb(KW, I32), "TT": _sb(2 * S, F32), "li": _sb(3 * L, I32), "lcol": _sb(L, F32),
    "pi": _sb(16, I32), "pj": _sb(16, I32), "pc": _sb(16, F32), "it": _sb(1024, BF), "it2": _sb(208, F32),
    "it4": _sb(144, F32), "it5": _sb(128, F32), "it6": _sb(128, F32), "it7": _sb(16, F32),
    "Wd": _sb(144, BF), "BO": _sb(128, BF), "BOf": _sb(128, F32), "BO8": _sb(128, BF), "RR": _sb(2048, BF),
    "Ib": _sb(128, BF), "In": _sb(128, BF), "I8": _sb(128, BF), "I192": _sb(128, BF), "I9": _sb(128, F32), "I16": _sb(128, BF),
    "Sw": _sb(128, BF), "Sel": _sb(1024, BF), "DG": _sb(208, F32), "NDG": _sb(208, F32), "NDm": _sb(208, BF), "sc1": _sb(L, F32),
    "DK": _sb(16, BF), "DP": _sb(48, BF), "DQ": _sb(48, BF), "MJ": _sb([NS, SL], BF), "CR": _sb(144, F16),
    "sa": _sb(12 * ST, I32), "sb": _sb(12 * ST, I32), "SP": _sb(12 * (ST + 1), F32), "w3": _sb(16, BF),
    "cJ": _sb(12, U16), "nid16": _sb(16, F16), "cst": _sb(24, BF),
    "E": _sb(L, U16), "Ec": _sb(L, F16), "xe": _sb(S, BF), "H": _sb(S, F16), "LT": _sb(128, F16), "cT": _sb(256, F16),
    "QS": _sb(2 * L, BF), "QT": _sb(256, F16), "qN": _sb(L, BF), "f4": _sb(L, BF), "yN": _sb(L, BF), "kc": _sb(L, F16), "ke": _sb(L, F16),
    "SX": _sb(L, F32), "th": _sb(4, F32), "hb": _sb(4, BF), "ab": _sb(4, F32),
    "Y": _sb(L, F32), "h16": _sb(L, F16), "tt": _sb(L, BF), "R1": _sb(L, I32), "R1k": _sb(L, F32), "R2": _sb(L, F32),
    "key": _sb(L, F32), "scn": _sb(L, I32),
    "kk": _sb(12, I32), "ku": _sb(12, U16), "z2": _sb(12, I32), "lo": _sb(12, I32), "hit": _sb(12, BF), "pb": _sb(12, F32),
    "pu": _sb(12, U16), "ms": _sb(12, F32), "mc": _sb(4, F32), "ymt": _sb(8, F32),
    "prE": _sb(L, F16), "mp": _sb(L, F32), "pr1": _sb([2 * NS, 64], F16), "pr2": _sb(2 * L, F16), "Lp": _sb([NS, 64], F16),
    "ew": _sb(12, U16), "ex": _sb(12, U16), "eN": _sb(12, U16), "ei": _sb(12, I32), "ej": _sb(12, I32), "c32": _sb(16, F32),
    "m1": _sb(24 * ST, U16), "m2": _sb(16 * ST, U16), "r1": _sb(24 * ST, U16), "r2": _sb(16 * ST, U16), "c2T": _sb(128, F16),
    "oo": _sb(16, U16), "op": _sb(16, U16), "aT2": _sb(128 * ST, F16), "aTo": _sb(128, F16), "aTp": _sb(128, F16),
    "ds2": _sb(16, F32), "dso": _sb(16, F32), "dsp": _sb(16, F32),
    "t1": _sb(L, F32), "t2": _sb(L, F32), "t3": _sb(L, F32), "t4": _sb(L, F32),
    "pm": _sb(12, F32), "pn": _sb(12, F32), "p16": _sb(16, F16), "su": _sb(12, U16), "cc": _sb(12, F32),
    "vals": _sb(2 * L, I32), "nv": _sb(L, BF),
    "D": _sb(12, BF), "Di": _sb(12, I32), "Dj": _sb(12, I32), "Sd": _sb(24, F32), "oN": _sb(12, U16), "ou": _sb(12, U16),
    "cu": _sb(12, U16), "QO": _sb(24, U16), "ci": _sb(12, I32), "cj": _sb(12, I32), "cw": _sb(12, U16),
    "yst": _sb(8, F32), "ysv": _sb(8, F32), "oc": _sb(3 * L, F32), "oi": _sb(L, I32), "oj": _sb(2 * L, I32),
    "Q0": _ps([512]), "Q1": _ps([512]), "Q2": _ps([512]), "P1": _ps([512]), "MA": _ps([512]), "MB": _ps([512]),
    "P2": _ps([NS, 170]), "RV": _ps([NS, 170]),
}
BUFS = dict(SCRATCH, MK=SCRATCH["MJ"])
PLACE = {}
_end = {}
for _n, (_w, _s, _d) in list(SCRATCH.items()):
    if _w == "sbuf" and len(_s) == 2 and _s[1] <= 48:
        _a = "short_" + _d
        PLACE[_n] = (_a, _end.get(_a, 0))
        _end[_a] = _end.get(_a, 0) + (_s[1] + 15) // 16 * 16
        del SCRATCH[_n]
        SCRATCH[_a] = _sb(_end[_a], _d)
    else:
        PLACE[_n] = (_n, 0)
NDMA = 48
SEMAPHORES = (["qv", "qa", "qp", "qg", "sent"] + ["d%d" % i for i in range(NDMA)]
              + ["ra%d" % t for t in range(ST)] + ["rb%d" % t for t in range(ST)])
PSUM = ("Q0", "Q1", "Q2", "P1", "P2", "MA", "MB", "RV")
WIDTH = {F32: 4, I32: 4, BF: 2, F16: 2, U16: 2}
CYC, PEC, GAT, SCA, HOP, FAR, FIX, DL, DB = 0.83, 0.42, 1.5, 3.5, 170.0, 2300.0, 50.0, 1300.0, 330.0
PLAN = {}
ROUNDS, NOISE, SHARE, SLACK = 500, 1500.0, (0.05, 0.2, 0.5), 300.0
NT, NK = 1, 2
PIECES = [(0, 32, "a"), (32, 72, "v"), (72, 96, "a"), (96, 128, "a"), (128, 160, "a"), (160, 180, "a"), (180, 192, "a")]
MINS = [0, 32, 64, 96, 128, 160, 180, 192]
ESPLIT, YSA = 32, 5
ON = dict(aT2="a", aTp="a", m1="a", ou="a", R1="v")


def plan(ops):
    n = len(ops)
    cost = [o["cost"] + 0.001 for o in ops]
    pred = [[] for _ in range(n)]
    succ = [[] for _ in range(n)]
    for i, o in enumerate(ops):
        for d in o["deps"] | o["order"]:
            lag = ops[d]["lat"] + HOP if d in o["deps"] else (ops[d]["lat"] if o["kind"] == "x" else 0.0)
            pred[i].append((d, lag))
            succ[d].append((i, lag))
    tail = [o["lat"] for o in ops]

    def fill(seq, before, first):
        st = [0.0] * n
        busy = {}
        for i in seq:
            t = max([st[d] + cost[d] + lag for d, lag in before[i]] + [first[i]])
            q = ops[i]["q"]
            if q != "x":
                a, b = busy.setdefault(q, ([], []))
                lo, hi = 0, len(b)
                while lo < hi:
                    m = (lo + hi) // 2
                    if b[m] <= t:
                        lo = m + 1
                    else:
                        hi = m
                while lo < len(a) and a[lo] < t + cost[i]:
                    t = max(t, b[lo])
                    lo += 1
                a.insert(lo, t)
                b.insert(lo, t + cost[i])
            st[i] = t
        return st

    far = [0.0] * n
    for i in range(n - 1, -1, -1):
        far[i] = cost[i] + max([far[s] + lag for s, lag in succ[i]] + [tail[i]])
    zero = [0.0] * n
    rng = np.random.default_rng(7)
    names = {}
    kin = np.array([names.setdefault((o["q"], o["tag"], o["nth"]), len(names)) for o in ops])

    def both(st, shift):
        key = [shift[i] - st[i] - cost[i] for i in range(n)]
        for i in range(n - 1, -1, -1):
            for d, _ in succ[i]:
                if key[i] <= key[d]:
                    key[i] = key[d] + 0.001
        back = fill(sorted(range(n), key=lambda i: key[i]), succ, tail)
        st = fill(sorted(range(n), key=lambda i: -(back[i] + cost[i])), pred, zero)
        return max(st[i] + cost[i] + tail[i] for i in range(n)), st

    best = both(fill(sorted(range(n), key=lambda i: -far[i]), pred, zero), zero)
    for k in range(ROUNDS):
        some = rng.random(n) < SHARE[k % len(SHARE)]
        new = both(best[1], ((rng.random(n) - 0.5) * some)[kin] * NOISE)
        if new[0] < best[0] + SLACK * (1 - k / ROUNDS):
            best = new
    st = best[1]
    PLAN["end"] = [st[i] + cost[i] + tail[i] for i in range(n)]
    return sorted(range(n), key=lambda i: st[i])


def rank_program(g, core, T, topo):
    rank = T.rank_of(core)
    if rank is None:
        return
    A, AF = AluOpType, ActivationFunctionType
    N = len(T.cores)
    ops = []
    seen = {}
    bank = {}
    ndma = [0]
    nth = {}

    def R(name, lo=0, hi=None, step=1, p0=0, p1=128, ps=1):
        w = BUFS[name][1][1]
        hi = w if hi is None else hi
        t, o = T[PLACE[name][0]], PLACE[name][1]
        rows = slice(None) if (p0, p1, ps) == (0, 128, 1) else slice(p0, p1, ps)
        ap = t[rows, o + lo:o + hi] if step == 1 else t[rows, o + lo:o + hi:step]
        cols = sum(1 << c for c in range(lo, hi, step)) if step > 1 else (1 << hi) - (1 << lo)
        return (ap, [(name, cols)], [], len(range(lo, hi, step)), WIDTH[BUFS[name][2]], name in PSUM)

    def M(name, *idx, p0=0, p1=128):
        shape = BUFS[name][1][1:]
        flat = np.arange(int(np.prod(shape))).reshape(shape)[idx]
        return (T[{"MK": "MJ"}.get(name, name)][(slice(p0, p1),) + idx], [(name, sum(1 << int(c) for c in flat.flat))], [], int(flat.size),
                WIDTH[BUFS[name][2]], name in PSUM)

    def G(win, off):
        return (win[0].indirect(off[0]), win[1], off[1], 16 * off[3], win[4], False)

    def add(q, call, outs, ins, cost, kind="c", sem=None, lat=0.0, after=(), wait=()):
        me = len(ops)
        acc = []
        for o in outs:
            acc += [(r, True) for r in o[1]] + [(r, False) for r in o[2]]
        for o in ins:
            if isinstance(o, tuple):
                acc += [(r, False) for r in o[1] + o[2]]
        deps, order = set(wait), set(after)
        for (name, cols), wr in acc:
            ps = name in PSUM
            if ps and name in bank:
                order.add(bank[name])
            for a in seen.get(name, []):
                other = ops[a[1]]
                same = other["q"] == q and other["kind"] == "c" and kind == "c"
                if ps and not same:
                    deps.add(a[1])
                elif wr and a[2] and kind == "d" and other["kind"] == "d":
                    continue
                elif a[0] & cols and (wr or a[2]) and not (same and q == "p" and ps):
                    deps.add(a[1])
        for (name, cols), wr in acc:
            lst = seen.setdefault(name, [])
            if name in PSUM:
                lst[:] = [a for a in lst if ops[a[1]]["q"] == q]
                bank[name] = me
            if wr:
                lst[:] = [a for a in lst if not (a[0] & ~cols == 0 and a[1] in deps)]
        tag = outs[0][1][0][0] if outs else kind
        ops.append({"q": q, "call": call, "deps": deps, "order": order - deps, "sem": sem, "kind": kind, "cost": cost, "lat": lat,
                    "tag": tag, "nth": nth.get((q, tag), 0) if q != "p" else 0})
        nth[(q, tag)] = ops[-1]["nth"] + 1
        for (name, cols), wr in acc:
            seen[name].append([cols, me, wr])
        return me

    def a0(x):
        return x[0] if isinstance(x, tuple) else x

    def vcost(o, ins, two=False):
        n = o[3]
        if o[2]:
            return FIX + n * SCA * CYC
        if ins and ins[0][2]:
            return FIX + n * GAT * CYC
        if two:
            return FIX + n * CYC * (1 if (ins[0][5] or ins[1][5]) else 2)
        return FIX + n * CYC * (0.5 if max([o[4]] + [i[4] for i in ins]) == 2 else 1)

    def cp(o, i):
        add("v", lambda: g.vector.tensor_copy(o[0], i[0]), [o], [i], vcost(o, [i]))

    def tt(o, i0, i1, op):
        add("v", lambda: g.vector.tensor_tensor(o[0], i0[0], i1[0], op), [o], [i0, i1], vcost(o, [i0, i1], True))

    def ts(o, i, s1, op0, s2=None, op1=None):
        if op1 is None:
            add("v", lambda: g.vector.tensor_scalar(o[0], i[0], a0(s1), None, op0), [o], [i, s1], vcost(o, [i]))
        else:
            add("v", lambda: g.vector.tensor_scalar(o[0], i[0], a0(s1), a0(s2), op0, op1), [o], [i, s1, s2], vcost(o, [i]))

    def scan(o, d0, d1, init, op0, op1):
        add("v", lambda: g.vector.tensor_tensor_scan(o[0], d0[0], d1[0], init, op0, op1), [o], [d0, d1], vcost(o, [d0, d1]))

    def least(o, i):
        add("v", lambda: g.vector.tensor_reduce(o[0], i[0], AxisListType.X, A.min, apply_absolute_value=True), [o], [i], FIX + i[3] * CYC)

    def total(o, i):
        add("v", lambda: g.vector.tensor_reduce(o[0], i[0], AxisListType.X, A.add), [o], [i], FIX + i[3] * CYC)

    def ms(o, c):
        add("v", lambda: g.vector.memset(o[0], c), [o], [], vcost(o, []))

    def act(o, i, func=None, bias=0.0, scale=1.0, acc=None):
        f = AF.Identity if func is None else func
        c = 65.0 + o[3] * CYC * (GAT if i[2] else 1)
        if acc is None:
            add("a", lambda: g.scalar.activation(o[0], i[0], f, bias=a0(bias), scale=a0(scale)), [o], [i, bias, scale], c)
        else:
            add("a", lambda: g.scalar.activation(o[0], i[0], f, bias=a0(bias), scale=scale, accum_out=acc[0]), [o, acc], [i, bias], c + 20)

    def plus(k, o, i, bias=0.0):
        if ON[k] == "a":
            act(o, i, bias=bias)
        else:
            ts(o, i, bias, A.add)

    def mm(o, l, r, start, stop):
        add("p", lambda: g.tensor.matmul(o[0], l[0], r[0], start, stop), [o], [l, r],
            max(min(64, l[3]), r[3]) * PEC * (4 if r[4] == 4 else 1))

    def iota(o, pat, base, cm):
        c = 130.0 + 2 * CYC * o[3]
        if BUFS[o[1][0][0]][2] == I32:
            add("g", lambda: g.iota(o[0], pat, base, cm), [o], [], c)
        else:
            add("g", lambda: g.iota(o[0], pat, base, cm, allow_small_or_imprecise_dtypes=True), [o], [], c)

    def select(o, i, pat, cm):
        add("g", lambda: g.affine_select(o[0], i[0], pat, A.is_equal, 0.0, 0, cm), [o], [i], 170.0 + 2 * CYC * o[3])

    def dma(q, o, i, wait=(), after=(), ahead=0):
        e = {"s": g.sync, "a": g.scalar, "g": g}[q]
        sem = "d%d" % ndma[0]
        ndma[0] += 1
        sb = o if isinstance(o, tuple) else i
        return add(q, lambda: e.dma_start(a0(o), a0(i)), [o] if isinstance(o, tuple) else [], [i], 100.0, kind="d", sem=sem,
                   lat=DL + 128 * (ahead + sb[3] * sb[4]) / DB, wait=wait, after=after)

    def engines_to(dst):
        es = topo.engines(core, dst)
        n = min(len(topo.engines(a, b)) for a in T.cores for b in T.cores if a != b)
        m = 0
        for e in es[:n]:
            m |= 1 << e
        return m, n

    nsent = [0]

    def send(src, dst, sem, to):
        rid, pid = topo.addr(to)[:2]
        m, n = engines_to(to)
        nsent[0] += n
        me = add("g", lambda: g.remote_dma(dst[0], src[0], T.sem[sem], T.sem.sent, pid, rid, m), [], [src], 300.0, kind="r", lat=FAR)
        add("x", None, [dst], [], 0.0, kind="x", sem=sem, after=[me])

    def Sr(r):
        return R("Wd", 16 - r, 144 - r)

    def every(a, b, step=None):
        return slice(a, b, step)

    ALL = slice(None)
    PC, PK, PR0, PPI, PNI, P64, PG, PX1, PLT, PU, PB16, PS16, PB17, PW = [R("pc", i, i + 1) for i in range(14)]
    SJ, GS, I12 = R("Sel", 0, L, p1=12), R("BO", 0, 128, 16), R("Ib", 0, 12, p1=12)
    U = M("P2", ALL, every(0, 64))
    PV1, PC1 = M("pr1", every(0, NS)), M("pr1", every(NS, 2 * NS))

    ms(R("li"), 0)
    big = [dma("a", R("xin", 0, S // 2), T.x[:, 0:S // 2])]
    small = [dma("s", R("li", L * k, L * k + L, ps=16), src[:]) for k, src in enumerate((T.lv, T.ld, T.lc))]
    big.append(dma("s", R("xin", S // 2, S), T.x[:, S // 2:S], after=small, ahead=S // 2))
    big.append(dma("s", R("Bi"), T.bnd[:], after=big[1:], ahead=3 * S // 2))
    dma("s", R("K", 0, KW), T.kt[:], after=big[2:], ahead=3 * S // 2 + 4 * NV)
    iota(R("pi", 0, 1), [[0, 1]], 0, 1)
    iota(R("it4"), [[1, 144]], -16, -1)
    iota(R("it5"), [[16, 8], [0, 16]], 0, -1)
    iota(R("it6"), [[1, 128]], 0, -1)
    iota(R("it7"), [[1, 16]], 0, 0)
    iota(R("it2"), [[0, 13], [1, 16]], 0, 0)
    iota(R("it"), [[1, 64], [0, 16]], 0, 0)
    ts(R("pj", 0, 1), R("pi", 0, 1), 15, A.bitwise_and)
    ts(R("pj", 1, 2), R("pi", 0, 1), 63, A.bitwise_and)
    ts(R("pj", 2, 3), R("pi", 0, 1), 1, A.bitwise_and)
    cp(PC, R("pj", 0, 1))
    cp(P64, R("pj", 1, 2))
    cp(PPI, R("pj", 2, 3))
    act(PG, R("pi", 0, 1), bias=-32.0)
    act(PK, PC, scale=-1.0, bias=15.0)
    ts(PR0, PC, 0.0, A.is_equal)
    act(PNI, PPI, scale=-2.0, bias=1.0)
    act(PX1, PC, bias=PNI)
    ts(PLT, PG, 16.0, A.is_lt)
    ts(PW, PG, 0.0, A.is_ge, PLT, A.mult)
    ts(PU, PG, PW, A.mult)
    ts(PU, PG, 16.0, A.is_ge, PU, A.add)
    ts(PB16, PG, 16.0, A.is_equal, float(NV), A.mult)
    act(PS16, PB16, scale=0.75)
    ts(PB17, PG, 17.0, A.is_equal, PB16, A.add)
    act(R("cJ"), R("it7", 0, 12))
    ts(R("nid16", 0, 12), R("it7", 0, 12), 16.0, A.mult, PC, A.add)
    ts(R("Wd"), R("it4"), PC, A.add, 0.0, A.is_equal)
    ts(R("BO"), R("it5"), PC, A.add, 0.0, A.is_equal)
    ts(R("Ib"), R("it6"), 0.0, A.is_equal)
    ts(R("Sw"), R("it6"), PNI, A.is_equal)
    ms(R("cst", 0, 12), 0.0)
    ms(R("cst", 12, 24), 1536.0)
    ts(R("DG"), R("it2"), PC, A.is_equal)
    ts(R("NDG"), R("it2"), PC, A.not_equal)
    ts(R("DK"), R("it7"), PK, A.is_equal)
    ts(R("DP"), R("it2", 15, 63), PX1, A.add, 0.0, A.is_equal)
    ts(R("DQ"), R("it2", 15, 63), PX1, A.add, 16.0, A.is_equal)
    tt(R("DP"), R("DP"), R("DQ"), A.add)
    ms(R("sc1"), 32.0)
    ms(R("sc1", 0, L, 16), -2.0 ** 24)
    ts(R("Sel"), R("it"), P64, A.is_equal)
    ms(R("th"), 1.0 / 32)
    iota(R("RR"), [[0, 2048]], 1, 0)
    select(R("RR"), R("RR"), [[-1, 16], [-16, 8], [0, 16]], 1)
    act(R("NDm"), R("NDG"), scale=-4096.0)
    for nm, k in (("I192", -float(L)), ("In", -1.0), ("I8", 8192.0), ("I9", -2.0 ** -9), ("I16", 16.0)):
        act(R(nm), R("Ib"), scale=k)
    act(R("BOf"), R("BO"))
    act(R("BO8"), R("BO"), scale=8192.0)
    ts(R("CR"), R("it2", 0, 144), PG, A.is_equal, PB16, A.add)
    for t in range(ST):
        s = (5 * t) % 16
        dma("s", R("aT2", 128 * t, 128 * t + 128, p0=12, p1=50), R("CR", 16 - s, 144 - s, p0=12, p1=50))
    ts(R("aTo"), R("it2", 0, 128), PG, A.is_equal, PB17, A.add)
    ts(R("aTp"), R("it2", 0, 128), PG, A.is_equal, PS16, A.add)
    UP = dict(p0=32, p1=64)
    for a in range(MB):
        iota(M("MJ", ALL, every(SEG[a], SEG[a + 1]), p1=32), [[MB, NS], [0, 16 * a + 16]], a, -1)
    ts(M("MJ", ALL, p1=32), M("MJ", ALL, p1=32), 0.0, A.is_equal, -8192.0, A.mult)
    ms(M("MK", ALL, **UP), 0.0)
    ts(R("w3", 0, NS, **UP), R("it2", 0, 48, 16, **UP), R("pc", 13, 14, **UP), A.add)
    for a in range(MB):
        e = SEG[a + 1] - 1
        act(M("MJ", ALL, e, p1=32), M("MJ", ALL, e, p1=32), scale=2.0 ** -13)
        ts(M("MK", ALL, every(e - 15, e + 1), **UP), R("it2", 0, 48, **UP), R("pc", 6, 7, **UP), A.is_ge, 4096.0, A.mult)
        ts(M("MK", ALL, e, **UP), R("w3", 0, NS, **UP), 16.0 * a, A.mult, R("pc", 9, 10, **UP), A.add)
    iota(R("sa"), [[-5, ST], [0, 12]], 48, 1)
    iota(R("sb"), [[0, ST * NS], [16, MB]], NV, 0)
    ts(R("sa"), R("sa"), 15, A.bitwise_and)
    tt(R("SP", 0, 12 * ST), R("sa"), R("sb"), A.add)
    act(R("SP", 12 * ST, 12 * ST + 12), R("SP", 0, 12), bias=float(S - NV))
    select(R("B", 0, NV), R("Bi"), [[0, NV]], 0)
    ms(R("B", NV, BS), 0.0)
    ts(R("ka"), R("K", 0, KW), 1023, A.bitwise_and)
    act(R("TT", S - KW, S), R("ka"), scale=2.0, bias=PPI)
    act(R("TT", S, S + KW), R("TT", S - KW, S), bias=PNI)
    for k in range(1, S // KW):
        dma("s", R("TT", S - KW * (k + 1), S - KW * k), R("TT", S - KW, S), ahead=8 * KW * (k - 1))
        more = dma("s", R("TT", S + KW * k, S + KW * (k + 1)), R("TT", S, S + KW), ahead=8 * KW * k - 4 * KW)
    for k in range(1, S // KW):
        dma("s", R("K", KW * k, KW * k + KW), T.kt[:], wait=[more], ahead=4 * KW * (k - 1))
    ts(R("X", 0, 1536), R("xin", 0, 1536), -127.5, A.add)
    ts(R("X", 1536, S), R("xin", 1536, S), -127.5, A.add)
    ms(R("X", S, XS), 0.0)
    ms(R("X", XS, XS + NV, 2), 0.0625)
    ms(R("X", XS + 1, XS + NV, 2), -0.0625)
    act(R("lcol"), R("li", 0, L), scale=2.0, bias=PR0)
    tt(PV1, R("lcol"), R("li", L, 2 * L), A.subtract)
    ts(PC1, R("li", 2 * L, 3 * L), -1536.0, A.add, PR0, A.mult)

    def lanes(t):
        s = (5 * t) % 16
        for a in range(16):
            at = 16 * (a % 4) + a // 4
            mm(R("Q0", 0, 24), Sr(a), M("pr1", ALL, every(at, at + 13, 4)), a == 0, a == 15)
        plus("ou", R("ou"), R("Q0", 0, 12))
        act(R("QO", 0, 12), R("Q0", 12, 24), bias=1536.0)
        act(R("QO", 12, 24), R("Q0", 0, 12), bias=float(XS))
        for o, k, w in ((0, 0, 0), (128, s, NS), (256, 0, NS)):
            for r in range(16):
                mm(R("MB", o + (r + k) % 16, o + 128, 16, p1=12), M("pr1", every(w, w + NS), every(r, 64, 16)), GS, True, True)
        act(R("aTo", p1=12), R("MB", 0, 128, p1=12))
        act(R("cT", p1=12), R("MB", 128, 384, p1=12))
        mm(R("Q1", 0, 12), R("aTo", p1=12), I12, True, True)
        mm(R("Q1", 12, 24), R("cT", 128, 256, p1=12), I12, True, True)
        act(R("oN"), R("Q1", 0, 12))
        act(R("cu"), R("Q1", 12, 24), bias=1536.0)
        act(R("cc"), R("Q1", 12, 24))
        act(R("Di"), R("Q1", 0, 12))
        ts(R("Dj"), R("Di"), 1, A.bitwise_and)
        act(R("D"), R("Dj"), scale=-2.0, bias=2.0)
        w, b = (float(KW), 0.0) if t < NT else (float(S), 1536.0)
        act(R("Sd", 0, 12), R("Dj"), scale=-w, bias=b + w)
        act(R("Sd", 12, 24), R("Dj"), scale=w, bias=b)
        act(R("QS"), G(R("X"), R("QO")))
        for b in range(2):
            mm(R("MA", 128 * b, 128 * b + 128), R("QS", 64 * b, 64 * b + 128), R("Ib"), True, False)
            mm(R("MA", 128 * b, 128 * b + 128), R("QS", L + 64 * b, L + 64 * b + 128), R("Ib"), False, True)
        act(R("QT"), R("MA", 0, 256))
        act(R("qN"), G(R("X", 0, XS), R("cu")))
        mm(M("P2", 0, every(0, 128), p1=12), R("D"), R("Ib"), True, False)
        for r in range(16):
            mm(M("P2", 0, every(r, 128, 16), p1=12), R("qN", r, L, 16), GS, False, r == 15)
        act(R("LT", p1=12), M("P2", 0, every(0, 128), p1=12), scale=-1.0, bias=1.0)
        act(R("SX"), G(R("D"), R("cJ")), scale=-2.0 ** -18, bias=2.0 ** -18)
        for c in range(3):
            spread(c)
        mm(R("P1", 0, L), R("LT", p1=12), SJ, True, False)
        mm(U, R("LT", p1=12), SJ, True, False)
        act(R("f4"), R("qN"), scale=-0.25, bias=-31.5 - 192.0)
        if t < NK:
            act(R("ci"), R("cc"), bias=1536.0)
            ts(R("cj"), R("ci"), KW - 1, A.bitwise_and)
            act(R("cw"), R("cj"))
        act(R("kc"), G(R("K", 0, KW), R("cw")) if t < NK else G(R("K"), R("cu")), bias=-1536.0)
        rivals("o", "RV", "pr1", "BO8", 0, R("SP", 0, 12), R("oo", 0, 12), "D")
        mm(R("MB", 0, L), R("Ib"), R("NDm", s, s + L), True, False)
        mm(R("MB", 0, L), R("cT", 0, 128, p1=12), SJ, False, True)
        act(R("t4"), R("MB", 0, L), AF.Relu, bias=1536.0)
        mm(R("MA", 0, L), R("Ib"), R("kc"), True, True)
        mm(R("MA", L, 2 * L), R("Sw"), R("kc"), True, True)

    def spread(c):
        b, p = (0, 0) if c < 2 else ((0, 64) if c < 4 else (1, 64))
        mm(R("Q%d" % (c % 3)), R("QT", 128 * b, 128 * b + 128, p0=p, p1=p + 64), R("Sel", 512 * (c % 2), 512 * (c % 2) + 512, p0=p, p1=p + 64),
           True, True)

    def rivals(k, RV, src, lw, at, spare, off, side="cst"):
        for a in range(MB):
            mm(M(RV, ALL, SEG[a + 1] - 1), R("In"), R(side, a, 12, MB), a == 0, False)
        for a in range(MB):
            if k == "2":
                for c in range(NS):
                    mm(M(RV, c, every(SEG[a], SEG[a + 1] - 1)), R(lw), R(src, 64 * c, 64 * c + 16 * a + 15), False, False)
            else:
                mm(M(RV, ALL, every(SEG[a], SEG[a + 1] - 1)), R(lw), M(src, every(0, NS), every(0, 16 * a + 15)), False, False)
        mj = M("MJ", ALL, p1=50)
        mm(M(RV, ALL, every(0, SL)), R("aT" + k, at, at + 128, p1=50), (mj[0], mj[1] + M("MK", ALL)[1]) + mj[2:], False, True)
        for a in range(MB - 1, -1, -1):
            least(R("ds" + k, a, 12, MB), M(RV, ALL, every(SEG[a], SEG[a + 1])))
        tt(off, spare, R("ds" + k, 0, 12), A.subtract)

    def append(cols, s, name, base, t1, t2):
        tt(R(t1), G(R("B"), cols), R("NDG", s, s + L), A.mult)
        for j in range(NS - 1, -1, -1):
            a, b = 16 * MB * j, 16 * MB * (j + 1)
            tt(G(R("B"), R(name, base + MB * j, base + MB * j + MB)), R(t1, a, b), R(t2, a, b), A.add)

    lanes(0)
    for t in range(ST):
        last = t == ST - 1
        to = T.cores[(rank + 1 + t % (N - 1)) % N]
        s = (5 * t) % 16
        Bt = R("Bi") if t == 0 else R("B")
        nth.clear()
        act(R("E", 0, ESPLIT), G(Bt, R("ou", 0, ESPLIT // 16)))
        cp(R("E", ESPLIT, L), G(Bt, R("ou", ESPLIT // 16, 12)))
        done, prev = [0, 0], []

        def sums(n, which):
            while 4 * (done[which] + 1) <= n:
                c, r = divmod(done[which], 16)
                o = R("P1", 64 * c, 64 * c + 64) if which else M("P2", c, every(0, 64))
                mm(o, Sr(r), R(("xe", "H")[which], 64 * done[which], 64 * done[which] + 64), False, (which, c, r) == (0, 2, 15))
                done[which] += 1

        for lo, hi, e in PIECES:
            o, i = R("xe", 16 * lo, 16 * hi), G(R("X", 0, XS), R("E", lo, hi))
            if e == "v":
                cp(o, i)
            else:
                act(o, i)
                if prev:
                    ops[-1]["order"].add(prev[-1])
                prev.append(len(ops) - 1)
            sums(hi, 0)
        act(R("Ec"), G(Bt, R("oN")), bias=-1536.0)
        append(R("oo", 0, 12), s, "oo", 0, "t3", "t4")
        tt(R("tt"), R("SX"), U, A.mult)
        act(R("Y"), U, scale=512.0, bias=512.0 * 8192)
        act(R("h16"), U, scale=1.0 / 16, bias=1536.0)
        for a, b in zip(MINS, MINS[1:]):
            c = a // 32
            tt(R("H", 16 * a, 16 * b), R("xe", 16 * a, 16 * b), R("Q%d" % (c % 3), 16 * (a - 32 * c), 16 * (b - 32 * c)), A.min)
            sums(b, 1)
            if b % 32 == 0 and c + 3 < 6:
                spread(c + 3)
        mm(R("P1", 0, L), R("Ib"), R("tt"), False, True)
        mm(R("Q1", 0, L), R("I9"), R("Y"), True, False)
        mm(R("Q1", 0, L), R("I16"), R("h16"), False, True)
        plus("R1", R("R1"), R("P1", 0, L), R("th", 0, 1))
        act(R("R1k"), R("R1"), scale=1024.0, bias=C0 - 16 * 1536.0 + 8192 + 18)
        tt(R("P1", 256, 256 + L), R("R1"), R("P1", 0, L), A.is_gt)
        tt(R("R2"), R("R1k"), R("Q1", 0, L), A.add)
        tt(R("P1", 256, 256 + L), R("P1", 256, 256 + L), R("Y"), A.mult)
        tt(R("key"), R("R2"), R("P1", 256, 256 + L), A.subtract)
        scan(R("scn"), R("sc1"), R("key"), 0.0, A.add, A.max)
        best = R("scn", 15, L, 16)
        ts(R("kk"), best, 5, A.arith_shift_right, 15, A.bitwise_and)
        cp(R("ku"), R("kk"))
        tt(R("prE"), G(R("DK"), R("ku")), R("Ec"), A.mult)
        ts(R("hit"), best, 512.0 * 4100, A.is_gt)
        ts(R("lo"), best, 31, A.bitwise_and)
        ts(R("z2"), best, 9, A.arith_shift_right, 15, A.bitwise_and)
        tt(R("pb"), R("lo"), R("hit"), A.mult)
        tt(R("pu"), R("pb"), R("z2"), A.add)
        act(R("mp"), G(R("DP"), R("pu")))
        act(R("ms"), R("hit"), scale=-1.0, bias=1.0, acc=R("mc", 0, 1))
        for r in range(16):
            mm(R("Q0", 0, 12), Sr(r), R("prE", r, L, 16), r == 0, r == 15)
        if t < NT:
            ts(R("ei"), R("Q0", 0, 12), 1536.0, A.add)
            ts(R("ej"), R("ei"), KW - 1, A.bitwise_and)
        eS, TW = (R("ej"), R("TT", S - KW, S + KW)) if t < NT else (R("Q0", 0, 12), R("TT"))
        tt(R("ew"), eS, R("Sd", 0, 12), A.add)
        tt(R("pr2", L, 2 * L), R("mp"), R("MA", 0, L), A.mult)
        tt(R("pr2", 0, L), G(TW, R("ew")), R("mp"), A.mult)
        for r in range(16):
            mm(R("Q2", (r + s) % 16, 128, 16, p1=12), R("pr2", r, L, 16), GS, True, True)
        plus("aT2", R("aT2", 128 * t, 128 * t + 128, p1=12), R("Q2", 0, 128, p1=12))
        rivals("2", "RV", "pr2", "BO8", 128 * t, R("SP", 12 * t, 12 * t + 12), R("m2", 16 * t, 16 * t + 12))
        for r in range(16):
            mm(R("MB", 256 + (r + s) % 16, 384, 16, p1=12), R("pr2", L + r, 2 * L, 16), GS, True, True)
        act(R("c2T", p1=12), R("MB", 256, 384, p1=12))
        mm(R("Q1", 12, 24), R("Ib"), R("cst", 12, 24), True, False)
        mm(R("Q1", 12, 24), R("c2T", p1=12), I12, False, True)
        mm(R("Q1", 0, 12), R("aT2", 128 * t, 128 * t + 128, p1=12), I12, True, True)
        plus("m1", R("m1", 24 * t, 24 * t + 24), R("Q1", 0, 24))
        send(R("m1", 24 * t, 24 * t + 24), R("r1", 24 * t, 24 * t + 24), "ra%d" % t, to)
        send(R("m2", 16 * t, 16 * t + 12), R("r2", 16 * t, 16 * t + 12), "rb%d" % t, to)
        act(R("eN"), R("Q0", 0, 12), bias=1536.0)
        tt(R("pm"), R("ms"), R("cc"), A.mult)
        tt(R("pn"), R("Q0", 0, 12), R("hit"), A.mult)
        act(R("yN"), G(R("X", 0, XS), R("eN")))
        tt(R("ex"), eS, R("Sd", 12, 24), A.add)
        act(R("ke"), G(TW, R("ex")))
        tt(R("p16", 0, 12), R("pn"), R("pm"), A.add)
        mm(R("MB", 0, L), R("Sw"), R("ke"), True, True)
        tt(PV1, R("mp"), R("MB", 0, L), A.mult)
        tt(PC1, R("mp"), R("MA", L, 2 * L), A.mult)
        mm(R("Q1", 32, 33), R("BOf"), R("mc", 0, 1), True, True)
        mm(R("Q1", 48, 60), R("Ib"), R("nid16", 0, 12), True, False)
        mm(R("Q1", 48, 60), R("I192"), R("hit"), False, True)
        act(R("su"), R("Q1", 48, 60), bias=float(L))
        act(R("ymt", t, t + 1), R("Q1", 32, 33))
        mm(R("P1", 0, L), R("Ib"), R("yN"), True, False)
        mm(R("P1", 0, L), R("Ib"), R("f4"), False, True)
        mm(R("P1", L, 2 * L), R("Ib"), R("yN"), True, False)
        mm(R("P1", L, 2 * L), R("Ib"), R("qN"), False, True)
        for r in range(16):
            mm(R("Q0", r, L, 16), R("RR", 128 * r, 128 * r + 128), R("p16", 0, 12), True, True)
        act(M("Lp", ALL), R("Q0", 0, L))
        act(R("vals", 0, L), R("P1", 0, L), AF.Abs, bias=127.5 + 192.0)
        act(R("vals", L, 2 * L), R("P1", L, 2 * L), scale=0.5, bias=127.25)
        act(R("nv"), G(R("vals"), R("su")), bias=-127.5)
        mm(R("Q2", 0, 128, p1=12), R("p16", 0, 12), R("Ib"), True, True)
        plus("aTp", R("aTp", p1=12), R("Q2", 0, 128, p1=12))
        rivals("p", "P2", "Lp", "I8", 0, R("SP", 12 * ST, 12 * ST + 12), R("op", 0, 12))
        for j in range(NS - 1, -1, -1):
            cp(G(R("X", 0, XS), R("op", MB * j, MB * j + MB)), R("nv", 16 * MB * j, 16 * MB * (j + 1)))
        act(R("c32", 0, 12), R("r1", 24 * t + 12, 24 * t + 24))
        tt(R("t2"), G(R("c32", 0, 12), R("cJ")), R("DG", 0, L), A.mult)
        if not last:
            act(R("hb", 0, 1), R("ymt", t, t + 1), scale=0.5, bias=143.75)
            act(R("ab", 0, 1), R("ymt", t, t + 1), scale=1.0 / 16, bias=18.0 + 1.0 / 32)
            act(R("th", 0, 1), R("hb", 0, 1), scale=-0.125, bias=R("ab", 0, 1))
            lanes(t + 1)
        else:
            mm(R("Q0", 0, 2 * L), R("BO"), M("pr1", ALL), True, True)
            for b in range(YSA):
                act(R("xin", 384 * b, 384 * b + 384), R("X", 384 * b, 384 * b + 384), bias=127.5, acc=R("yst", b, b + 1))
            for b in range(YSA, 8):
                total(R("ysv", b, b + 1), R("X", 384 * b, 384 * b + 384))
            ts(R("yst", YSA, 8), R("ysv", YSA, 8), 127.5 * 384, A.add)
        append(R("r1", 24 * t, 24 * t + 12), 0, "r2", 16 * t, "t1", "t2")

    dma("s", T.yb[:, 0:1024], R("B", 0, 1024))
    dma("a", T.yb[:, 1024:2048], R("B", 1024, 2048), ahead=4096)
    ts(R("oc", 0, L), R("Q0", L, 2 * L), 1536.0, A.add)
    cp(R("oi"), R("Q0", 0, L))
    ts(R("oj", 0, L), R("oi"), 1, A.arith_shift_right)
    ts(R("oj", L, 2 * L), R("oi"), 1, A.bitwise_and)
    cp(R("oc", L, 2 * L), R("oj", 0, L))
    ts(R("oc", 2 * L, 3 * L), R("oj", L, 2 * L), -1.0, A.mult, 1.0, A.add)
    dma("s", T.yc[:], R("oc", 0, L, ps=16))
    dma("s", T.ys[:], R("yst"))
    dma("s", T.ym[:], R("ymt", 0, ST, ps=16))
    dma("s", T.yv[:], R("oc", L, 2 * L, ps=16))
    dma("s", T.yd[:], R("oc", 2 * L, 3 * L, ps=16))

    if "order" not in PLAN:
        PLAN["order"] = plan(ops)
        PLAN["ops"] = ops
    order = PLAN["order"]
    where = {i: k for k, i in enumerate(order)}
    queue = {"v": g.vector, "a": g.scalar, "p": g.tensor, "g": g, "s": g.sync}
    qsem = {"v": "qv", "a": "qa", "p": "qp", "g": "qg"}
    narr = engines_to(T.cores[(rank + 1) % N])[1]
    need, waits = set(), {}
    for i, o in enumerate(ops):
        latest = {}
        for d in o["deps"]:
            if ops[d]["kind"] == "c":
                q = ops[d]["q"]
                if q not in latest or where[d] > where[latest[q]]:
                    latest[q] = d
        waits[i] = set(d for d in o["deps"] if ops[d]["kind"] in "dx") | set(latest.values())
        need |= waits[i]
    count, mark, clock, known = {}, {}, {}, {q: {} for q in queue}
    for i in order:
        q, sem, kind = ops[i]["q"], ops[i]["sem"], ops[i]["kind"]
        if kind == "x":
            mark[i] = (sem, narr)
            clock[i] = {sem: narr}
            continue
        kn = known[q]
        for d in sorted(waits[i], key=lambda k: -where[k]):
            s, v = mark[d]
            if kn.get(s, 0) < v:
                queue[q].wait_ge(T.sem[s], v)
            for s2, v2 in clock[d].items():
                if kn.get(s2, 0) < v2:
                    kn[s2] = v2
        ins = ops[i]["call"]()
        if kind == "d":
            ins.then_inc(T.sem[sem], 16)
            mark[i] = (sem, 16)
            count[sem] = 16
        elif kind == "c" and i in need:
            s = qsem[q]
            count[s] = count.get(s, 0) + 1
            ins.then_inc(T.sem[s], 1)
            mark[i] = (s, count[s])
        if i in mark:
            clock[i] = dict(kn)
            clock[i][mark[i][0]] = mark[i][1]
    for s, v in count.items():
        if max(kn.get(s, 0) for kn in known.values()) < v:
            g.wait_ge(T.sem[s], v)
    g.wait_ge(T.sem.sent, nsent[0])
